import numpy as np
import ml_dtypes


def mxq(x, axis, fmt="e4m3"):
    dtype, down = {"e4m3": (ml_dtypes.float8_e4m3fn, 7), "e5m2": (ml_dtypes.float8_e5m2, 14)}[fmt]
    v = np.moveaxis(np.asarray(x, np.float32).astype(ml_dtypes.bfloat16).astype(np.float64), axis, -1)
    blocks = v.reshape(v.shape[:-1] + (-1, 32))
    amax = np.abs(blocks).max(-1, keepdims=True)
    byte = np.maximum(np.where(amax > 0, np.frexp(amax)[1] - 1 + 127, 0) - down, 1)
    scale = np.exp2(byte - 127.0)
    codes = (blocks / scale).astype(np.float32).astype(dtype).astype(np.float64)
    return np.moveaxis((codes * scale).reshape(v.shape), -1, axis)


WIDE = False


def mx_kscale(k):
    if not WIDE:
        return np.ones(k)
    levels = np.array([10, -10, 5, -5, 0])
    if k % 512:
        return np.exp2(np.random.permutation(np.resize(levels, k // 32))).repeat(32)
    a = np.empty((k // 512, 16))
    for p in range(k // 512):
        a[p, :8] = np.random.permutation(np.resize(levels, 8))
        for g in range(8):
            far = levels[np.abs(levels - a[p, g]) >= 10]
            a[p, g + 8] = far[np.random.randint(len(far))]
    return np.exp2(a.ravel()).repeat(32)


def f64(x):
    return np.asarray(x).astype(np.float64)


def striped(idx):
    return np.tile(idx.reshape(-1, 16).T, (8, 1)).astype(np.uint16)


def unstriped(offs):
    return offs[:16].T.reshape(-1).astype(np.int64)


E2M1 = np.array([0.0, 0.5, 1.0, 1.5, 2.0, 3.0, 4.0, 6.0, -0.0, -0.5, -1.0, -1.5, -2.0, -3.0, -4.0, -6.0])


def pack_weight(w, fmt):
    k, n = w.shape
    w = f64(np.asarray(w, np.float32).astype(ml_dtypes.bfloat16)).reshape(k // 32, 32, n)
    amax = np.abs(w).max(1)
    if fmt == "e4m3":
        byte = np.frexp(amax)[1] - 1 + 127 - 7
    else:
        mant, ex = np.frexp(amax / 6.0)
        byte = np.where(mant > 0.5, ex, ex - 1) + 127
    byte = np.clip(np.where(amax > 0, byte, 1), 1, 254)
    scaled = (w * np.exp2(127.0 - byte)[:, None, :]).reshape(k, n).astype(np.float32)
    by_word = np.ascontiguousarray(scaled.reshape(k // 512, 128, 4, n).transpose(0, 1, 3, 2))
    if fmt == "e4m3":
        words = by_word.astype(ml_dtypes.float8_e4m3fn).view(np.uint8)
    else:
        c = by_word.astype(ml_dtypes.float4_e2m1fn).view(np.uint8) & 0xF
        words = (c[..., 0::2] | (c[..., 1::2] << 4)).reshape(k // 512, 128, 2 * n)
    return np.ascontiguousarray(words), np.ascontiguousarray(byte.astype(np.uint8).reshape(k // 512, 16, n))


def unpack_weight(words, scales, fmt):
    g, _, n = scales.shape
    words = np.ascontiguousarray(words).reshape(g, 128, n, -1)
    if fmt == "e4m3":
        vals = words.view(ml_dtypes.float8_e4m3fn).astype(np.float64)
    else:
        nib = np.empty((g, 128, n, 4), np.uint8)
        nib[..., 0::2] = words & 0xF
        nib[..., 1::2] = words >> 4
        vals = E2M1[nib]
    vals = vals * np.repeat(np.exp2(scales.astype(np.float64) - 127.0), 8, axis=1)[..., None]
    return vals.transpose(0, 1, 3, 2).reshape(g * 512, n)


def gelu(v):
    return 0.5 * v * (1.0 + np.tanh(np.sqrt(2.0 / np.pi) * (v + 0.044715 * v**3)))


K, T, S, H, P, N = 1536, 4096, 1024, 1024, 512, 768

def setup_inputs():
    n = np.random.standard_normal
    s = mx_kscale(K)[:, None]
    u = mx_kscale(H)[:, None]
    tab_words, tab_scales = pack_weight(n((K, T)) * s, "e4m3")
    wf_words, wf_scales = pack_weight(n((K, H)) / np.sqrt(K) / s, "e2m1")
    wt_words, wt_scales = pack_weight(0.7 * n((H, N)) / np.sqrt(H) / u, "e4m3")
    return {
        "tab_words": tab_words, "tab_scales": tab_scales,
        "offs": striped(np.random.permutation(T)[:S]),
        "pos1": striped(np.random.permutation(S)[:P]),
        "pos2": striped(np.random.permutation(S)[:P]),
        "pos3": striped(np.random.permutation(S)[:P]),
        "wf_words": wf_words, "wf_scales": wf_scales,
        "ga": (np.exp(0.3 * n(H)) * u[:, 0]).astype(np.float32),
        "gt": (np.exp(0.3 * n(H)) * u[:, 0]).astype(np.float32),
        "wa": (1.5 * n((H, N)) / np.sqrt(H) / u).astype(np.float32),
        "wt_words": wt_words, "wt_scales": wt_scales,
    }

def reference(tab_words, tab_scales, offs, pos1, pos2, pos3, wf_words, wf_scales, ga, gt, wa, wt_words, wt_scales):
    v = unpack_weight(tab_words, tab_scales, "e4m3")[:, unstriped(offs)]
    wf = unpack_weight(wf_words, wf_scales, "e2m1")
    h = wf.T @ v
    tree = h[:, unstriped(pos1)]
    awning = h[:, unstriped(pos2)]
    tower = h[:, unstriped(pos3)]
    za = f64(ga)[:, None] * (awning / (1.0 + np.exp(-tree)))
    zt = f64(gt)[:, None] * np.square(tower)
    wt = unpack_weight(wt_words, wt_scales, "e4m3")
    y = mxq(f64(wa), 0, "e4m3").T @ mxq(za, 0, "e4m3") + wt.T @ mxq(zt, 0, "e4m3")
    return 1.0 / (1.0 + np.exp(-y))

@@ -1,0 +1,310 @@
+from contextlib import ExitStack
+
+import concourse.mybir as mybir
+
+K, T, S, H, M, N = 1536, 4096, 1024, 1024, 512, 768
+FLOPS = 2 * K * H * S + 2 * 2 * H * N * M
+
+F32 = mybir.dt.float32
+BF16 = mybir.dt.bfloat16
+I32 = mybir.dt.int32
+U32 = mybir.dt.uint32
+U16 = mybir.dt.uint16
+U8 = mybir.dt.uint8
+FP8X4 = mybir.dt.float8_e4m3fn_x4
+FP4X4 = mybir.dt.float4_e2m1fn_x4
+ACT = mybir.ActivationFunctionType
+MULT = mybir.AluOpType.mult
+
+P = 128
+PACK = 4
+K_PASS = P * PACK
+A = K // K_PASS
+B = H // K_PASS
+BANK = 512
+QUADS = 4
+N_TILES = N // P
+WA_CHUNK = 256
+HALF = M // 2
+ODD = 4 * T
+
+
+def interleaved(tile_ap):
+    return tile_ap.rearrange("p (c i t) -> p c t i", i=4, t=PACK)
+
+
+def by_slot(tile_ap):
+    return tile_ap.rearrange("p t (c i) -> p c t i", i=4)
+
+
+def tile_list_street_shade_exposure_kernel(
+    tc, tab_words, tab_scales, offs, pos1, pos2, pos3, wf_words, wf_scales, ga, gt, wa, wt_words, wt_scales, out
+):
+    nc = tc.nc
+    with ExitStack() as ctx:
+        keep = ctx.enter_context(tc.tile_pool(name="keep", bufs=1))
+        stream = ctx.enter_context(tc.tile_pool(name="stream", bufs=1))
+        ring = ctx.enter_context(tc.tile_pool(name="ring", bufs=2))
+        psum = ctx.enter_context(tc.psum_pool(name="psum", bufs=1))
+
+        ts_rows = keep.tile([P, T], U8, name="ts_rows", align_bytes=64)
+        nc.vector.memset(ts_rows[:].bitcast(I32), 0)
+        wfs_raw = stream.tile([P, H], U8, name="wfs_raw", offset=2 * ODD - H // 2, align_bytes=64)
+        nc.gpsimd.memset(wfs_raw[:].bitcast(I32), 0)
+
+        offs_sb = keep.tile([P, S // 16], U16, name="offs_sb")
+        nc.sync.dma_start(offs_sb[:], offs)
+        wf_hbm = wf_words.bitcast(I32).rearrange("a p (b x) -> b p a x", b=B)
+
+        def load_wf(b):
+            raw = stream.tile([P, A * K_PASS * 2], U8, name="wf_raw%d" % b, offset=ODD, align_bytes=64)
+            nc.sync.dma_start(raw[:].bitcast(I32).rearrange("p (a x) -> p a x", a=A), wf_hbm[b])
+            return raw
+
+        def order_wf(b, raw):
+            ordered = keep.tile([P, A * K_PASS * 2], U8, name="wf_sb%d" % b, align_bytes=64)
+            nc.vector.tensor_copy(
+                ordered[:].bitcast(U16).rearrange("p (a t m) -> p t a m", t=PACK, m=P),
+                raw[:].bitcast(U16).rearrange("p (a m t) -> p t a m", t=PACK, m=P),
+            )
+            return ordered
+
+        wf_raw0 = load_wf(0)
+        pos_sb = []
+        for i, pos in enumerate((pos1, pos2, pos3)):
+            lst = keep.tile([P, M // 16], U16, name="pos%d" % i)
+            nc.sync.dma_start(lst[:], pos)
+            pos_sb.append(lst)
+
+        ts_hbm = tab_scales.rearrange("a q t -> (a q) t").bitcast(I32)
+        nc.sync.dma_start(ts_rows[:].bitcast(I32)[0:64:2, :], ts_hbm[0:32, :])
+        nc.sync.dma_start(ts_rows[:].bitcast(I32)[64:96:2, :], ts_hbm[32:48, :])
+
+        wfs_hbm = wf_scales.rearrange("a q c -> (a q) c").bitcast(I32)
+        nc.gpsimd.dma_start(wfs_raw[:].bitcast(I32)[0:96:2, :], wfs_hbm)
+        tab_sb = []
+
+        def load_table(a):
+            words = stream.tile([P, T], U32, name="tab%d" % a, offset=ODD * (a % 2), align_bytes=64)
+            nc.sync.dma_start(words[:].bitcast(I32), tab_words[a].rearrange("p t i -> p (t i)").bitcast(I32))
+            tab_sb.append(words)
+
+        load_table(0)
+
+        planes = keep.tile([P, A * (S + H)], U8, name="planes", align_bytes=64)
+        nc.gpsimd.memset(planes[:].bitcast(I32), 0)
+        pass_planes = [planes[:, a * (S + H) : (a + 1) * (S + H)] for a in range(A)]
+        wts = keep.tile([P, B * N], U8, name="wts", align_bytes=64)
+        nc.gpsimd.memset(wts[:].bitcast(I32), 0)
+        for q in range(QUADS):
+            nc.gpsimd.dma_start(
+                wts[:].bitcast(I32)[32 * q : 32 * q + 4, :].rearrange("r (b x) -> r b x", b=B),
+                wt_scales.bitcast(I32)[:, 4 * q : 4 * q + 4, :].rearrange("b r x -> r b x"),
+            )
+        gains = []
+        for name, g in (("ga_sb", ga), ("gt_sb", gt)):
+            g_sb = keep.tile([P, B, PACK], F32, name=name)
+            nc.gpsimd.dma_start(g_sb[:], g.rearrange("(b p t) -> p b t", b=B, t=PACK))
+            gains.append(g_sb)
+        ga_sb, gt_sb = gains
+        warm = keep.tile([P, 1], F32, name="warm")
+        warm_out = keep.tile([P, 1], F32, name="warm_out")
+        nc.vector.memset(warm[:], 0.0)
+        nc.scalar.activation(warm_out[:], warm[:], ACT.Sigmoid)
+
+        wf_sb = [order_wf(0, wf_raw0)]
+        rows = keep.tile([P, S + H], U8, name="rows", align_bytes=64)
+        nc.vector.tensor_copy(
+            rows[:, S : S + H].rearrange("p (b t m) -> p b t m", t=PACK, m=P),
+            wfs_raw[:].rearrange("p (b m t) -> p b t m", t=PACK, m=P),
+        )
+        load_table(1)
+        vs_rows = stream.tile([P, S], U8, name="vs_rows", offset=2 * ODD + 4 * BANK, align_bytes=64)
+        nc.vector.tensor_copy(vs_rows[:], ts_rows[:].indirect(offs_sb[:]))
+        nc.vector.tensor_copy(rows[:, 0:S].bitcast(I32), vs_rows[:].bitcast(I32))
+        for a in range(A):
+            for q in range(QUADS):
+                r0 = 2 * (16 * a + 4 * q)
+                nc.scalar.dma_start(
+                    pass_planes[a].bitcast(I32)[32 * q : 32 * q + 4, :], rows[:].bitcast(I32)[r0 : r0 + 8 : 2, :]
+                )
+
+        v_sb = []
+        for a in range(A):
+            picks = []
+            for h in range(S // BANK):
+                picked = stream.tile(
+                    [P, BANK], U32, name="v%d_%d" % (a, h), offset=2 * ODD + 4 * BANK * (2 * a + h), align_bytes=64
+                )
+                nc.vector.tensor_copy(picked[:], tab_sb[a][:].indirect(offs_sb[:, 32 * h : 32 * (h + 1)]))
+                picks.append(picked)
+            v_sb.append(picks)
+            if a == 0:
+                load_table(2)
+            if a == 1:
+                wf_raw1 = load_wf(1)
+        wf_sb.append(order_wf(1, wf_raw1))
+
+        wa_raw = []
+        for b in range(B):
+            raw = stream.tile([P, PACK, N], F32, name="wa_raw%d" % b, offset=(ODD + A * K_PASS * 2, 0)[b], align_bytes=64)
+            nc.sync.dma_start(raw[:], wa[b * K_PASS : (b + 1) * K_PASS, :].rearrange("(p j) n -> p j n", j=PACK))
+            wa_raw.append(raw)
+        wt_sb = stream.tile([P, B * N], U32, name="wt_sb", offset=4 * PACK * N, align_bytes=64)
+        nc.sync.dma_start(
+            wt_sb[:].bitcast(I32).rearrange("p (b n) -> p b n", b=B),
+            wt_words.rearrange("b p n i -> p b (n i)").bitcast(I32),
+        )
+
+        def bank(i):
+            return psum.tile([P, BANK], F32, name="bank%d" % i, tag="bank%d" % i)
+
+        def first_pass(acc, b, t, a, h):
+            w0 = a * K_PASS + t * P
+            s0 = S + b * K_PASS + t * P
+            nc.tensor.matmul_mx(
+                out=acc[:],
+                lhsT=wf_sb[b][:, 2 * w0 : 2 * (w0 + P)].bitcast(FP4X4),
+                lhsT_scale=pass_planes[a][:, s0 : s0 + P],
+                rhs=v_sb[a][h][:].bitcast(FP8X4),
+                rhs_scale=pass_planes[a][:, h * BANK : (h + 1) * BANK],
+                start=(a == 0),
+                stop=(a == A - 1),
+            )
+
+        h_banks = {}
+        for t in range(PACK):
+            for h in range(2):
+                h_banks[(t, h)] = bank(2 * t + h)
+        for a in range(A):
+            for h in range(2):
+                for t in range(PACK):
+                    first_pass(h_banks[(t, h)], 0, t, a, h)
+
+        wa_codes = keep.tile([P, B * N], U32, name="wa_codes", align_bytes=64)
+        wa_scales = keep.tile([P, B * N], U8, name="wa_scales", align_bytes=64)
+        wa_bf = [keep.tile([P, N * PACK], BF16, name="wa_bf%d" % b, align_bytes=64) for b in range(B)]
+
+        def round_wa(b, c):
+            nc.scalar.copy(
+                interleaved(wa_bf[b][:, c * WA_CHUNK * PACK : (c + 1) * WA_CHUNK * PACK]),
+                by_slot(wa_raw[b][:, :, c * WA_CHUNK : (c + 1) * WA_CHUNK]),
+            )
+
+        def quantize_wa(b):
+            for n0, n1 in ((0, 512), (512, N)):
+                nc.vector.quantize_mx(
+                    out=wa_codes[:, b * N + n0 : b * N + n1].bitcast(FP8X4),
+                    scales=wa_scales[:, b * N + n0 : b * N + n1],
+                    in_=wa_bf[b][:, n0 * PACK : n1 * PACK],
+                )
+
+        canopy = [keep.tile([P, PACK, M], F32, name="canopy%d" % b) for b in range(B)]
+        tower_sq = [keep.tile([P, PACK, M], F32, name="tower_sq%d" % b) for b in range(B)]
+        towers = {}
+        z_codes = {}
+
+        def look_up(b, t):
+            if b > 0:
+                for h in range(2):
+                    h_banks[(t, h)] = bank(2 * t + h)
+                    for a in range(A):
+                        first_pass(h_banks[(t, h)], b, t, a, h)
+            h_sb = ring.tile([P, S], F32, name="h_sb", bufs=8)
+            for h in range(2):
+                nc.scalar.copy(h_sb[:, h * BANK : (h + 1) * BANK], h_banks[(t, h)][:])
+            gate = ring.tile([P, M], F32, name="gate", bufs=4)
+            nc.scalar.activation(gate[:], h_sb[:].indirect(pos_sb[0][:]), ACT.Sigmoid)
+            tower = ring.tile([P, M], F32, name="tower", bufs=3)
+            nc.vector.tensor_copy(tower[:], h_sb[:].indirect(pos_sb[2][:]))
+            nc.vector.tensor_tensor(canopy[b][:, t, :], h_sb[:].indirect(pos_sb[1][:]), gate[:], MULT)
+            towers[(b, t)] = tower
+
+        def square(b, t):
+            nc.scalar.activation(tower_sq[b][:, t, :], towers[(b, t)][:], ACT.Square)
+
+        def apply_gain(name, b, cols):
+            src, gain = (tower_sq, gt_sb) if name == "zt" else (canopy, ga_sb)
+            width = cols.stop - cols.start
+            rounded = ring.tile([P, width * PACK], BF16, name="z_bf", bufs=3, align_bytes=64)
+            nc.vector.tensor_tensor(
+                interleaved(rounded[:]),
+                by_slot(src[b][:, :, cols]),
+                gain[:, b, :].unsqueeze(1).unsqueeze(3).to_broadcast([P, width // 4, PACK, 4]),
+                MULT,
+            )
+            return rounded
+
+        def quantize_map(name, b, cols, rounded):
+            codes, scales = z_codes[(name, b)]
+            nc.vector.quantize_mx(out=codes[:, cols].bitcast(FP8X4), scales=scales[:, cols], in_=rounded[:])
+
+        for name in ("za", "zt"):
+            for b in range(B):
+                codes = keep.tile([P, M], U32, name="%s_codes%d" % (name, b), align_bytes=64)
+                scales = keep.tile([P, M], U8, name="%s_scales%d" % (name, b), align_bytes=64)
+                z_codes[(name, b)] = (codes, scales)
+
+        whole = slice(0, M)
+        halves = [slice(0, HALF), slice(HALF, M)]
+        y_banks = {}
+
+        def second_passes(name, b, half, start, stop):
+            w_codes, w_scales = (wt_sb, wts) if name == "zt" else (wa_codes, wa_scales)
+            codes, scales = z_codes[(name, b)]
+            for pair in range(N_TILES // 2):
+                if start:
+                    y_banks[(half, pair)] = bank(half * (N_TILES // 2) + pair)
+                for j in range(2):
+                    n0 = b * N + (2 * pair + j) * P
+                    nc.tensor.matmul_mx(
+                        out=y_banks[(half, pair)][:, j * HALF : (j + 1) * HALF],
+                        lhsT=w_codes[:, n0 : n0 + P].bitcast(FP8X4),
+                        lhsT_scale=w_scales[:, n0 : n0 + P],
+                        rhs=codes[:, halves[half]].bitcast(FP8X4),
+                        rhs_scale=scales[:, halves[half]],
+                        start=(start and j == 0),
+                        stop=(stop and j == 1),
+                    )
+                if stop:
+                    result = keep.tile([P, 2, HALF], F32, name="result%d_%d" % (half, pair))
+                    nc.scalar.activation(
+                        result[:].rearrange("p j m -> p (j m)"), y_banks[(half, pair)][:], ACT.Sigmoid
+                    )
+                    rows_out = out[2 * pair * P : (2 * pair + 2) * P, halves[half]]
+                    nc.sync.dma_start(rows_out.rearrange("(j p) m -> p j m", p=P), result[:])
+
+        for t in range(PACK):
+            look_up(0, t)
+            if t > 0:
+                square(0, t - 1)
+        square(0, PACK - 1)
+        za0 = apply_gain("za", 0, whole)
+        zt0 = apply_gain("zt", 0, whole)
+        quantize_map("za", 0, whole, za0)
+        quantize_map("zt", 0, whole, zt0)
+        wa_pieces = [(b, c) for b in range(B) for c in range(N // WA_CHUNK)]
+        for t in range(PACK):
+            look_up(1, t)
+            if t < PACK - 1:
+                round_wa(*wa_pieces[2 * t])
+            if t > 0:
+                square(1, t - 1)
+            if t < PACK - 1:
+                round_wa(*wa_pieces[2 * t + 1])
+            if t in (1, 2):
+                quantize_wa(t - 1)
+        square(1, PACK - 1)
+        for half in range(2):
+            second_passes("zt", 0, half, True, False)
+            second_passes("za", 0, half, False, False)
+        zt1 = apply_gain("zt", 1, whole)
+        za1 = apply_gain("za", 1, halves[0])
+        quantize_map("zt", 1, whole, zt1)
+        quantize_map("za", 1, halves[0], za1)
+        for half in range(2):
+            second_passes("zt", 1, half, False, False)
+        second_passes("za", 1, 0, False, True)
+        za1 = apply_gain("za", 1, halves[1])
+        quantize_map("za", 1, halves[1], za1)
+        second_passes("za", 1, 1, False, True)

@@ -49,15 +49,30 @@ def tile_list_street_shade_exposure_kernel(
 
         ts_rows = keep.tile([P, T], U8, name="ts_rows", align_bytes=64)
         nc.vector.memset(ts_rows[:].bitcast(I32), 0)
-        wfs_raw = stream.tile([P, H], U8, name="wfs_raw", offset=2 * ODD - H // 2, align_bytes=64)
+        wfs_raw = keep.tile([P, H], U8, name="wfs_raw", align_bytes=64)
         nc.gpsimd.memset(wfs_raw[:].bitcast(I32), 0)
+
+        def load_rows(queue, rows_sb, rows_hbm):
+            rows_i32 = rows_hbm.rearrange("a q t -> (a q) t").bitcast(I32)
+            queue.dma_start(rows_sb[:].bitcast(I32)[0:64:2, :], rows_i32[0:32, :])
+            queue.dma_start(rows_sb[:].bitcast(I32)[64:96:2, :], rows_i32[32:48, :])
+
+        def row_home(a, q):
+            return 32 * a + 8 * q
+
+        nc.scalar.dma_start(wfs_raw[:].bitcast(I32)[0:96:2, :], wf_scales.rearrange("a q t -> (a q) t").bitcast(I32))
 
         offs_sb = keep.tile([P, S // 16], U16, name="offs_sb")
         nc.sync.dma_start(offs_sb[:], offs)
+        pos_sb = []
+        for i, pos in enumerate((pos1, pos2, pos3)):
+            lst = keep.tile([P, M // 16], U16, name="pos%d" % i)
+            nc.sync.dma_start(lst[:], pos)
+            pos_sb.append(lst)
+        load_rows(nc.sync, ts_rows, tab_scales)
         wf_hbm = wf_words.bitcast(I32).rearrange("a p (b x) -> b p a x", b=B)
 
-        def load_wf(b):
-            raw = stream.tile([P, A * K_PASS * 2], U8, name="wf_raw%d" % b, offset=ODD, align_bytes=64)
+        def load_wf(b, raw):
             nc.sync.dma_start(raw[:].bitcast(I32).rearrange("p (a x) -> p a x", a=A), wf_hbm[b])
             return raw
 
@@ -69,38 +84,20 @@ def tile_list_street_shade_exposure_kernel(
             )
             return ordered
 
-        wf_raw0 = load_wf(0)
-        pos_sb = []
-        for i, pos in enumerate((pos1, pos2, pos3)):
-            lst = keep.tile([P, M // 16], U16, name="pos%d" % i)
-            nc.sync.dma_start(lst[:], pos)
-            pos_sb.append(lst)
-
-        ts_hbm = tab_scales.rearrange("a q t -> (a q) t").bitcast(I32)
-        nc.sync.dma_start(ts_rows[:].bitcast(I32)[0:64:2, :], ts_hbm[0:32, :])
-        nc.sync.dma_start(ts_rows[:].bitcast(I32)[64:96:2, :], ts_hbm[32:48, :])
-
-        wfs_hbm = wf_scales.rearrange("a q c -> (a q) c").bitcast(I32)
-        nc.gpsimd.dma_start(wfs_raw[:].bitcast(I32)[0:96:2, :], wfs_hbm)
         tab_sb = []
 
         def load_table(a):
-            words = stream.tile([P, T], U32, name="tab%d" % a, offset=ODD * (a % 2), align_bytes=64)
+            words = stream.tile([P, T], U32, name="tab%d" % a, offset=ODD * a, align_bytes=64)
             nc.sync.dma_start(words[:].bitcast(I32), tab_words[a].rearrange("p t i -> p (t i)").bitcast(I32))
             tab_sb.append(words)
 
         load_table(0)
+        wf_raw0 = load_wf(0, keep.tile([P, A * K_PASS * 2], U8, name="wf_raw0", align_bytes=64))
+        load_table(1)
 
         planes = keep.tile([P, A * (S + H)], U8, name="planes", align_bytes=64)
-        nc.gpsimd.memset(planes[:].bitcast(I32), 0)
+        nc.vector.memset(planes[:].bitcast(I32), 0)
         pass_planes = [planes[:, a * (S + H) : (a + 1) * (S + H)] for a in range(A)]
-        wts = keep.tile([P, B * N], U8, name="wts", align_bytes=64)
-        nc.gpsimd.memset(wts[:].bitcast(I32), 0)
-        for q in range(QUADS):
-            nc.gpsimd.dma_start(
-                wts[:].bitcast(I32)[32 * q : 32 * q + 4, :].rearrange("r (b x) -> r b x", b=B),
-                wt_scales.bitcast(I32)[:, 4 * q : 4 * q + 4, :].rearrange("b r x -> r b x"),
-            )
         gains = []
         for name, g in (("ga_sb", ga), ("gt_sb", gt)):
             g_sb = keep.tile([P, B, PACK], F32, name=name)
@@ -112,49 +109,52 @@ def tile_list_street_shade_exposure_kernel(
         nc.vector.memset(warm[:], 0.0)
         nc.scalar.activation(warm_out[:], warm[:], ACT.Sigmoid)
 
-        wf_sb = [order_wf(0, wf_raw0)]
         rows = keep.tile([P, S + H], U8, name="rows", align_bytes=64)
+        vs_rows = stream.tile([P, S], U8, name="vs_rows", offset=2 * ODD, align_bytes=64)
+        nc.vector.tensor_copy(vs_rows[:], ts_rows[:].indirect(offs_sb[:]))
         nc.vector.tensor_copy(
             rows[:, S : S + H].rearrange("p (b t m) -> p b t m", t=PACK, m=P),
             wfs_raw[:].rearrange("p (b m t) -> p b t m", t=PACK, m=P),
         )
-        load_table(1)
-        vs_rows = stream.tile([P, S], U8, name="vs_rows", offset=2 * ODD + 4 * BANK, align_bytes=64)
-        nc.vector.tensor_copy(vs_rows[:], ts_rows[:].indirect(offs_sb[:]))
         nc.vector.tensor_copy(rows[:, 0:S].bitcast(I32), vs_rows[:].bitcast(I32))
-        for a in range(A):
-            for q in range(QUADS):
-                r0 = 2 * (16 * a + 4 * q)
-                nc.scalar.dma_start(
-                    pass_planes[a].bitcast(I32)[32 * q : 32 * q + 4, :], rows[:].bitcast(I32)[r0 : r0 + 8 : 2, :]
-                )
+        carries = [(a, q) for a in range(A) for q in range(QUADS)]
+        for i, (a, q) in enumerate(carries):
+            r0 = row_home(a, q)
+            nc.sync.dma_start(
+                pass_planes[a].bitcast(I32)[32 * q : 32 * q + 4, :], rows[:].bitcast(I32)[r0 : r0 + 8 : 2, :]
+            )
+            if i == 5:
+                load_table(2)
+        wf_sb = [order_wf(0, wf_raw0)]
 
         v_sb = []
         for a in range(A):
             picks = []
             for h in range(S // BANK):
-                picked = stream.tile(
-                    [P, BANK], U32, name="v%d_%d" % (a, h), offset=2 * ODD + 4 * BANK * (2 * a + h), align_bytes=64
-                )
+                picked = keep.tile([P, BANK], U32, name="v%d_%d" % (a, h), align_bytes=64)
                 nc.vector.tensor_copy(picked[:], tab_sb[a][:].indirect(offs_sb[:, 32 * h : 32 * (h + 1)]))
                 picks.append(picked)
             v_sb.append(picks)
-            if a == 0:
-                load_table(2)
-            if a == 1:
-                wf_raw1 = load_wf(1)
+        wf_raw1 = load_wf(1, stream.tile([P, A * K_PASS * 2], U8, name="wf_raw1", offset=0, align_bytes=64))
         wf_sb.append(order_wf(1, wf_raw1))
 
         wa_raw = []
         for b in range(B):
-            raw = stream.tile([P, PACK, N], F32, name="wa_raw%d" % b, offset=(ODD + A * K_PASS * 2, 0)[b], align_bytes=64)
+            raw = stream.tile([P, PACK, N], F32, name="wa_raw%d" % b, offset=(A * K_PASS * 2, ODD)[b], align_bytes=64)
             nc.sync.dma_start(raw[:], wa[b * K_PASS : (b + 1) * K_PASS, :].rearrange("(p j) n -> p j n", j=PACK))
             wa_raw.append(raw)
-        wt_sb = stream.tile([P, B * N], U32, name="wt_sb", offset=4 * PACK * N, align_bytes=64)
+        wt_sb = stream.tile([P, B * N], U32, name="wt_sb", offset=2 * ODD, align_bytes=64)
         nc.sync.dma_start(
             wt_sb[:].bitcast(I32).rearrange("p (b n) -> p b n", b=B),
             wt_words.rearrange("b p n i -> p b (n i)").bitcast(I32),
         )
+        wts = stream.tile([P, B * N], U8, name="wts", offset=2 * ODD + 4 * B * N, align_bytes=64)
+        nc.gpsimd.memset(wts[:].bitcast(I32), 0)
+        for q in range(QUADS):
+            nc.sync.dma_start(
+                wts[:].bitcast(I32)[32 * q : 32 * q + 4, :].rearrange("r (b x) -> r b x", b=B),
+                wt_scales.bitcast(I32)[:, 4 * q : 4 * q + 4, :].rearrange("b r x -> r b x"),
+            )
 
         def bank(i):
             return psum.tile([P, BANK], F32, name="bank%d" % i, tag="bank%d" % i)
@@ -176,9 +176,12 @@ def tile_list_street_shade_exposure_kernel(
         for t in range(PACK):
             for h in range(2):
                 h_banks[(t, h)] = bank(2 * t + h)
-        for a in range(A):
-            for h in range(2):
-                for t in range(PACK):
+        for h in range(2):
+            for t in range(PACK):
+                first_pass(h_banks[(t, h)], 0, t, 0, h)
+        for t in range(PACK):
+            for a in range(1, A):
+                for h in range(2):
                     first_pass(h_banks[(t, h)], 0, t, a, h)
 
         wa_codes = keep.tile([P, B * N], U32, name="wa_codes", align_bytes=64)
@@ -199,37 +202,53 @@ def tile_list_street_shade_exposure_kernel(
                     in_=wa_bf[b][:, n0 * PACK : n1 * PACK],
                 )
 
-        canopy = [keep.tile([P, PACK, M], F32, name="canopy%d" % b) for b in range(B)]
-        tower_sq = [keep.tile([P, PACK, M], F32, name="tower_sq%d" % b) for b in range(B)]
-        towers = {}
+        whole = slice(0, M)
+        halves = [slice(0, HALF), slice(HALF, M)]
+        h_sb = {}
+        work = {}
         z_codes = {}
 
-        def look_up(b, t):
+        def empty(b, t):
             if b > 0:
                 for h in range(2):
                     h_banks[(t, h)] = bank(2 * t + h)
                     for a in range(A):
                         first_pass(h_banks[(t, h)], b, t, a, h)
-            h_sb = ring.tile([P, S], F32, name="h_sb", bufs=8)
+            h_sb[(b, t)] = keep.tile([P, S], F32, name="h_sb%d_%d" % (b, t))
             for h in range(2):
-                nc.scalar.copy(h_sb[:, h * BANK : (h + 1) * BANK], h_banks[(t, h)][:])
-            gate = ring.tile([P, M], F32, name="gate", bufs=4)
-            nc.scalar.activation(gate[:], h_sb[:].indirect(pos_sb[0][:]), ACT.Sigmoid)
-            tower = ring.tile([P, M], F32, name="tower", bufs=3)
-            nc.vector.tensor_copy(tower[:], h_sb[:].indirect(pos_sb[2][:]))
-            nc.vector.tensor_tensor(canopy[b][:, t, :], h_sb[:].indirect(pos_sb[1][:]), gate[:], MULT)
-            towers[(b, t)] = tower
+                nc.scalar.copy(h_sb[(b, t)][:, h * BANK : (h + 1) * BANK], h_banks[(t, h)][:])
 
-        def square(b, t):
-            nc.scalar.activation(tower_sq[b][:, t, :], towers[(b, t)][:], ACT.Square)
+        def picked(b, t, which, cols):
+            return h_sb[(b, t)][:].indirect(pos_sb[which][:, cols.start // 16 : cols.stop // 16])
+
+        def piece_tile(name, b, cols):
+            key = (name, b, cols.start)
+            if key not in work:
+                work[key] = keep.tile([P, PACK, cols.stop - cols.start], F32, name="%s%d_%d" % key)
+            return work[key]
+
+        def gate(b, t, cols):
+            nc.scalar.activation(piece_tile("gate", b, cols)[:, t, :], picked(b, t, 0, cols), ACT.Sigmoid)
+
+        def tower(b, t, cols):
+            nc.vector.tensor_copy(piece_tile("tower", b, cols)[:, t, :], picked(b, t, 2, cols))
+
+        def canopy(b, t, cols):
+            nc.vector.tensor_tensor(
+                piece_tile("za", b, cols)[:, t, :], picked(b, t, 1, cols), piece_tile("gate", b, cols)[:, t, :], MULT
+            )
+
+        def square(b, t0, t1, cols):
+            tile = piece_tile("tower", b, cols)
+            nc.scalar.activation(tile[:, t0:t1, :], tile[:, t0:t1, :], ACT.Square)
 
         def apply_gain(name, b, cols):
-            src, gain = (tower_sq, gt_sb) if name == "zt" else (canopy, ga_sb)
+            src, gain = (piece_tile("tower", b, cols), gt_sb) if name == "zt" else (piece_tile("za", b, cols), ga_sb)
             width = cols.stop - cols.start
             rounded = ring.tile([P, width * PACK], BF16, name="z_bf", bufs=3, align_bytes=64)
             nc.vector.tensor_tensor(
                 interleaved(rounded[:]),
-                by_slot(src[b][:, :, cols]),
+                by_slot(src[:]),
                 gain[:, b, :].unsqueeze(1).unsqueeze(3).to_broadcast([P, width // 4, PACK, 4]),
                 MULT,
             )
@@ -245,8 +264,6 @@ def tile_list_street_shade_exposure_kernel(
                 scales = keep.tile([P, M], U8, name="%s_scales%d" % (name, b), align_bytes=64)
                 z_codes[(name, b)] = (codes, scales)
 
-        whole = slice(0, M)
-        halves = [slice(0, HALF), slice(HALF, M)]
         y_banks = {}
 
         def second_passes(name, b, half, start, stop):
@@ -266,45 +283,59 @@ def tile_list_street_shade_exposure_kernel(
                         start=(start and j == 0),
                         stop=(stop and j == 1),
                     )
-                if stop:
-                    result = keep.tile([P, 2, HALF], F32, name="result%d_%d" % (half, pair))
-                    nc.scalar.activation(
-                        result[:].rearrange("p j m -> p (j m)"), y_banks[(half, pair)][:], ACT.Sigmoid
-                    )
-                    rows_out = out[2 * pair * P : (2 * pair + 2) * P, halves[half]]
-                    nc.sync.dma_start(rows_out.rearrange("(j p) m -> p j m", p=P), result[:])
+
+        def finish(half):
+            for pair in range(N_TILES // 2):
+                result = keep.tile([P, 2, HALF], F32, name="result%d_%d" % (half, pair))
+                nc.scalar.activation(result[:].rearrange("p j m -> p (j m)"), y_banks[(half, pair)][:], ACT.Sigmoid)
+                rows_out = out[2 * pair * P : (2 * pair + 2) * P, halves[half]]
+                nc.sync.dma_start(rows_out.rearrange("(j p) m -> p j m", p=P), result[:])
 
         for t in range(PACK):
-            look_up(0, t)
-            if t > 0:
-                square(0, t - 1)
-        square(0, PACK - 1)
+            empty(0, t)
+            gate(0, t, whole)
+            tower(0, t, whole)
+            canopy(0, t, whole)
+        square(0, 0, PACK, whole)
         za0 = apply_gain("za", 0, whole)
         zt0 = apply_gain("zt", 0, whole)
         quantize_map("za", 0, whole, za0)
         quantize_map("zt", 0, whole, zt0)
-        wa_pieces = [(b, c) for b in range(B) for c in range(N // WA_CHUNK)]
+        first, last = halves
         for t in range(PACK):
-            look_up(1, t)
-            if t < PACK - 1:
-                round_wa(*wa_pieces[2 * t])
-            if t > 0:
-                square(1, t - 1)
-            if t < PACK - 1:
-                round_wa(*wa_pieces[2 * t + 1])
-            if t in (1, 2):
-                quantize_wa(t - 1)
-        square(1, PACK - 1)
+            empty(1, t)
+            gate(1, t, first)
+            tower(1, t, first)
+            canopy(1, t, first)
+        square(1, 0, PACK, first)
         for half in range(2):
             second_passes("zt", 0, half, True, False)
-            second_passes("za", 0, half, False, False)
-        zt1 = apply_gain("zt", 1, whole)
-        za1 = apply_gain("za", 1, halves[0])
-        quantize_map("zt", 1, whole, zt1)
-        quantize_map("za", 1, halves[0], za1)
+        for t in range(PACK):
+            gate(1, t, last)
+        za1 = apply_gain("za", 1, first)
+        zt1 = apply_gain("zt", 1, first)
+        quantize_map("za", 1, first, za1)
+        quantize_map("zt", 1, first, zt1)
+        second_passes("zt", 1, 0, False, False)
+        for c in range(N // WA_CHUNK):
+            round_wa(0, c)
+        for t in range(PACK):
+            tower(1, t, last)
+        quantize_wa(0)
         for half in range(2):
-            second_passes("zt", 1, half, False, False)
+            second_passes("za", 0, half, False, False)
+        square(1, 0, PACK, last)
+        for c in range(N // WA_CHUNK):
+            round_wa(1, c)
+        for t in range(PACK):
+            canopy(1, t, last)
+        quantize_wa(1)
         second_passes("za", 1, 0, False, True)
-        za1 = apply_gain("za", 1, halves[1])
-        quantize_map("za", 1, halves[1], za1)
+        finish(0)
+        zt1 = apply_gain("zt", 1, last)
+        za1 = apply_gain("za", 1, last)
+        quantize_map("zt", 1, last, zt1)
+        quantize_map("za", 1, last, za1)
+        second_passes("zt", 1, 1, False, False)
         second_passes("za", 1, 1, False, True)
+        finish(1)

@@ -15,6 +15,7 @@ FP8X4 = mybir.dt.float8_e4m3fn_x4
 FP4X4 = mybir.dt.float4_e2m1fn_x4
 ACT = mybir.ActivationFunctionType
 MULT = mybir.AluOpType.mult
+ADD = mybir.AluOpType.add
 
 P = 128
 PACK = 4
@@ -184,29 +185,48 @@ def tile_list_street_shade_exposure_kernel(
                 for h in range(2):
                     first_pass(h_banks[(t, h)], 0, t, a, h)
 
-        wa_codes = keep.tile([P, B * N], U32, name="wa_codes", align_bytes=64)
-        wa_scales = keep.tile([P, B * N], U8, name="wa_scales", align_bytes=64)
-        wa_bf = [keep.tile([P, N * PACK], BF16, name="wa_bf%d" % b, align_bytes=64) for b in range(B)]
-
-        def round_wa(b, c):
-            nc.scalar.copy(
-                interleaved(wa_bf[b][:, c * WA_CHUNK * PACK : (c + 1) * WA_CHUNK * PACK]),
-                by_slot(wa_raw[b][:, :, c * WA_CHUNK : (c + 1) * WA_CHUNK]),
-            )
-
-        def quantize_wa(b):
-            for n0, n1 in ((0, 512), (512, N)):
-                nc.vector.quantize_mx(
-                    out=wa_codes[:, b * N + n0 : b * N + n1].bitcast(FP8X4),
-                    scales=wa_scales[:, b * N + n0 : b * N + n1],
-                    in_=wa_bf[b][:, n0 * PACK : n1 * PACK],
-                )
-
+        arena = ctx.enter_context(tc.tile_pool(name="arena", bufs=1))
+        KB = 1024
         whole = slice(0, M)
-        halves = [slice(0, HALF), slice(HALF, M)]
+        first, last = slice(0, HALF), slice(HALF, M)
+        quarters = [slice(HALF, HALF + P), slice(HALF + P, M)]
         h_sb = {}
-        work = {}
         z_codes = {}
+        wa_tiles = {}
+        gate_at = [0, 2 * KB, 5 * KB, 7 * KB]
+        zt0_at = 12 * KB
+        tower1_at = 18 * KB
+        gates = {}
+        towers = [keep.tile([P, PACK, M], F32, name="tower0"), arena.tile([P, PACK, M], F32, name="tower1", offset=tower1_at, align_bytes=64)]
+        canopies = {}
+        za1_at = 30 * KB
+        gate1_at = 32 * KB
+        canopy_at = {(1, quarters[0].start): tower1_at + 4 * KB, (1, quarters[1].start): za1_at}
+
+        def round_wa(engine, b, n0, n1, offset):
+            rounded = arena.tile([P, (n1 - n0) * PACK], BF16, name="wa_bf%d_%d" % (b, n0), offset=offset, align_bytes=64)
+            src = wa_raw[b][:, :, n0:n1]
+            if engine == "pool":
+                nc.gpsimd.tensor_scalar(
+                    rounded[:].rearrange("p (c t) -> p c t", t=PACK), src.rearrange("p t c -> p c t"), 1.0, 0.0, MULT, ADD
+                )
+            else:
+                nc.scalar.copy(interleaved(rounded[:]), by_slot(src))
+            return (b, n0, n1, rounded)
+
+        def quantize_wa(piece, offset):
+            b, n0, n1, rounded = piece
+            codes = arena.tile([P, n1 - n0], U32, name="wa_codes%d_%d" % (b, n0), offset=offset, align_bytes=64)
+            scales = keep.tile([P, n1 - n0], U8, name="wa_scales%d_%d" % (b, n0), align_bytes=64)
+            nc.vector.quantize_mx(out=codes[:].bitcast(FP8X4), scales=scales[:], in_=rounded[:])
+            for n in range(n0, n1, P):
+                wa_tiles[(b, n // P)] = (codes[:, n - n0 : n - n0 + P], scales[:, n - n0 : n - n0 + P])
+
+        def weights(name, b, n_tile):
+            if name == "za":
+                return wa_tiles[(b, n_tile)]
+            n0 = b * N + n_tile * P
+            return wt_sb[:, n0 : n0 + P], wts[:, n0 : n0 + P]
 
         def empty(b, t):
             if b > 0:
@@ -221,31 +241,44 @@ def tile_list_street_shade_exposure_kernel(
         def picked(b, t, which, cols):
             return h_sb[(b, t)][:].indirect(pos_sb[which][:, cols.start // 16 : cols.stop // 16])
 
-        def piece_tile(name, b, cols):
-            key = (name, b, cols.start)
-            if key not in work:
-                work[key] = keep.tile([P, PACK, cols.stop - cols.start], F32, name="%s%d_%d" % key)
-            return work[key]
-
         def gate(b, t, cols):
-            nc.scalar.activation(piece_tile("gate", b, cols)[:, t, :], picked(b, t, 0, cols), ACT.Sigmoid)
+            shape = [P, cols.stop - cols.start]
+            key = (b, t, cols.start)
+            if b == 0:
+                gates[key] = arena.tile(shape, F32, name="gate0_%d" % t, offset=gate_at[t], align_bytes=64)
+            elif cols == first:
+                gates[key] = arena.tile(shape, F32, name="gate1_%d" % t, offset=gate1_at + t * KB, align_bytes=64)
+            else:
+                gates[key] = keep.tile(shape, F32, name="gate1_last%d" % t)
+            nc.scalar.activation(gates[key][:], picked(b, t, 0, cols), ACT.Sigmoid)
 
-        def tower(b, t, cols):
-            nc.vector.tensor_copy(piece_tile("tower", b, cols)[:, t, :], picked(b, t, 2, cols))
+        def tower(b, t):
+            nc.vector.tensor_copy(towers[b][:, t, :], picked(b, t, 2, whole))
 
         def canopy(b, t, cols):
-            nc.vector.tensor_tensor(
-                piece_tile("za", b, cols)[:, t, :], picked(b, t, 1, cols), piece_tile("gate", b, cols)[:, t, :], MULT
-            )
+            key = (b, cols.start)
+            if key not in canopies:
+                shape = [P, PACK, cols.stop - cols.start]
+                if key in canopy_at:
+                    canopies[key] = arena.tile(shape, F32, name="canopy%d_%d" % key, offset=canopy_at[key], align_bytes=64)
+                else:
+                    canopies[key] = keep.tile(shape, F32, name="canopy%d_%d" % key)
+            g0 = cols.start // HALF * HALF if b > 0 else 0
+            gated = gates[(b, t, g0)][:, cols.start - g0 : cols.stop - g0]
+            nc.vector.tensor_tensor(canopies[key][:, t, :], picked(b, t, 1, cols), gated, MULT)
 
-        def square(b, t0, t1, cols):
-            tile = piece_tile("tower", b, cols)
-            nc.scalar.activation(tile[:, t0:t1, :], tile[:, t0:t1, :], ACT.Square)
+        def square(b):
+            nc.scalar.activation(towers[b][:], towers[b][:], ACT.Square)
 
         def apply_gain(name, b, cols):
-            src, gain = (piece_tile("tower", b, cols), gt_sb) if name == "zt" else (piece_tile("za", b, cols), ga_sb)
+            src, gain = (towers[b], gt_sb) if name == "zt" else (canopies[(b, cols.start)], ga_sb)
             width = cols.stop - cols.start
-            rounded = ring.tile([P, width * PACK], BF16, name="z_bf", bufs=3, align_bytes=64)
+            if (name, b) == ("zt", 0):
+                rounded = arena.tile([P, width * PACK], BF16, name="zt0_bf", offset=zt0_at, align_bytes=64)
+            elif (name, b, cols.start) == ("za", 1, 0):
+                rounded = arena.tile([P, width * PACK], BF16, name="za1_bf", offset=za1_at, align_bytes=64)
+            else:
+                rounded = ring.tile([P, width * PACK], BF16, name="z_bf", bufs=2, align_bytes=64)
             nc.vector.tensor_tensor(
                 interleaved(rounded[:]),
                 by_slot(src[:]),
@@ -266,76 +299,100 @@ def tile_list_street_shade_exposure_kernel(
 
         y_banks = {}
 
-        def second_passes(name, b, half, start, stop):
-            w_codes, w_scales = (wt_sb, wts) if name == "zt" else (wa_codes, wa_scales)
+        def groups(cols):
+            width = cols.stop - cols.start
+            per_bank = 2 if width == HALF else 3
+            first_bank = 0 if cols.start < HALF else 3 + 2 * ((cols.start - HALF) // width)
+            return [(first_bank + g, range(g * per_bank, (g + 1) * per_bank)) for g in range(N_TILES // per_bank)]
+
+        def second_passes(name, b, cols, start, stop, only=range(N_TILES)):
             codes, scales = z_codes[(name, b)]
-            for pair in range(N_TILES // 2):
+            width = cols.stop - cols.start
+            for bank_no, n_tiles in groups(cols):
                 if start:
-                    y_banks[(half, pair)] = bank(half * (N_TILES // 2) + pair)
-                for j in range(2):
-                    n0 = b * N + (2 * pair + j) * P
+                    y_banks[bank_no] = bank(bank_no)
+                for j, n_tile in enumerate(n_tiles):
+                    if n_tile not in only:
+                        continue
+                    w_codes, w_scales = weights(name, b, n_tile)
                     nc.tensor.matmul_mx(
-                        out=y_banks[(half, pair)][:, j * HALF : (j + 1) * HALF],
-                        lhsT=w_codes[:, n0 : n0 + P].bitcast(FP8X4),
-                        lhsT_scale=w_scales[:, n0 : n0 + P],
-                        rhs=codes[:, halves[half]].bitcast(FP8X4),
-                        rhs_scale=scales[:, halves[half]],
+                        out=y_banks[bank_no][:, j * width : (j + 1) * width],
+                        lhsT=w_codes.bitcast(FP8X4),
+                        lhsT_scale=w_scales,
+                        rhs=codes[:, cols].bitcast(FP8X4),
+                        rhs_scale=scales[:, cols],
                         start=(start and j == 0),
-                        stop=(stop and j == 1),
+                        stop=(stop and j == len(n_tiles) - 1),
                     )
 
-        def finish(half):
-            for pair in range(N_TILES // 2):
-                result = keep.tile([P, 2, HALF], F32, name="result%d_%d" % (half, pair))
-                nc.scalar.activation(result[:].rearrange("p j m -> p (j m)"), y_banks[(half, pair)][:], ACT.Sigmoid)
-                rows_out = out[2 * pair * P : (2 * pair + 2) * P, halves[half]]
+        def finish(cols):
+            width = cols.stop - cols.start
+            for bank_no, n_tiles in groups(cols):
+                result = keep.tile([P, len(n_tiles), width], F32, name="result%d" % bank_no)
+                nc.scalar.activation(
+                    result[:].rearrange("p j m -> p (j m)"), y_banks[bank_no][:, 0 : len(n_tiles) * width], ACT.Sigmoid
+                )
+                rows_out = out[n_tiles.start * P : n_tiles.stop * P, cols]
                 nc.sync.dma_start(rows_out.rearrange("(j p) m -> p j m", p=P), result[:])
 
-        for t in range(PACK):
+        for t in range(2):
             empty(0, t)
             gate(0, t, whole)
-            tower(0, t, whole)
+            tower(0, t)
             canopy(0, t, whole)
-        square(0, 0, PACK, whole)
+        p1 = round_wa("pool", 0, 0, 128, 0)
+        p2 = round_wa("pool", 0, 256, 512, 2 * KB + 64)
+        p3 = round_wa("pool", 0, 128, 256, KB + 64)
+        empty(0, 2)
+        empty(0, 3)
+        gate(0, 2, whole)
+        gate(0, 3, whole)
+        tower(0, 2)
+        tower(0, 3)
+        canopy(0, 2, whole)
+        canopy(0, 3, whole)
+        square(0)
         za0 = apply_gain("za", 0, whole)
+        quantize_wa(p1, gate_at[3])
+        quantize_wa(p3, gate_at[3] + 512)
+        quantize_wa(p2, gate_at[3] + KB)
         zt0 = apply_gain("zt", 0, whole)
         quantize_map("za", 0, whole, za0)
         quantize_map("zt", 0, whole, zt0)
-        first, last = halves
+        p4 = round_wa("pool", 0, 512, 768, zt0_at - KB)
+        p5 = round_wa("pool", 1, 0, 256, zt0_at + KB)
+        p6 = round_wa("pool", 1, 256, 512, zt0_at + 3 * KB)
         for t in range(PACK):
             empty(1, t)
+            tower(1, t)
+        for cols in [first] + quarters:
+            second_passes("zt", 0, cols, True, False)
+        for cols in [first] + quarters:
+            second_passes("za", 0, cols, False, False, range(4))
+        for t in range(PACK):
             gate(1, t, first)
-            tower(1, t, first)
             canopy(1, t, first)
-        square(1, 0, PACK, first)
-        for half in range(2):
-            second_passes("zt", 0, half, True, False)
+        p7 = round_wa("act", 1, 512, 768, 27 * KB)
+        square(1)
         for t in range(PACK):
             gate(1, t, last)
+        for i, piece in enumerate((p4, p5, p6, p7)):
+            quantize_wa(piece, gate1_at + i * KB)
+        for cols in [first] + quarters:
+            second_passes("za", 0, cols, False, False, range(4, N_TILES))
         za1 = apply_gain("za", 1, first)
-        zt1 = apply_gain("zt", 1, first)
+        zt1 = apply_gain("zt", 1, whole)
         quantize_map("za", 1, first, za1)
-        quantize_map("zt", 1, first, zt1)
-        second_passes("zt", 1, 0, False, False)
-        for c in range(N // WA_CHUNK):
-            round_wa(0, c)
-        for t in range(PACK):
-            tower(1, t, last)
-        quantize_wa(0)
-        for half in range(2):
-            second_passes("za", 0, half, False, False)
-        square(1, 0, PACK, last)
-        for c in range(N // WA_CHUNK):
-            round_wa(1, c)
-        for t in range(PACK):
-            canopy(1, t, last)
-        quantize_wa(1)
-        second_passes("za", 1, 0, False, True)
-        finish(0)
-        zt1 = apply_gain("zt", 1, last)
-        za1 = apply_gain("za", 1, last)
-        quantize_map("zt", 1, last, zt1)
-        quantize_map("za", 1, last, za1)
-        second_passes("zt", 1, 1, False, False)
-        second_passes("za", 1, 1, False, True)
-        finish(1)
+        second_passes("za", 1, first, False, False)
+        quantize_map("zt", 1, whole, zt1)
+        second_passes("zt", 1, first, False, True)
+        finish(first)
+        for cols in quarters:
+            second_passes("zt", 1, cols, False, False)
+        for cols in quarters:
+            for t in range(PACK):
+                canopy(1, t, cols)
+            za1 = apply_gain("za", 1, cols)
+            quantize_map("za", 1, cols, za1)
+            second_passes("za", 1, cols, False, True)
+            finish(cols)

@@ -16,6 +16,9 @@ FP4X4 = mybir.dt.float4_e2m1fn_x4
 ACT = mybir.ActivationFunctionType
 MULT = mybir.AluOpType.mult
 ADD = mybir.AluOpType.add
+SUB = mybir.AluOpType.subtract
+MAX = mybir.AluOpType.max
+POW = mybir.AluOpType.pow
 
 P = 128
 PACK = 4
@@ -48,10 +51,13 @@ def tile_list_street_shade_exposure_kernel(
         ring = ctx.enter_context(tc.tile_pool(name="ring", bufs=2))
         psum = ctx.enter_context(tc.psum_pool(name="psum", bufs=1))
 
+        wfs_raw = keep.tile([P, H], U8, name="wfs_raw", align_bytes=64)
+        nc.vector.memset(wfs_raw[:].bitcast(I32), 0)
         ts_rows = keep.tile([P, T], U8, name="ts_rows", align_bytes=64)
         nc.vector.memset(ts_rows[:].bitcast(I32), 0)
-        wfs_raw = keep.tile([P, H], U8, name="wfs_raw", align_bytes=64)
-        nc.gpsimd.memset(wfs_raw[:].bitcast(I32), 0)
+        warm = keep.tile([P, 1], F32, name="warm")
+        warm_out = keep.tile([P, 1], F32, name="warm_out")
+        nc.vector.memset(warm[:], 0.0)
 
         def load_rows(queue, rows_sb, rows_hbm):
             rows_i32 = rows_hbm.rearrange("a q t -> (a q) t").bitcast(I32)
@@ -100,14 +106,11 @@ def tile_list_street_shade_exposure_kernel(
         nc.vector.memset(planes[:].bitcast(I32), 0)
         pass_planes = [planes[:, a * (S + H) : (a + 1) * (S + H)] for a in range(A)]
         gains = []
-        for name, g in (("ga_sb", ga), ("gt_sb", gt)):
+        for name, g in (("gt_sb", gt), ("ga_sb", ga)):
             g_sb = keep.tile([P, B, PACK], F32, name=name)
             nc.gpsimd.dma_start(g_sb[:], g.rearrange("(b p t) -> p b t", b=B, t=PACK))
             gains.append(g_sb)
-        ga_sb, gt_sb = gains
-        warm = keep.tile([P, 1], F32, name="warm")
-        warm_out = keep.tile([P, 1], F32, name="warm_out")
-        nc.vector.memset(warm[:], 0.0)
+        gt_sb, ga_sb = gains
         nc.scalar.activation(warm_out[:], warm[:], ACT.Sigmoid)
 
         rows = keep.tile([P, S + H], U8, name="rows", align_bytes=64)
@@ -185,6 +188,28 @@ def tile_list_street_shade_exposure_kernel(
                 for h in range(2):
                     first_pass(h_banks[(t, h)], 0, t, a, h)
 
+        def small(name):
+            return keep.tile([P, B * PACK], F32, name=name)
+
+        gt_flat = gt_sb[:].rearrange("p b t -> p (b t)")
+        size, sign = small("size"), small("sign")
+        nc.scalar.activation(size[:], gt_flat, ACT.Abs)
+        nc.scalar.activation(sign[:], gt_flat, ACT.Sign)
+        minus_half, floor, inv_root, root, rest = (small(n) for n in ("minus_half", "floor", "inv_root", "root", "rest"))
+        nc.gpsimd.memset(minus_half[:], -0.5)
+        nc.gpsimd.tensor_scalar(floor[:], size[:], 1e-37, None, MAX)
+        nc.gpsimd.tensor_tensor(inv_root[:], floor[:], minus_half[:], POW)
+        nc.gpsimd.tensor_tensor(root[:], size[:], inv_root[:], MULT)
+        nc.gpsimd.tensor_tensor(rest[:], root[:], root[:], MULT)
+        nc.gpsimd.tensor_tensor(rest[:], size[:], rest[:], SUB)
+        nc.gpsimd.tensor_tensor(rest[:], rest[:], inv_root[:], MULT)
+        nc.gpsimd.tensor_scalar(rest[:], rest[:], 0.5, None, MULT)
+        nc.gpsimd.tensor_tensor(root[:], root[:], rest[:], ADD)
+        roots = keep.tile([P, B * PACK, M], F32, name="roots")
+        nc.scalar.copy(roots[:], root[:].unsqueeze(2).to_broadcast([P, B * PACK, M]))
+        signs = keep.tile([P, B, P, PACK], BF16, name="signs", align_bytes=64)
+        nc.scalar.copy(signs[:], sign[:].rearrange("p (b t) -> p b t", b=B).unsqueeze(2).to_broadcast([P, B, P, PACK]))
+
         arena = ctx.enter_context(tc.tile_pool(name="arena", bufs=1))
         KB = 1024
         whole = slice(0, M)
@@ -206,10 +231,8 @@ def tile_list_street_shade_exposure_kernel(
         def round_wa(engine, b, n0, n1, offset):
             rounded = arena.tile([P, (n1 - n0) * PACK], BF16, name="wa_bf%d_%d" % (b, n0), offset=offset, align_bytes=64)
             src = wa_raw[b][:, :, n0:n1]
-            if engine == "pool":
-                nc.gpsimd.tensor_scalar(
-                    rounded[:].rearrange("p (c t) -> p c t", t=PACK), src.rearrange("p t c -> p c t"), 1.0, 0.0, MULT, ADD
-                )
+            if engine == "dve":
+                nc.vector.tensor_copy(interleaved(rounded[:]), by_slot(src))
             else:
                 nc.scalar.copy(interleaved(rounded[:]), by_slot(src))
             return (b, n0, n1, rounded)
@@ -253,7 +276,7 @@ def tile_list_street_shade_exposure_kernel(
             nc.scalar.activation(gates[key][:], picked(b, t, 0, cols), ACT.Sigmoid)
 
         def tower(b, t):
-            nc.vector.tensor_copy(towers[b][:, t, :], picked(b, t, 2, whole))
+            nc.vector.tensor_tensor(towers[b][:, t, :], picked(b, t, 2, whole), roots[:, PACK * b + t, :], MULT)
 
         def canopy(b, t, cols):
             key = (b, cols.start)
@@ -268,7 +291,15 @@ def tile_list_street_shade_exposure_kernel(
             nc.vector.tensor_tensor(canopies[key][:, t, :], picked(b, t, 1, cols), gated, MULT)
 
         def square(b):
-            nc.scalar.activation(towers[b][:], towers[b][:], ACT.Square)
+            squared = arena.tile([P, M * PACK], BF16, name="zt_bf%d" % b, offset=zt0_at, align_bytes=64)
+            nc.scalar.activation(interleaved(squared[:]), by_slot(towers[b][:]), ACT.Square)
+            return squared
+
+        def apply_sign(b, squared):
+            runs = squared[:].rearrange("p (r x) -> p r x", x=P * PACK)
+            pattern = signs[:, b, :, :].rearrange("p m t -> p (m t)").unsqueeze(1).to_broadcast([P, M // P, P * PACK])
+            nc.vector.tensor_tensor(runs, runs, pattern, MULT)
+            return squared
 
         def apply_gain(name, b, cols):
             src, gain = (towers[b], gt_sb) if name == "zt" else (canopies[(b, cols.start)], ga_sb)
@@ -335,57 +366,45 @@ def tile_list_street_shade_exposure_kernel(
                 rows_out = out[n_tiles.start * P : n_tiles.stop * P, cols]
                 nc.sync.dma_start(rows_out.rearrange("(j p) m -> p j m", p=P), result[:])
 
-        for t in range(2):
+        for t in range(PACK):
             empty(0, t)
             gate(0, t, whole)
             tower(0, t)
             canopy(0, t, whole)
-        p1 = round_wa("pool", 0, 0, 128, 0)
-        p2 = round_wa("pool", 0, 256, 512, 2 * KB + 64)
-        p3 = round_wa("pool", 0, 128, 256, KB + 64)
-        empty(0, 2)
-        empty(0, 3)
-        gate(0, 2, whole)
-        gate(0, 3, whole)
-        tower(0, 2)
-        tower(0, 3)
-        canopy(0, 2, whole)
-        canopy(0, 3, whole)
-        square(0)
+        empty(1, 0)
+        sq0 = square(0)
         za0 = apply_gain("za", 0, whole)
-        quantize_wa(p1, gate_at[3])
-        quantize_wa(p3, gate_at[3] + 512)
-        quantize_wa(p2, gate_at[3] + KB)
-        zt0 = apply_gain("zt", 0, whole)
+        p1 = round_wa("dve", 0, 0, 256, 8 * KB)
         quantize_map("za", 0, whole, za0)
+        zt0 = apply_sign(0, sq0)
+        quantize_wa(p1, 36 * KB)
         quantize_map("zt", 0, whole, zt0)
-        p4 = round_wa("pool", 0, 512, 768, zt0_at - KB)
-        p5 = round_wa("pool", 1, 0, 256, zt0_at + KB)
-        p6 = round_wa("pool", 1, 256, 512, zt0_at + 3 * KB)
         for t in range(PACK):
-            empty(1, t)
+            if t > 0:
+                empty(1, t)
             tower(1, t)
         for cols in [first] + quarters:
             second_passes("zt", 0, cols, True, False)
-        for cols in [first] + quarters:
-            second_passes("za", 0, cols, False, False, range(4))
         for t in range(PACK):
             gate(1, t, first)
             canopy(1, t, first)
-        p7 = round_wa("act", 1, 512, 768, 27 * KB)
-        square(1)
+        p2 = round_wa("act", 0, 256, 768, 0)
+        sq1 = square(1)
         for t in range(PACK):
             gate(1, t, last)
-        for i, piece in enumerate((p4, p5, p6, p7)):
-            quantize_wa(piece, gate1_at + i * KB)
+        p3 = round_wa("act", 1, 0, 512, 4 * KB)
+        p4 = round_wa("dve", 1, 512, 768, gate1_at)
+        quantize_wa(p2, 28 * KB)
         for cols in [first] + quarters:
-            second_passes("za", 0, cols, False, False, range(4, N_TILES))
+            second_passes("za", 0, cols, False, False)
         za1 = apply_gain("za", 1, first)
-        zt1 = apply_gain("zt", 1, whole)
+        quantize_wa(p4, 37 * KB)
+        zt1 = apply_sign(1, sq1)
         quantize_map("za", 1, first, za1)
-        second_passes("za", 1, first, False, False)
         quantize_map("zt", 1, whole, zt1)
-        second_passes("zt", 1, first, False, True)
+        quantize_wa(p3, 38 * KB)
+        second_passes("zt", 1, first, False, False)
+        second_passes("za", 1, first, False, True)
         finish(first)
         for cols in quarters:
             second_passes("zt", 1, cols, False, False)

@@ -54,15 +54,15 @@ def tile_list_street_shade_exposure_kernel(
         wfs_raw = keep.tile([P, H], U8, name="wfs_raw", align_bytes=64)
         nc.vector.memset(wfs_raw[:].bitcast(I32), 0)
         ts_rows = keep.tile([P, T], U8, name="ts_rows", align_bytes=64)
-        nc.vector.memset(ts_rows[:].bitcast(I32), 0)
+        nc.gpsimd.memset(ts_rows[:].bitcast(I32)[:, 0:640], 0)
+        nc.vector.memset(ts_rows[:].bitcast(I32)[:, 640:1024], 0)
         warm = keep.tile([P, 1], F32, name="warm")
         warm_out = keep.tile([P, 1], F32, name="warm_out")
         nc.vector.memset(warm[:], 0.0)
 
         def load_rows(queue, rows_sb, rows_hbm):
             rows_i32 = rows_hbm.rearrange("a q t -> (a q) t").bitcast(I32)
-            queue.dma_start(rows_sb[:].bitcast(I32)[0:64:2, :], rows_i32[0:32, :])
-            queue.dma_start(rows_sb[:].bitcast(I32)[64:96:2, :], rows_i32[32:48, :])
+            queue.dma_start(rows_sb[:].bitcast(I32)[0:96:2, :], rows_i32)
 
         def row_home(a, q):
             return 32 * a + 8 * q
@@ -71,18 +71,19 @@ def tile_list_street_shade_exposure_kernel(
 
         offs_sb = keep.tile([P, S // 16], U16, name="offs_sb")
         nc.sync.dma_start(offs_sb[:], offs)
-        pos_sb = []
-        for i, pos in enumerate((pos1, pos2, pos3)):
-            lst = keep.tile([P, M // 16], U16, name="pos%d" % i)
-            nc.sync.dma_start(lst[:], pos)
-            pos_sb.append(lst)
-        load_rows(nc.sync, ts_rows, tab_scales)
         wf_hbm = wf_words.bitcast(I32).rearrange("a p (b x) -> b p a x", b=B)
 
         def load_wf(b, raw):
             nc.sync.dma_start(raw[:].bitcast(I32).rearrange("p (a x) -> p a x", a=A), wf_hbm[b])
             return raw
 
+        wf_raw0 = load_wf(0, keep.tile([P, A * K_PASS * 2], U8, name="wf_raw0", align_bytes=64))
+        pos_sb = []
+        for i, pos in enumerate((pos1, pos2, pos3)):
+            lst = keep.tile([P, M // 16], U16, name="pos%d" % i)
+            nc.sync.dma_start(lst[:], pos)
+            pos_sb.append(lst)
+        load_rows(nc.sync, ts_rows, tab_scales)
         def order_wf(b, raw):
             ordered = keep.tile([P, A * K_PASS * 2], U8, name="wf_sb%d" % b, align_bytes=64)
             nc.vector.tensor_copy(
@@ -99,7 +100,6 @@ def tile_list_street_shade_exposure_kernel(
             tab_sb.append(words)
 
         load_table(0)
-        wf_raw0 = load_wf(0, keep.tile([P, A * K_PASS * 2], U8, name="wf_raw0", align_bytes=64))
         load_table(1)
 
         planes = keep.tile([P, A * (S + H)], U8, name="planes", align_bytes=64)
@@ -195,16 +195,9 @@ def tile_list_street_shade_exposure_kernel(
         size, sign = small("size"), small("sign")
         nc.scalar.activation(size[:], gt_flat, ACT.Abs)
         nc.scalar.activation(sign[:], gt_flat, ACT.Sign)
-        minus_half, floor, inv_root, root, rest = (small(n) for n in ("minus_half", "floor", "inv_root", "root", "rest"))
-        nc.gpsimd.memset(minus_half[:], -0.5)
-        nc.gpsimd.tensor_scalar(floor[:], size[:], 1e-37, None, MAX)
-        nc.gpsimd.tensor_tensor(inv_root[:], floor[:], minus_half[:], POW)
-        nc.gpsimd.tensor_tensor(root[:], size[:], inv_root[:], MULT)
-        nc.gpsimd.tensor_tensor(rest[:], root[:], root[:], MULT)
-        nc.gpsimd.tensor_tensor(rest[:], size[:], rest[:], SUB)
-        nc.gpsimd.tensor_tensor(rest[:], rest[:], inv_root[:], MULT)
-        nc.gpsimd.tensor_scalar(rest[:], rest[:], 0.5, None, MULT)
-        nc.gpsimd.tensor_tensor(root[:], root[:], rest[:], ADD)
+        half, root = small("half"), small("root")
+        nc.gpsimd.memset(half[:], 0.5)
+        nc.gpsimd.tensor_tensor(root[:], size[:], half[:], POW)
         roots = keep.tile([P, B * PACK, M], F32, name="roots")
         nc.scalar.copy(roots[:], root[:].unsqueeze(2).to_broadcast([P, B * PACK, M]))
         signs = keep.tile([P, B, P, PACK], BF16, name="signs", align_bytes=64)
@@ -371,13 +364,14 @@ def tile_list_street_shade_exposure_kernel(
             gate(0, t, whole)
             tower(0, t)
             canopy(0, t, whole)
+            if t == 2:
+                p1 = round_wa("dve", 0, 0, 256, gate_at[2])
         empty(1, 0)
         sq0 = square(0)
+        quantize_wa(p1, gate_at[3])
         za0 = apply_gain("za", 0, whole)
-        p1 = round_wa("dve", 0, 0, 256, 8 * KB)
-        quantize_map("za", 0, whole, za0)
         zt0 = apply_sign(0, sq0)
-        quantize_wa(p1, 36 * KB)
+        quantize_map("za", 0, whole, za0)
         quantize_map("zt", 0, whole, zt0)
         for t in range(PACK):
             if t > 0:
@@ -388,13 +382,13 @@ def tile_list_street_shade_exposure_kernel(
         for t in range(PACK):
             gate(1, t, first)
             canopy(1, t, first)
-        p2 = round_wa("act", 0, 256, 768, 0)
+        p2 = round_wa("act", 0, 256, 768, 26 * KB)
         sq1 = square(1)
         for t in range(PACK):
             gate(1, t, last)
-        p3 = round_wa("act", 1, 0, 512, 4 * KB)
+        p3 = round_wa("act", 1, 0, 512, 3 * KB)
         p4 = round_wa("dve", 1, 512, 768, gate1_at)
-        quantize_wa(p2, 28 * KB)
+        quantize_wa(p2, 0)
         for cols in [first] + quarters:
             second_passes("za", 0, cols, False, False)
         za1 = apply_gain("za", 1, first)
@@ -408,10 +402,18 @@ def tile_list_street_shade_exposure_kernel(
         finish(first)
         for cols in quarters:
             second_passes("zt", 1, cols, False, False)
-        for cols in quarters:
-            for t in range(PACK):
-                canopy(1, t, cols)
-            za1 = apply_gain("za", 1, cols)
-            quantize_map("za", 1, cols, za1)
-            second_passes("za", 1, cols, False, True)
-            finish(cols)
+        third, fourth = quarters
+        for t in range(PACK):
+            canopy(1, t, third)
+        canopy(1, 0, fourth)
+        za1 = apply_gain("za", 1, third)
+        canopy(1, 1, fourth)
+        quantize_map("za", 1, third, za1)
+        second_passes("za", 1, third, False, True)
+        finish(third)
+        for t in range(2, PACK):
+            canopy(1, t, fourth)
+        za1 = apply_gain("za", 1, fourth)
+        quantize_map("za", 1, fourth, za1)
+        second_passes("za", 1, fourth, False, True)
+        finish(fourth)

@@ -31,6 +31,8 @@ N_TILES = N // P
 WA_CHUNK = 256
 HALF = M // 2
 ODD = 4 * T
+ROW0 = 36
+SIGN_COLS = 16
 
 
 def interleaved(tile_ap):
@@ -62,12 +64,12 @@ def tile_list_street_shade_exposure_kernel(
 
         def load_rows(queue, rows_sb, rows_hbm):
             rows_i32 = rows_hbm.rearrange("a q t -> (a q) t").bitcast(I32)
-            queue.dma_start(rows_sb[:].bitcast(I32)[0:96:2, :], rows_i32)
+            queue.dma_start(rows_sb[:].bitcast(I32)[ROW0 : ROW0 + 16 * A, :], rows_i32)
 
         def row_home(a, q):
-            return 32 * a + 8 * q
+            return ROW0 + 16 * a + 4 * q
 
-        nc.scalar.dma_start(wfs_raw[:].bitcast(I32)[0:96:2, :], wf_scales.rearrange("a q t -> (a q) t").bitcast(I32))
+        nc.scalar.dma_start(wfs_raw[:].bitcast(I32)[ROW0 : ROW0 + 16 * A, :], wf_scales.rearrange("a q t -> (a q) t").bitcast(I32))
 
         offs_sb = keep.tile([P, S // 16], U16, name="offs_sb")
         nc.sync.dma_start(offs_sb[:], offs)
@@ -121,11 +123,11 @@ def tile_list_street_shade_exposure_kernel(
             wfs_raw[:].rearrange("p (b m t) -> p b t m", t=PACK, m=P),
         )
         nc.vector.tensor_copy(rows[:, 0:S].bitcast(I32), vs_rows[:].bitcast(I32))
-        carries = [(a, q) for a in range(A) for q in range(QUADS)]
+        carries = [(0, q) for q in range(QUADS)] + [(1, 0), (1, 1), (1, 2), (2, 0), (1, 3), (2, 1), (2, 2), (2, 3)]
         for i, (a, q) in enumerate(carries):
             r0 = row_home(a, q)
             nc.sync.dma_start(
-                pass_planes[a].bitcast(I32)[32 * q : 32 * q + 4, :], rows[:].bitcast(I32)[r0 : r0 + 8 : 2, :]
+                pass_planes[a].bitcast(I32)[32 * q : 32 * q + 4, :], rows[:].bitcast(I32)[r0 : r0 + 4, :]
             )
             if i == 5:
                 load_table(2)
@@ -200,8 +202,10 @@ def tile_list_street_shade_exposure_kernel(
         nc.gpsimd.tensor_tensor(root[:], size[:], half[:], POW)
         roots = keep.tile([P, B * PACK, M], F32, name="roots")
         nc.scalar.copy(roots[:], root[:].unsqueeze(2).to_broadcast([P, B * PACK, M]))
-        signs = keep.tile([P, B, P, PACK], BF16, name="signs", align_bytes=64)
-        nc.scalar.copy(signs[:], sign[:].rearrange("p (b t) -> p b t", b=B).unsqueeze(2).to_broadcast([P, B, P, PACK]))
+        signs = keep.tile([P, B, SIGN_COLS, PACK], BF16, name="signs", align_bytes=64)
+        nc.scalar.copy(
+            signs[:], sign[:].rearrange("p (b t) -> p b t", b=B).unsqueeze(2).to_broadcast([P, B, SIGN_COLS, PACK])
+        )
 
         arena = ctx.enter_context(tc.tile_pool(name="arena", bufs=1))
         KB = 1024
@@ -289,8 +293,8 @@ def tile_list_street_shade_exposure_kernel(
             return squared
 
         def apply_sign(b, squared):
-            runs = squared[:].rearrange("p (r x) -> p r x", x=P * PACK)
-            pattern = signs[:, b, :, :].rearrange("p m t -> p (m t)").unsqueeze(1).to_broadcast([P, M // P, P * PACK])
+            runs = squared[:].rearrange("p (r x) -> p r x", x=SIGN_COLS * PACK)
+            pattern = signs[:, b, :, :].rearrange("p m t -> p (m t)").unsqueeze(1).to_broadcast([P, M // SIGN_COLS, SIGN_COLS * PACK])
             nc.vector.tensor_tensor(runs, runs, pattern, MULT)
             return squared
 

@@ -56,8 +56,7 @@ def tile_list_street_shade_exposure_kernel(
         wfs_raw = keep.tile([P, H], U8, name="wfs_raw", align_bytes=64)
         nc.vector.memset(wfs_raw[:].bitcast(I32), 0)
         ts_rows = keep.tile([P, T], U8, name="ts_rows", align_bytes=64)
-        nc.gpsimd.memset(ts_rows[:].bitcast(I32)[:, 0:640], 0)
-        nc.vector.memset(ts_rows[:].bitcast(I32)[:, 640:1024], 0)
+        nc.vector.memset(ts_rows[:].bitcast(I32), 0)
         warm = keep.tile([P, 1], F32, name="warm")
         warm_out = keep.tile([P, 1], F32, name="warm_out")
         nc.vector.memset(warm[:], 0.0)
@@ -72,14 +71,20 @@ def tile_list_street_shade_exposure_kernel(
         nc.scalar.dma_start(wfs_raw[:].bitcast(I32)[ROW0 : ROW0 + 16 * A, :], wf_scales.rearrange("a q t -> (a q) t").bitcast(I32))
 
         offs_sb = keep.tile([P, S // 16], U16, name="offs_sb")
-        nc.sync.dma_start(offs_sb[:], offs)
         wf_hbm = wf_words.bitcast(I32).rearrange("a p (b x) -> b p a x", b=B)
 
         def load_wf(b, raw):
             nc.sync.dma_start(raw[:].bitcast(I32).rearrange("p (a x) -> p a x", a=A), wf_hbm[b])
             return raw
 
-        wf_raw0 = load_wf(0, keep.tile([P, A * K_PASS * 2], U8, name="wf_raw0", align_bytes=64))
+        tab_sb = [stream.tile([P, T], U32, name="tab0", offset=0, align_bytes=64)]
+
+        def load_columns(a, t0, t1):
+            words = tab_words[a].rearrange("p t i -> p (t i)").bitcast(I32)
+            nc.sync.dma_start(tab_sb[a][:].bitcast(I32)[:, t0:t1], words[:, t0:t1])
+
+        load_columns(0, 0, T // 2)
+        nc.sync.dma_start(offs_sb[:], offs)
         pos_sb = []
         for i, pos in enumerate((pos1, pos2, pos3)):
             lst = keep.tile([P, M // 16], U16, name="pos%d" % i)
@@ -94,14 +99,12 @@ def tile_list_street_shade_exposure_kernel(
             )
             return ordered
 
-        tab_sb = []
-
         def load_table(a):
-            words = stream.tile([P, T], U32, name="tab%d" % a, offset=ODD * a, align_bytes=64)
-            nc.sync.dma_start(words[:].bitcast(I32), tab_words[a].rearrange("p t i -> p (t i)").bitcast(I32))
-            tab_sb.append(words)
+            tab_sb.append(stream.tile([P, T], U32, name="tab%d" % a, offset=ODD * a, align_bytes=64))
+            load_columns(a, 0, T)
 
-        load_table(0)
+        load_columns(0, T // 2, T)
+        wf_raw0 = load_wf(0, keep.tile([P, A * K_PASS * 2], U8, name="wf_raw0", align_bytes=64))
         load_table(1)
 
         planes = keep.tile([P, A * (S + H)], U8, name="planes", align_bytes=64)

@@ -31,7 +31,7 @@ N_TILES = N // P
 WA_CHUNK = 256
 HALF = M // 2
 ODD = 4 * T
-ROW0 = 36
+ROW0 = 40
 SIGN_COLS = 16
 
 
@@ -64,9 +64,6 @@ def tile_list_street_shade_exposure_kernel(
         def load_rows(queue, rows_sb, rows_hbm):
             rows_i32 = rows_hbm.rearrange("a q t -> (a q) t").bitcast(I32)
             queue.dma_start(rows_sb[:].bitcast(I32)[ROW0 : ROW0 + 16 * A, :], rows_i32)
-
-        def row_home(a, q):
-            return ROW0 + 16 * a + 4 * q
 
         nc.scalar.dma_start(wfs_raw[:].bitcast(I32)[ROW0 : ROW0 + 16 * A, :], wf_scales.rearrange("a q t -> (a q) t").bitcast(I32))
 
@@ -107,9 +104,10 @@ def tile_list_street_shade_exposure_kernel(
         wf_raw0 = load_wf(0, keep.tile([P, A * K_PASS * 2], U8, name="wf_raw0", align_bytes=64))
         load_table(1)
 
-        planes = keep.tile([P, A * (S + H)], U8, name="planes", align_bytes=64)
+        planes = keep.tile([P, 2 * (S + H)], U8, name="planes", align_bytes=64)
         nc.vector.memset(planes[:].bitcast(I32), 0)
-        pass_planes = [planes[:, a * (S + H) : (a + 1) * (S + H)] for a in range(A)]
+        rows = keep.tile([P, S + H], U8, name="rows", align_bytes=64)
+        pass_planes = [planes[:, 0 : S + H], rows[:], planes[:, S + H : 2 * (S + H)]]
         gains = []
         for name, g in (("gt_sb", gt), ("ga_sb", ga)):
             g_sb = keep.tile([P, B, PACK], F32, name=name)
@@ -118,7 +116,6 @@ def tile_list_street_shade_exposure_kernel(
         gt_sb, ga_sb = gains
         nc.scalar.activation(warm_out[:], warm[:], ACT.Sigmoid)
 
-        rows = keep.tile([P, S + H], U8, name="rows", align_bytes=64)
         vs_rows = stream.tile([P, S], U8, name="vs_rows", offset=2 * ODD, align_bytes=64)
         nc.vector.tensor_copy(vs_rows[:], ts_rows[:].indirect(offs_sb[:]))
         nc.vector.tensor_copy(
@@ -126,14 +123,14 @@ def tile_list_street_shade_exposure_kernel(
             wfs_raw[:].rearrange("p (b m t) -> p b t m", t=PACK, m=P),
         )
         nc.vector.tensor_copy(rows[:, 0:S].bitcast(I32), vs_rows[:].bitcast(I32))
-        carries = [(0, q) for q in range(QUADS)] + [(1, 0), (1, 1), (1, 2), (2, 0), (1, 3), (2, 1), (2, 2), (2, 3)]
-        for i, (a, q) in enumerate(carries):
-            r0 = row_home(a, q)
-            nc.sync.dma_start(
-                pass_planes[a].bitcast(I32)[32 * q : 32 * q + 4, :], rows[:].bitcast(I32)[r0 : r0 + 4, :]
-            )
+        tab_sb.append(stream.tile([P, T], U32, name="tab2", offset=ODD * 2, align_bytes=64))
+        carries = [(a, r) for a in range(A) for r in (0, 2, 1, 3) if ROW0 + 16 * a + 4 * r != 32 * r]
+        for i, (a, r) in enumerate(carries):
+            r0 = ROW0 + 16 * a + 4 * r
+            nc.sync.dma_start(pass_planes[a].bitcast(I32)[32 * r : 32 * r + 4, :], rows[:].bitcast(I32)[r0 : r0 + 4, :])
             if i == 5:
-                load_table(2)
+                load_columns(2, 0, T // 2)
+        load_columns(2, T // 2, T)
         wf_sb = [order_wf(0, wf_raw0)]
 
         v_sb = []
@@ -185,12 +182,9 @@ def tile_list_street_shade_exposure_kernel(
         for t in range(PACK):
             for h in range(2):
                 h_banks[(t, h)] = bank(2 * t + h)
-        for h in range(2):
-            for t in range(PACK):
-                first_pass(h_banks[(t, h)], 0, t, 0, h)
-        for t in range(PACK):
-            for a in range(1, A):
-                for h in range(2):
+        for a in range(A):
+            for h in range(2):
+                for t in range(PACK):
                     first_pass(h_banks[(t, h)], 0, t, a, h)
 
         def small(name):
@@ -251,15 +245,23 @@ def tile_list_street_shade_exposure_kernel(
             n0 = b * N + n_tile * P
             return wt_sb[:, n0 : n0 + P], wts[:, n0 : n0 + P]
 
+        emptied = set()
+
+        def empty_half(b, t, h):
+            if (b, t) not in h_sb:
+                h_sb[(b, t)] = keep.tile([P, S], F32, name="h_sb%d_%d" % (b, t))
+            nc.scalar.copy(h_sb[(b, t)][:, h * BANK : (h + 1) * BANK], h_banks[(t, h)][:])
+            emptied.add((b, t, h))
+
         def empty(b, t):
             if b > 0:
                 for h in range(2):
                     h_banks[(t, h)] = bank(2 * t + h)
                     for a in range(A):
                         first_pass(h_banks[(t, h)], b, t, a, h)
-            h_sb[(b, t)] = keep.tile([P, S], F32, name="h_sb%d_%d" % (b, t))
             for h in range(2):
-                nc.scalar.copy(h_sb[(b, t)][:, h * BANK : (h + 1) * BANK], h_banks[(t, h)][:])
+                if (b, t, h) not in emptied:
+                    empty_half(b, t, h)
 
         def picked(b, t, which, cols):
             return h_sb[(b, t)][:].indirect(pos_sb[which][:, cols.start // 16 : cols.stop // 16])
@@ -366,6 +368,8 @@ def tile_list_street_shade_exposure_kernel(
                 rows_out = out[n_tiles.start * P : n_tiles.stop * P, cols]
                 nc.sync.dma_start(rows_out.rearrange("(j p) m -> p j m", p=P), result[:])
 
+        empty_half(0, 0, 0)
+        empty_half(0, 1, 0)
         for t in range(PACK):
             empty(0, t)
             gate(0, t, whole)

@@ -204,47 +204,19 @@ def tile_list_street_shade_exposure_kernel(
             signs[:], sign[:].rearrange("p (b t) -> p b t", b=B).unsqueeze(2).to_broadcast([P, B, SIGN_COLS, PACK])
         )
 
-        arena = ctx.enter_context(tc.tile_pool(name="arena", bufs=1))
-        KB = 1024
+        work = ctx.enter_context(tc.tile_pool(name="work", bufs=1))
         whole = slice(0, M)
-        first, last = slice(0, HALF), slice(HALF, M)
-        quarters = [slice(HALF, HALF + P), slice(HALF + P, M)]
+        first = slice(0, HALF)
+        third, fourth = slice(HALF, HALF + P), slice(HALF + P, M)
         h_sb = {}
-        z_codes = {}
-        wa_tiles = {}
-        gate_at = [0, 2 * KB, 5 * KB, 7 * KB]
-        zt0_at = 12 * KB
-        tower1_at = 18 * KB
         gates = {}
-        towers = [keep.tile([P, PACK, M], F32, name="tower0"), arena.tile([P, PACK, M], F32, name="tower1", offset=tower1_at, align_bytes=64)]
+        wa_tiles = {}
+        wa_rounded = {}
+        towers = {}
         canopies = {}
-        za1_at = 30 * KB
-        gate1_at = 32 * KB
-        canopy_at = {(1, quarters[0].start): tower1_at + 4 * KB, (1, quarters[1].start): za1_at}
-
-        def round_wa(engine, b, n0, n1, offset):
-            rounded = arena.tile([P, (n1 - n0) * PACK], BF16, name="wa_bf%d_%d" % (b, n0), offset=offset, align_bytes=64)
-            src = wa_raw[b][:, :, n0:n1]
-            if engine == "dve":
-                nc.vector.tensor_copy(interleaved(rounded[:]), by_slot(src))
-            else:
-                nc.scalar.copy(interleaved(rounded[:]), by_slot(src))
-            return (b, n0, n1, rounded)
-
-        def quantize_wa(piece, offset):
-            b, n0, n1, rounded = piece
-            codes = arena.tile([P, n1 - n0], U32, name="wa_codes%d_%d" % (b, n0), offset=offset, align_bytes=64)
-            scales = keep.tile([P, n1 - n0], U8, name="wa_scales%d_%d" % (b, n0), align_bytes=64)
-            nc.vector.quantize_mx(out=codes[:].bitcast(FP8X4), scales=scales[:], in_=rounded[:])
-            for n in range(n0, n1, P):
-                wa_tiles[(b, n // P)] = (codes[:, n - n0 : n - n0 + P], scales[:, n - n0 : n - n0 + P])
-
-        def weights(name, b, n_tile):
-            if name == "za":
-                return wa_tiles[(b, n_tile)]
-            n0 = b * N + n_tile * P
-            return wt_sb[:, n0 : n0 + P], wts[:, n0 : n0 + P]
-
+        rounded_maps = {}
+        z_codes = {}
+        y_banks = {}
         emptied = set()
 
         def empty_half(b, t, h):
@@ -267,70 +239,71 @@ def tile_list_street_shade_exposure_kernel(
             return h_sb[(b, t)][:].indirect(pos_sb[which][:, cols.start // 16 : cols.stop // 16])
 
         def gate(b, t, cols):
-            shape = [P, cols.stop - cols.start]
-            key = (b, t, cols.start)
-            if b == 0:
-                gates[key] = arena.tile(shape, F32, name="gate0_%d" % t, offset=gate_at[t], align_bytes=64)
-            elif cols == first:
-                gates[key] = arena.tile(shape, F32, name="gate1_%d" % t, offset=gate1_at + t * KB, align_bytes=64)
-            else:
-                gates[key] = keep.tile(shape, F32, name="gate1_last%d" % t)
-            nc.scalar.activation(gates[key][:], picked(b, t, 0, cols), ACT.Sigmoid)
+            tile = work.tile([P, cols.stop - cols.start], F32, name="gate%d_%d_%d" % (b, t, cols.start))
+            gates[(b, t, cols.start)] = tile
+            nc.scalar.activation(tile[:], picked(b, t, 0, cols), ACT.Sigmoid)
 
         def tower(b, t):
+            if b not in towers:
+                towers[b] = work.tile([P, PACK, M], F32, name="tower%d" % b, tag="tower")
             nc.vector.tensor_tensor(towers[b][:, t, :], picked(b, t, 2, whole), roots[:, PACK * b + t, :], MULT)
 
         def canopy(b, t, cols):
             key = (b, cols.start)
             if key not in canopies:
-                shape = [P, PACK, cols.stop - cols.start]
-                if key in canopy_at:
-                    canopies[key] = arena.tile(shape, F32, name="canopy%d_%d" % key, offset=canopy_at[key], align_bytes=64)
-                else:
-                    canopies[key] = keep.tile(shape, F32, name="canopy%d_%d" % key)
-            g0 = cols.start // HALF * HALF if b > 0 else 0
-            gated = gates[(b, t, g0)][:, cols.start - g0 : cols.stop - g0]
-            nc.vector.tensor_tensor(canopies[key][:, t, :], picked(b, t, 1, cols), gated, MULT)
+                canopies[key] = work.tile([P, PACK, cols.stop - cols.start], F32, name="canopy%d_%d" % key)
+            nc.vector.tensor_tensor(canopies[key][:, t, :], picked(b, t, 1, cols), gates[(b, t, cols.start)][:], MULT)
 
         def square(b):
-            squared = arena.tile([P, M * PACK], BF16, name="zt_bf%d" % b, offset=zt0_at, align_bytes=64)
+            squared = work.tile([P, M * PACK], BF16, name="zt_bf%d" % b, align_bytes=64)
             nc.scalar.activation(interleaved(squared[:]), by_slot(towers[b][:]), ACT.Square)
-            return squared
+            rounded_maps[("zt", b, 0)] = squared
 
-        def apply_sign(b, squared):
-            runs = squared[:].rearrange("p (r x) -> p r x", x=SIGN_COLS * PACK)
+        def apply_sign(b):
+            runs = rounded_maps[("zt", b, 0)][:].rearrange("p (r x) -> p r x", x=SIGN_COLS * PACK)
             pattern = signs[:, b, :, :].rearrange("p m t -> p (m t)").unsqueeze(1).to_broadcast([P, M // SIGN_COLS, SIGN_COLS * PACK])
             nc.vector.tensor_tensor(runs, runs, pattern, MULT)
-            return squared
 
-        def apply_gain(name, b, cols):
-            src, gain = (towers[b], gt_sb) if name == "zt" else (canopies[(b, cols.start)], ga_sb)
+        def apply_gain(b, cols):
             width = cols.stop - cols.start
-            if (name, b) == ("zt", 0):
-                rounded = arena.tile([P, width * PACK], BF16, name="zt0_bf", offset=zt0_at, align_bytes=64)
-            elif (name, b, cols.start) == ("za", 1, 0):
-                rounded = arena.tile([P, width * PACK], BF16, name="za1_bf", offset=za1_at, align_bytes=64)
-            else:
-                rounded = ring.tile([P, width * PACK], BF16, name="z_bf", bufs=2, align_bytes=64)
+            rounded = work.tile([P, width * PACK], BF16, name="za_bf%d_%d" % (b, cols.start), align_bytes=64)
             nc.vector.tensor_tensor(
                 interleaved(rounded[:]),
-                by_slot(src[:]),
-                gain[:, b, :].unsqueeze(1).unsqueeze(3).to_broadcast([P, width // 4, PACK, 4]),
+                by_slot(canopies[(b, cols.start)][:]),
+                ga_sb[:, b, :].unsqueeze(1).unsqueeze(3).to_broadcast([P, width // 4, PACK, 4]),
                 MULT,
             )
-            return rounded
+            rounded_maps[("za", b, cols.start)] = rounded
 
-        def quantize_map(name, b, cols, rounded):
-            codes, scales = z_codes[(name, b)]
-            nc.vector.quantize_mx(out=codes[:, cols].bitcast(FP8X4), scales=scales[:, cols], in_=rounded[:])
-
-        for name in ("za", "zt"):
-            for b in range(B):
+        def quantize_map(name, b, cols):
+            if (name, b) not in z_codes:
                 codes = keep.tile([P, M], U32, name="%s_codes%d" % (name, b), align_bytes=64)
                 scales = keep.tile([P, M], U8, name="%s_scales%d" % (name, b), align_bytes=64)
                 z_codes[(name, b)] = (codes, scales)
+            codes, scales = z_codes[(name, b)]
+            nc.vector.quantize_mx(out=codes[:, cols].bitcast(FP8X4), scales=scales[:, cols], in_=rounded_maps[(name, b, cols.start)][:])
 
-        y_banks = {}
+        def round_wa(on_vector, b, j):
+            rounded = ring.tile([P, WA_CHUNK * PACK], BF16, name="wa_bf", bufs=4, align_bytes=64)
+            src = wa_raw[b][:, :, j * WA_CHUNK : (j + 1) * WA_CHUNK]
+            if on_vector:
+                nc.vector.tensor_copy(interleaved(rounded[:]), by_slot(src))
+            else:
+                nc.scalar.copy(interleaved(rounded[:]), by_slot(src))
+            wa_rounded[(b, j)] = rounded
+
+        def quantize_wa(b, j):
+            codes = keep.tile([P, WA_CHUNK], U32, name="wa_codes%d_%d" % (b, j), align_bytes=64)
+            scales = keep.tile([P, WA_CHUNK], U8, name="wa_scales%d_%d" % (b, j), align_bytes=64)
+            nc.vector.quantize_mx(out=codes[:].bitcast(FP8X4), scales=scales[:], in_=wa_rounded[(b, j)][:])
+            for i in range(WA_CHUNK // P):
+                wa_tiles[(b, j * (WA_CHUNK // P) + i)] = (codes[:, i * P : (i + 1) * P], scales[:, i * P : (i + 1) * P])
+
+        def weights(name, b, n_tile):
+            if name == "za":
+                return wa_tiles[(b, n_tile)]
+            n0 = b * N + n_tile * P
+            return wt_sb[:, n0 : n0 + P], wts[:, n0 : n0 + P]
 
         def groups(cols):
             width = cols.stop - cols.start
@@ -338,15 +311,15 @@ def tile_list_street_shade_exposure_kernel(
             first_bank = 0 if cols.start < HALF else 3 + 2 * ((cols.start - HALF) // width)
             return [(first_bank + g, range(g * per_bank, (g + 1) * per_bank)) for g in range(N_TILES // per_bank)]
 
-        def second_passes(name, b, cols, start, stop, only=range(N_TILES)):
+        def second_passes(name, b, cols, start, stop, only=None):
             codes, scales = z_codes[(name, b)]
             width = cols.stop - cols.start
-            for bank_no, n_tiles in groups(cols):
+            for g, (bank_no, n_tiles) in enumerate(groups(cols)):
+                if only is not None and g not in only:
+                    continue
                 if start:
                     y_banks[bank_no] = bank(bank_no)
                 for j, n_tile in enumerate(n_tiles):
-                    if n_tile not in only:
-                        continue
                     w_codes, w_scales = weights(name, b, n_tile)
                     nc.tensor.matmul_mx(
                         out=y_banks[bank_no][:, j * width : (j + 1) * width],
@@ -358,9 +331,11 @@ def tile_list_street_shade_exposure_kernel(
                         stop=(stop and j == len(n_tiles) - 1),
                     )
 
-        def finish(cols):
+        def finish(cols, only=None):
             width = cols.stop - cols.start
-            for bank_no, n_tiles in groups(cols):
+            for g, (bank_no, n_tiles) in enumerate(groups(cols)):
+                if only is not None and g not in only:
+                    continue
                 result = keep.tile([P, len(n_tiles), width], F32, name="result%d" % bank_no)
                 nc.scalar.activation(
                     result[:].rearrange("p j m -> p (j m)"), y_banks[bank_no][:, 0 : len(n_tiles) * width], ACT.Sigmoid
@@ -368,63 +343,75 @@ def tile_list_street_shade_exposure_kernel(
                 rows_out = out[n_tiles.start * P : n_tiles.stop * P, cols]
                 nc.sync.dma_start(rows_out.rearrange("(j p) m -> p j m", p=P), result[:])
 
+        pieces = [first, third, fourth]
         empty_half(0, 0, 0)
         empty_half(0, 1, 0)
-        for t in range(PACK):
+        for t in range(2):
             empty(0, t)
             gate(0, t, whole)
             tower(0, t)
             canopy(0, t, whole)
-            if t == 2:
-                p1 = round_wa("dve", 0, 0, 256, gate_at[2])
+        for t in range(2, PACK):
+            empty(0, t)
+            tower(0, t)
+        for t in range(2, PACK):
+            gate(0, t, whole)
+            canopy(0, t, whole)
+        square(0)
         empty(1, 0)
-        sq0 = square(0)
-        quantize_wa(p1, gate_at[3])
-        za0 = apply_gain("za", 0, whole)
-        zt0 = apply_sign(0, sq0)
-        quantize_map("za", 0, whole, za0)
-        quantize_map("zt", 0, whole, zt0)
+        apply_gain(0, whole)
+        empty(1, 1)
+        apply_sign(0)
+        round_wa(False, 0, 0)
+        quantize_map("za", 0, whole)
+        quantize_map("zt", 0, whole)
         for t in range(PACK):
-            if t > 0:
+            if t > 1:
                 empty(1, t)
             tower(1, t)
-        for cols in [first] + quarters:
+        quantize_wa(0, 0)
+        for cols in pieces:
             second_passes("zt", 0, cols, True, False)
         for t in range(PACK):
             gate(1, t, first)
             canopy(1, t, first)
-        p2 = round_wa("act", 0, 256, 768, 26 * KB)
-        sq1 = square(1)
-        for t in range(PACK):
-            gate(1, t, last)
-        p3 = round_wa("act", 1, 0, 512, 3 * KB)
-        p4 = round_wa("dve", 1, 512, 768, gate1_at)
-        quantize_wa(p2, 0)
-        for cols in [first] + quarters:
+        round_wa(False, 0, 1)
+        square(1)
+        round_wa(False, 0, 2)
+        round_wa(False, 1, 0)
+        round_wa(False, 1, 1)
+        quantize_wa(0, 1)
+        apply_gain(1, first)
+        apply_sign(1)
+        quantize_map("za", 1, first)
+        quantize_map("zt", 1, whole)
+        quantize_wa(0, 2)
+        for cols in pieces:
             second_passes("za", 0, cols, False, False)
-        za1 = apply_gain("za", 1, first)
-        quantize_wa(p4, 37 * KB)
-        zt1 = apply_sign(1, sq1)
-        quantize_map("za", 1, first, za1)
-        quantize_map("zt", 1, whole, zt1)
-        quantize_wa(p3, 38 * KB)
-        second_passes("zt", 1, first, False, False)
-        second_passes("za", 1, first, False, True)
-        finish(first)
-        for cols in quarters:
+        for cols in pieces:
             second_passes("zt", 1, cols, False, False)
-        third, fourth = quarters
+        for t in range(PACK):
+            gate(1, t, third)
+        round_wa(False, 1, 2)
+        for t in range(PACK):
+            gate(1, t, fourth)
+        quantize_wa(1, 0)
+        quantize_wa(1, 1)
+        second_passes("za", 1, first, False, True, only=(0, 1))
+        finish(first, only=(0, 1))
         for t in range(PACK):
             canopy(1, t, third)
+        quantize_wa(1, 2)
+        second_passes("za", 1, first, False, True, only=(2,))
+        finish(first, only=(2,))
+        apply_gain(1, third)
         canopy(1, 0, fourth)
-        za1 = apply_gain("za", 1, third)
-        canopy(1, 1, fourth)
-        quantize_map("za", 1, third, za1)
+        quantize_map("za", 1, third)
         second_passes("za", 1, third, False, True)
         finish(third)
-        for t in range(2, PACK):
+        for t in range(1, PACK):
             canopy(1, t, fourth)
-        za1 = apply_gain("za", 1, fourth)
-        quantize_map("za", 1, fourth, za1)
+        apply_gain(1, fourth)
+        quantize_map("za", 1, fourth)
         second_passes("za", 1, fourth, False, True)
         finish(fourth)

@@ -205,6 +205,7 @@ def tile_list_street_shade_exposure_kernel(
         )
 
         work = ctx.enter_context(tc.tile_pool(name="work", bufs=1))
+        shared = ctx.enter_context(tc.tile_pool(name="shared", bufs=1))
         whole = slice(0, M)
         first = slice(0, HALF)
         third, fourth = slice(HALF, HALF + P), slice(HALF + P, M)
@@ -239,13 +240,16 @@ def tile_list_street_shade_exposure_kernel(
             return h_sb[(b, t)][:].indirect(pos_sb[which][:, cols.start // 16 : cols.stop // 16])
 
         def gate(b, t, cols):
-            tile = work.tile([P, cols.stop - cols.start], F32, name="gate%d_%d_%d" % (b, t, cols.start))
+            if (b, t, cols) == (1, 2, fourth):
+                tile = shared.tile([P, P], F32, name="gate_late", offset=0, align_bytes=64)
+            else:
+                tile = work.tile([P, cols.stop - cols.start], F32, name="gate%d_%d_%d" % (b, t, cols.start))
             gates[(b, t, cols.start)] = tile
             nc.scalar.activation(tile[:], picked(b, t, 0, cols), ACT.Sigmoid)
 
         def tower(b, t):
             if b not in towers:
-                towers[b] = work.tile([P, PACK, M], F32, name="tower%d" % b, tag="tower")
+                towers[b] = work.tile([P, PACK, M], F32, name="tower%d" % b)
             nc.vector.tensor_tensor(towers[b][:, t, :], picked(b, t, 2, whole), roots[:, PACK * b + t, :], MULT)
 
         def canopy(b, t, cols):
@@ -264,24 +268,39 @@ def tile_list_street_shade_exposure_kernel(
             pattern = signs[:, b, :, :].rearrange("p m t -> p (m t)").unsqueeze(1).to_broadcast([P, M // SIGN_COLS, SIGN_COLS * PACK])
             nc.vector.tensor_tensor(runs, runs, pattern, MULT)
 
-        def apply_gain(b, cols):
+        def apply_gain(b, cols, piece=None):
+            piece = piece or cols
             width = cols.stop - cols.start
             rounded = work.tile([P, width * PACK], BF16, name="za_bf%d_%d" % (b, cols.start), align_bytes=64)
             nc.vector.tensor_tensor(
                 interleaved(rounded[:]),
-                by_slot(canopies[(b, cols.start)][:]),
+                by_slot(canopies[(b, piece.start)][:, :, cols.start - piece.start : cols.stop - piece.start]),
                 ga_sb[:, b, :].unsqueeze(1).unsqueeze(3).to_broadcast([P, width // 4, PACK, 4]),
                 MULT,
             )
             rounded_maps[("za", b, cols.start)] = rounded
 
-        def quantize_map(name, b, cols):
-            if (name, b) not in z_codes:
-                codes = keep.tile([P, M], U32, name="%s_codes%d" % (name, b), align_bytes=64)
-                scales = keep.tile([P, M], U8, name="%s_scales%d" % (name, b), align_bytes=64)
-                z_codes[(name, b)] = (codes, scales)
-            codes, scales = z_codes[(name, b)]
-            nc.vector.quantize_mx(out=codes[:, cols].bitcast(FP8X4), scales=scales[:, cols], in_=rounded_maps[(name, b, cols.start)][:])
+        def holding(table, name, b, cols):
+            start = max(s for (n, bb, s) in table if (n, bb) == (name, b) and s <= cols.start)
+            return table[(name, b, start)], slice(cols.start - start, cols.stop - start)
+
+        def quantize_map(name, b, cols, piece=None, late=False):
+            piece = piece or cols
+            width = piece.stop - piece.start
+            key = (name, b, piece.start)
+            if key not in z_codes:
+                if late:
+                    codes = shared.tile([P, width], U32, name="codes_late", offset=0, align_bytes=64)
+                else:
+                    codes = keep.tile([P, width], U32, name="%s_codes%d_%d" % key, align_bytes=64)
+                z_codes[key] = (codes, keep.tile([P, width], U8, name="%s_scales%d_%d" % key, align_bytes=64))
+            (codes, scales), local = holding(z_codes, name, b, cols)
+            rounded, source = holding(rounded_maps, name, b, cols)
+            nc.vector.quantize_mx(
+                out=codes[:, local].bitcast(FP8X4),
+                scales=scales[:, local],
+                in_=rounded[:, PACK * source.start : PACK * source.stop],
+            )
 
         def round_wa(on_vector, b, j):
             rounded = ring.tile([P, WA_CHUNK * PACK], BF16, name="wa_bf", bufs=4, align_bytes=64)
@@ -312,7 +331,7 @@ def tile_list_street_shade_exposure_kernel(
             return [(first_bank + g, range(g * per_bank, (g + 1) * per_bank)) for g in range(N_TILES // per_bank)]
 
         def second_passes(name, b, cols, start, stop, only=None):
-            codes, scales = z_codes[(name, b)]
+            (codes, scales), local = holding(z_codes, name, b, cols)
             width = cols.stop - cols.start
             for g, (bank_no, n_tiles) in enumerate(groups(cols)):
                 if only is not None and g not in only:
@@ -325,8 +344,8 @@ def tile_list_street_shade_exposure_kernel(
                         out=y_banks[bank_no][:, j * width : (j + 1) * width],
                         lhsT=w_codes.bitcast(FP8X4),
                         lhsT_scale=w_scales,
-                        rhs=codes[:, cols].bitcast(FP8X4),
-                        rhs_scale=scales[:, cols],
+                        rhs=codes[:, local].bitcast(FP8X4),
+                        rhs_scale=scales[:, local],
                         start=(start and j == 0),
                         stop=(stop and j == len(n_tiles) - 1),
                     )
@@ -353,21 +372,23 @@ def tile_list_street_shade_exposure_kernel(
             canopy(0, t, whole)
         for t in range(2, PACK):
             empty(0, t)
-            tower(0, t)
-        for t in range(2, PACK):
             gate(0, t, whole)
-            canopy(0, t, whole)
-        square(0)
+        tower(0, 2)
+        canopy(0, 2, whole)
+        canopy(0, 3, whole)
+        tower(0, 3)
         empty(1, 0)
-        apply_gain(0, whole)
-        empty(1, 1)
-        apply_sign(0)
         round_wa(False, 0, 0)
+        square(0)
+        apply_gain(0, whole)
+        tower(1, 0)
         quantize_map("za", 0, whole)
+        apply_sign(0)
+        empty(1, 1)
+        tower(1, 1)
         quantize_map("zt", 0, whole)
-        for t in range(PACK):
-            if t > 1:
-                empty(1, t)
+        for t in range(2, PACK):
+            empty(1, t)
             tower(1, t)
         quantize_wa(0, 0)
         for cols in pieces:
@@ -384,11 +405,12 @@ def tile_list_street_shade_exposure_kernel(
         apply_gain(1, first)
         apply_sign(1)
         quantize_map("za", 1, first)
-        quantize_map("zt", 1, whole)
+        quantize_map("zt", 1, first)
+        quantize_map("zt", 1, third)
         quantize_wa(0, 2)
         for cols in pieces:
             second_passes("za", 0, cols, False, False)
-        for cols in pieces:
+        for cols in (first, third):
             second_passes("zt", 1, cols, False, False)
         for t in range(PACK):
             gate(1, t, third)
@@ -411,7 +433,12 @@ def tile_list_street_shade_exposure_kernel(
         finish(third)
         for t in range(1, PACK):
             canopy(1, t, fourth)
-        apply_gain(1, fourth)
-        quantize_map("za", 1, fourth)
+        quantize_map("zt", 1, fourth, late=True)
+        second_passes("zt", 1, fourth, False, False)
+        eighths = [slice(fourth.start, fourth.start + P // 2), slice(fourth.start + P // 2, M)]
+        for cols in eighths:
+            apply_gain(1, cols, fourth)
+        for cols in eighths:
+            quantize_map("za", 1, cols, fourth)
         second_passes("za", 1, fourth, False, True)
         finish(fourth)

@@ -108,12 +108,9 @@ def tile_list_street_shade_exposure_kernel(
         nc.vector.memset(planes[:].bitcast(I32), 0)
         rows = keep.tile([P, S + H], U8, name="rows", align_bytes=64)
         pass_planes = [planes[:, 0 : S + H], rows[:], planes[:, S + H : 2 * (S + H)]]
-        gains = []
-        for name, g in (("gt_sb", gt), ("ga_sb", ga)):
-            g_sb = keep.tile([P, B, PACK], F32, name=name)
-            nc.gpsimd.dma_start(g_sb[:], g.rearrange("(b p t) -> p b t", b=B, t=PACK))
-            gains.append(g_sb)
-        gt_sb, ga_sb = gains
+        gt_pad = keep.tile([P, B, 2 * PACK], F32, name="gt_pad")
+        gt_sb = gt_pad[:, :, 0:PACK]
+        nc.gpsimd.dma_start(gt_sb, gt.rearrange("(b p t) -> p b t", b=B, t=PACK))
         nc.scalar.activation(warm_out[:], warm[:], ACT.Sigmoid)
 
         vs_rows = stream.tile([P, S], U8, name="vs_rows", offset=2 * ODD, align_bytes=64)
@@ -144,6 +141,9 @@ def tile_list_street_shade_exposure_kernel(
         wf_raw1 = load_wf(1, stream.tile([P, A * K_PASS * 2], U8, name="wf_raw1", offset=0, align_bytes=64))
         wf_sb.append(order_wf(1, wf_raw1))
 
+        ga_pad = stream.tile([P, B, 2 * PACK], F32, name="ga_pad", offset=2 * ODD + 4 * B * N, align_bytes=64)
+        ga_sb = ga_pad[:, :, 0:PACK]
+        nc.sync.dma_start(ga_sb, ga.rearrange("(b p t) -> p b t", b=B, t=PACK))
         wa_raw = []
         for b in range(B):
             raw = stream.tile([P, PACK, N], F32, name="wa_raw%d" % b, offset=(A * K_PASS * 2, ODD)[b], align_bytes=64)
@@ -154,8 +154,8 @@ def tile_list_street_shade_exposure_kernel(
             wt_sb[:].bitcast(I32).rearrange("p (b n) -> p b n", b=B),
             wt_words.rearrange("b p n i -> p b (n i)").bitcast(I32),
         )
-        wts = stream.tile([P, B * N], U8, name="wts", offset=2 * ODD + 4 * B * N, align_bytes=64)
-        nc.gpsimd.memset(wts[:].bitcast(I32), 0)
+        wts = stream.tile([P, B * N], U8, name="wts", offset=ODD + 4 * PACK * N, align_bytes=64)
+        nc.vector.memset(wts[:].bitcast(I32), 0)
         for q in range(QUADS):
             nc.sync.dma_start(
                 wts[:].bitcast(I32)[32 * q : 32 * q + 4, :].rearrange("r (b x) -> r b x", b=B),
@@ -190,10 +190,9 @@ def tile_list_street_shade_exposure_kernel(
         def small(name):
             return keep.tile([P, B * PACK], F32, name=name)
 
-        gt_flat = gt_sb[:].rearrange("p b t -> p (b t)")
         size, sign = small("size"), small("sign")
-        nc.scalar.activation(size[:], gt_flat, ACT.Abs)
-        nc.scalar.activation(sign[:], gt_flat, ACT.Sign)
+        nc.scalar.activation(size[:].rearrange("p (b t) -> p b t", b=B), gt_sb, ACT.Abs)
+        nc.scalar.activation(sign[:].rearrange("p (b t) -> p b t", b=B), gt_sb, ACT.Sign)
         half, root = small("half"), small("root")
         nc.gpsimd.memset(half[:], 0.5)
         nc.gpsimd.tensor_tensor(root[:], size[:], half[:], POW)
@@ -242,6 +241,8 @@ def tile_list_street_shade_exposure_kernel(
         def gate(b, t, cols):
             if (b, t, cols) == (1, 2, fourth):
                 tile = shared.tile([P, P], F32, name="gate_late", offset=0, align_bytes=64)
+            elif (b, t) == (0, 2):
+                tile = shared.tile([P, M], F32, name="gate_early", offset=1024, align_bytes=64)
             else:
                 tile = work.tile([P, cols.stop - cols.start], F32, name="gate%d_%d_%d" % (b, t, cols.start))
             gates[(b, t, cols.start)] = tile
@@ -303,7 +304,10 @@ def tile_list_street_shade_exposure_kernel(
             )
 
         def round_wa(on_vector, b, j):
-            rounded = ring.tile([P, WA_CHUNK * PACK], BF16, name="wa_bf", bufs=4, align_bytes=64)
+            if on_vector:
+                rounded = shared.tile([P, WA_CHUNK * PACK], BF16, name="wa_bf_vector", offset=1024, align_bytes=64)
+            else:
+                rounded = ring.tile([P, WA_CHUNK * PACK], BF16, name="wa_bf", bufs=4, align_bytes=64)
             src = wa_raw[b][:, :, j * WA_CHUNK : (j + 1) * WA_CHUNK]
             if on_vector:
                 nc.vector.tensor_copy(interleaved(rounded[:]), by_slot(src))
@@ -372,21 +376,20 @@ def tile_list_street_shade_exposure_kernel(
             canopy(0, t, whole)
         for t in range(2, PACK):
             empty(0, t)
+            tower(0, t)
+        for t in range(2, PACK):
             gate(0, t, whole)
-        tower(0, 2)
-        canopy(0, 2, whole)
-        canopy(0, 3, whole)
-        tower(0, 3)
-        empty(1, 0)
-        round_wa(False, 0, 0)
+            canopy(0, t, whole)
         square(0)
+        round_wa(True, 0, 0)
         apply_gain(0, whole)
-        tower(1, 0)
-        quantize_map("za", 0, whole)
+        empty(1, 0)
         apply_sign(0)
         empty(1, 1)
-        tower(1, 1)
+        quantize_map("za", 0, whole)
         quantize_map("zt", 0, whole)
+        tower(1, 0)
+        tower(1, 1)
         for t in range(2, PACK):
             empty(1, t)
             tower(1, t)

@@ -400,19 +400,19 @@ def tile_list_street_shade_exposure_kernel(
             gate(1, t, first)
             canopy(1, t, first)
         round_wa(False, 0, 1)
-        square(1)
         round_wa(False, 0, 2)
+        square(1)
         round_wa(False, 1, 0)
         round_wa(False, 1, 1)
         quantize_wa(0, 1)
+        quantize_wa(0, 2)
+        for cols in pieces:
+            second_passes("za", 0, cols, False, False)
         apply_gain(1, first)
         apply_sign(1)
         quantize_map("za", 1, first)
         quantize_map("zt", 1, first)
         quantize_map("zt", 1, third)
-        quantize_wa(0, 2)
-        for cols in pieces:
-            second_passes("za", 0, cols, False, False)
         for cols in (first, third):
             second_passes("zt", 1, cols, False, False)
         for t in range(PACK):

@@ -35,12 +35,12 @@ ROW0 = 40
 SIGN_COLS = 16
 
 
-def interleaved(tile_ap):
-    return tile_ap.rearrange("p (c i t) -> p c t i", i=4, t=PACK)
+def interleaved(tile_ap, run=4):
+    return tile_ap.rearrange("p (c i t) -> p c t i", i=run, t=PACK)
 
 
-def by_slot(tile_ap):
-    return tile_ap.rearrange("p t (c i) -> p c t i", i=4)
+def by_slot(tile_ap, run=4):
+    return tile_ap.rearrange("p t (c i) -> p c t i", i=run)
 
 
 def tile_list_street_shade_exposure_kernel(
@@ -261,7 +261,7 @@ def tile_list_street_shade_exposure_kernel(
 
         def square(b):
             squared = work.tile([P, M * PACK], BF16, name="zt_bf%d" % b, align_bytes=64)
-            nc.scalar.activation(interleaved(squared[:]), by_slot(towers[b][:]), ACT.Square)
+            nc.scalar.activation(interleaved(squared[:], 2), by_slot(towers[b][:], 2), ACT.Square)
             rounded_maps[("zt", b, 0)] = squared
 
         def apply_sign(b):
@@ -312,7 +312,7 @@ def tile_list_street_shade_exposure_kernel(
             if on_vector:
                 nc.vector.tensor_copy(interleaved(rounded[:]), by_slot(src))
             else:
-                nc.scalar.copy(interleaved(rounded[:]), by_slot(src))
+                nc.scalar.copy(interleaved(rounded[:], 2), by_slot(src, 2))
             wa_rounded[(b, j)] = rounded
 
         def quantize_wa(b, j):
@@ -330,7 +330,7 @@ def tile_list_street_shade_exposure_kernel(
 
         def groups(cols):
             width = cols.stop - cols.start
-            per_bank = 2 if width == HALF else 3
+            per_bank = 3 if cols == third else 2
             first_bank = 0 if cols.start < HALF else 3 + 2 * ((cols.start - HALF) // width)
             return [(first_bank + g, range(g * per_bank, (g + 1) * per_bank)) for g in range(N_TILES // per_bank)]
 

@@ -183,9 +183,10 @@ def tile_list_street_shade_exposure_kernel(
             for h in range(2):
                 h_banks[(t, h)] = bank(2 * t + h)
         for a in range(A):
-            for h in range(2):
-                for t in range(PACK):
-                    first_pass(h_banks[(t, h)], 0, t, a, h)
+            for pair in range(2):
+                for h in range(2):
+                    for t in (2 * pair, 2 * pair + 1):
+                        first_pass(h_banks[(t, h)], 0, t, a, h)
 
         def small(name):
             return keep.tile([P, B * PACK], F32, name=name)

@@ -15,10 +15,6 @@ FP8X4 = mybir.dt.float8_e4m3fn_x4
 FP4X4 = mybir.dt.float4_e2m1fn_x4
 ACT = mybir.ActivationFunctionType
 MULT = mybir.AluOpType.mult
-ADD = mybir.AluOpType.add
-SUB = mybir.AluOpType.subtract
-MAX = mybir.AluOpType.max
-POW = mybir.AluOpType.pow
 
 P = 128
 PACK = 4
@@ -27,20 +23,23 @@ A = K // K_PASS
 B = H // K_PASS
 BANK = 512
 QUADS = 4
+ROWS = 16
 N_TILES = N // P
 WA_CHUNK = 256
-HALF = M // 2
-ODD = 4 * T
-ROW0 = 40
-SIGN_COLS = 16
+TAB_BYTES = 4 * T
+WA_BYTES = 4 * PACK * WA_CHUNK
+PLANE = S + H
+ROW0 = (0, 56, 72)
+TAB0_CUT = 3 * T // 8
+TAB2_CUT = 3 * T // 4
 
 
-def interleaved(tile_ap, run=4):
-    return tile_ap.rearrange("p (c i t) -> p c t i", i=run, t=PACK)
+def woven(tile_ap):
+    return tile_ap.rearrange("p (c i t) -> p c t i", i=4, t=PACK)
 
 
-def by_slot(tile_ap, run=4):
-    return tile_ap.rearrange("p t (c i) -> p c t i", i=run)
+def by_slot(tile_ap):
+    return tile_ap.rearrange("p t (c i) -> p c t i", i=4)
 
 
 def tile_list_street_shade_exposure_kernel(
@@ -50,11 +49,11 @@ def tile_list_street_shade_exposure_kernel(
     with ExitStack() as ctx:
         keep = ctx.enter_context(tc.tile_pool(name="keep", bufs=1))
         stream = ctx.enter_context(tc.tile_pool(name="stream", bufs=1))
-        ring = ctx.enter_context(tc.tile_pool(name="ring", bufs=2))
+        ring = ctx.enter_context(tc.tile_pool(name="ring", bufs=3))
         psum = ctx.enter_context(tc.psum_pool(name="psum", bufs=1))
 
         wfs_raw = keep.tile([P, H], U8, name="wfs_raw", align_bytes=64)
-        nc.vector.memset(wfs_raw[:].bitcast(I32), 0)
+        nc.gpsimd.memset(wfs_raw[:].bitcast(I32), 0)
         ts_rows = keep.tile([P, T], U8, name="ts_rows", align_bytes=64)
         nc.vector.memset(ts_rows[:].bitcast(I32), 0)
         warm = keep.tile([P, 1], F32, name="warm")
@@ -63,74 +62,82 @@ def tile_list_street_shade_exposure_kernel(
 
         def load_rows(queue, rows_sb, rows_hbm):
             rows_i32 = rows_hbm.rearrange("a q t -> (a q) t").bitcast(I32)
-            queue.dma_start(rows_sb[:].bitcast(I32)[ROW0 : ROW0 + 16 * A, :], rows_i32)
+            queue.dma_start(rows_sb[:].bitcast(I32)[ROW0[0] : ROW0[0] + ROWS, :], rows_i32[0:ROWS, :])
+            queue.dma_start(rows_sb[:].bitcast(I32)[ROW0[1] : ROW0[1] + 2 * ROWS, :], rows_i32[ROWS : 3 * ROWS, :])
 
-        nc.scalar.dma_start(wfs_raw[:].bitcast(I32)[ROW0 : ROW0 + 16 * A, :], wf_scales.rearrange("a q t -> (a q) t").bitcast(I32))
+        load_rows(nc.scalar, wfs_raw, wf_scales)
+        nc.scalar.activation(warm_out[:], warm[:], ACT.Sigmoid)
 
-        offs_sb = keep.tile([P, S // 16], U16, name="offs_sb")
+        gains = []
+        for name, gain in (("ga_sb", ga), ("gt_sb", gt)):
+            padded = keep.tile([P, B, 2 * PACK], F32, name=name)
+            nc.gpsimd.dma_start(padded[:, :, 0:PACK], gain.rearrange("(b p t) -> p b t", b=B, t=PACK))
+            gains.append(padded)
+        ga_sb, gt_sb = gains
+
+        tab_sb = []
+
+        def load_table(a, t0, t1):
+            if len(tab_sb) == a:
+                tab_sb.append(stream.tile([P, T], U32, name="tab%d" % a, offset=TAB_BYTES * a, align_bytes=64))
+            words = tab_words[a].rearrange("p t i -> p (t i)").bitcast(I32)
+            nc.sync.dma_start(tab_sb[a][:].bitcast(I32)[:, t0:t1], words[:, t0:t1])
+
         wf_hbm = wf_words.bitcast(I32).rearrange("a p (b x) -> b p a x", b=B)
 
         def load_wf(b, raw):
             nc.sync.dma_start(raw[:].bitcast(I32).rearrange("p (a x) -> p a x", a=A), wf_hbm[b])
             return raw
 
-        tab_sb = [stream.tile([P, T], U32, name="tab0", offset=0, align_bytes=64)]
-
-        def load_columns(a, t0, t1):
-            words = tab_words[a].rearrange("p t i -> p (t i)").bitcast(I32)
-            nc.sync.dma_start(tab_sb[a][:].bitcast(I32)[:, t0:t1], words[:, t0:t1])
-
-        load_columns(0, 0, T // 2)
-        nc.sync.dma_start(offs_sb[:], offs)
-        pos_sb = []
-        for i, pos in enumerate((pos1, pos2, pos3)):
-            lst = keep.tile([P, M // 16], U16, name="pos%d" % i)
-            nc.sync.dma_start(lst[:], pos)
-            pos_sb.append(lst)
-        load_rows(nc.sync, ts_rows, tab_scales)
-        def order_wf(b, raw):
+        def order_wf(b, raw, copy):
             ordered = keep.tile([P, A * K_PASS * 2], U8, name="wf_sb%d" % b, align_bytes=64)
-            nc.vector.tensor_copy(
+            copy(
                 ordered[:].bitcast(U16).rearrange("p (a t m) -> p t a m", t=PACK, m=P),
                 raw[:].bitcast(U16).rearrange("p (a m t) -> p t a m", t=PACK, m=P),
             )
             return ordered
 
-        def load_table(a):
-            tab_sb.append(stream.tile([P, T], U32, name="tab%d" % a, offset=ODD * a, align_bytes=64))
-            load_columns(a, 0, T)
+        load_table(0, 0, TAB0_CUT)
+        offs_sb = keep.tile([P, S // 16], U16, name="offs_sb")
+        nc.sync.dma_start(offs_sb[:], offs)
+        load_rows(nc.sync, ts_rows, tab_scales)
+        load_table(0, TAB0_CUT, T)
+        pos_sb = []
+        for i, pos in enumerate((pos1, pos2, pos3)):
+            lst = keep.tile([P, M // 16], U16, name="pos%d" % i)
+            nc.sync.dma_start(lst[:], pos)
+            pos_sb.append(lst)
+        wf_raw0 = load_wf(0, stream.tile([P, A * K_PASS * 2], U8, name="wf_raw0", offset=3 * TAB_BYTES, align_bytes=64))
+        load_table(1, 0, T)
 
-        load_columns(0, T // 2, T)
-        wf_raw0 = load_wf(0, keep.tile([P, A * K_PASS * 2], U8, name="wf_raw0", align_bytes=64))
-        load_table(1)
-
-        planes = keep.tile([P, 2 * (S + H)], U8, name="planes", align_bytes=64)
-        nc.vector.memset(planes[:].bitcast(I32), 0)
-        rows = keep.tile([P, S + H], U8, name="rows", align_bytes=64)
-        pass_planes = [planes[:, 0 : S + H], rows[:], planes[:, S + H : 2 * (S + H)]]
-        gt_pad = keep.tile([P, B, 2 * PACK], F32, name="gt_pad")
-        gt_sb = gt_pad[:, :, 0:PACK]
-        nc.gpsimd.dma_start(gt_sb, gt.rearrange("(b p t) -> p b t", b=B, t=PACK))
-        nc.scalar.activation(warm_out[:], warm[:], ACT.Sigmoid)
-
-        vs_rows = stream.tile([P, S], U8, name="vs_rows", offset=2 * ODD, align_bytes=64)
-        nc.vector.tensor_copy(vs_rows[:], ts_rows[:].indirect(offs_sb[:]))
+        planes = keep.tile([P, A * PLANE], U8, name="planes", align_bytes=64)
+        plane = [planes[:, a * PLANE : (a + 1) * PLANE] for a in range(A)]
+        nc.vector.memset(plane[2].bitcast(I32), 0)
         nc.vector.tensor_copy(
-            rows[:, S : S + H].rearrange("p (b t m) -> p b t m", t=PACK, m=P),
+            plane[0][:, S:PLANE].rearrange("p (b t m) -> p b t m", t=PACK, m=P),
             wfs_raw[:].rearrange("p (b m t) -> p b t m", t=PACK, m=P),
         )
-        nc.vector.tensor_copy(rows[:, 0:S].bitcast(I32), vs_rows[:].bitcast(I32))
-        tab_sb.append(stream.tile([P, T], U32, name="tab2", offset=ODD * 2, align_bytes=64))
-        carries = [(a, r) for a in range(A) for r in (0, 2, 1, 3) if ROW0 + 16 * a + 4 * r != 32 * r]
-        for i, (a, r) in enumerate(carries):
-            r0 = ROW0 + 16 * a + 4 * r
-            nc.sync.dma_start(pass_planes[a].bitcast(I32)[32 * r : 32 * r + 4, :], rows[:].bitcast(I32)[r0 : r0 + 4, :])
-            if i == 5:
-                load_columns(2, 0, T // 2)
-        load_columns(2, T // 2, T)
-        wf_sb = [order_wf(0, wf_raw0)]
+        nc.vector.tensor_copy(plane[1][:, S:PLANE].bitcast(I32), plane[0][:, S:PLANE].bitcast(I32))
+        vs_rows = stream.tile([P, S], U8, name="vs_rows", offset=2 * TAB_BYTES, align_bytes=64)
+        nc.vector.tensor_copy(vs_rows[:], ts_rows[:].indirect(offs_sb[:]))
+        for a in range(2):
+            nc.vector.tensor_copy(plane[a][:, 0:S].bitcast(I32), vs_rows[:].bitcast(I32))
+
+        def carry(a):
+            source = plane[min(a, 1)].bitcast(I32)
+            for q in (0, 2, 1, 3):
+                r0 = ROW0[a] + 4 * q
+                if r0 != 32 * q:
+                    nc.sync.dma_start(plane[a].bitcast(I32)[32 * q : 32 * q + 4, :], source[r0 : r0 + 4, :])
+
+        carry(0)
+        carry(1)
+        load_table(2, 0, TAB2_CUT)
+        carry(2)
+        load_table(2, TAB2_CUT, T)
 
         v_sb = []
+        wf_sb = []
         for a in range(A):
             picks = []
             for h in range(S // BANK):
@@ -138,23 +145,34 @@ def tile_list_street_shade_exposure_kernel(
                 nc.vector.tensor_copy(picked[:], tab_sb[a][:].indirect(offs_sb[:, 32 * h : 32 * (h + 1)]))
                 picks.append(picked)
             v_sb.append(picks)
-        wf_raw1 = load_wf(1, stream.tile([P, A * K_PASS * 2], U8, name="wf_raw1", offset=0, align_bytes=64))
-        wf_sb.append(order_wf(1, wf_raw1))
+            if a == 0:
+                wf_sb.append(order_wf(0, wf_raw0, nc.scalar.copy))
 
-        ga_pad = stream.tile([P, B, 2 * PACK], F32, name="ga_pad", offset=2 * ODD + 4 * B * N, align_bytes=64)
-        ga_sb = ga_pad[:, :, 0:PACK]
-        nc.sync.dma_start(ga_sb, ga.rearrange("(b p t) -> p b t", b=B, t=PACK))
-        wa_raw = []
-        for b in range(B):
-            raw = stream.tile([P, PACK, N], F32, name="wa_raw%d" % b, offset=(A * K_PASS * 2, ODD)[b], align_bytes=64)
-            nc.sync.dma_start(raw[:], wa[b * K_PASS : (b + 1) * K_PASS, :].rearrange("(p j) n -> p j n", j=PACK))
-            wa_raw.append(raw)
-        wt_sb = stream.tile([P, B * N], U32, name="wt_sb", offset=2 * ODD, align_bytes=64)
+        wf_raw1 = load_wf(1, stream.tile([P, A * K_PASS * 2], U8, name="wf_raw1", offset=0, align_bytes=64))
+        wf_sb.append(order_wf(1, wf_raw1, nc.scalar.copy))
+        wa_raw = {}
+
+        def load_wa(b, j0, j1, flat):
+            raw = flat.rearrange("p (j n) -> p j n", j=PACK)
+            rows = wa[b * K_PASS : (b + 1) * K_PASS, j0 * WA_CHUNK : j1 * WA_CHUNK]
+            nc.sync.dma_start(raw, rows.rearrange("(p j) n -> p j n", j=PACK))
+            for j in range(j0, j1):
+                wa_raw[(b, j)] = raw[:, :, (j - j0) * WA_CHUNK : (j - j0 + 1) * WA_CHUNK]
+
+        def raw_tile(name, pieces, offset):
+            return stream.tile([P, pieces * PACK * WA_CHUNK], F32, name=name, offset=offset, align_bytes=64)
+
+        load_wa(0, 0, 1, raw_tile("wa_first", 1, 4 * S)[:])
+        maps0 = stream.tile([P, PACK * 2 * M], F32, name="maps0", offset=8 * S, align_bytes=64)
+        for slot, (b, j) in enumerate(((0, 1), (0, 2), (1, 0), (1, 1))):
+            load_wa(b, j, j + 1, maps0[:, 2 * slot * M : 2 * (slot + 1) * M])
+        load_wa(1, 2, 3, raw_tile("wa_last", 1, 26 * S)[:])
+        wt_sb = stream.tile([P, B * N], U32, name="wt_sb", offset=40 * S, align_bytes=64)
         nc.sync.dma_start(
             wt_sb[:].bitcast(I32).rearrange("p (b n) -> p b n", b=B),
             wt_words.rearrange("b p n i -> p b (n i)").bitcast(I32),
         )
-        wts = stream.tile([P, B * N], U8, name="wts", offset=ODD + 4 * PACK * N, align_bytes=64)
+        wts = stream.tile([P, B * N], U8, name="wts", offset=3 * TAB_BYTES, align_bytes=64)
         nc.vector.memset(wts[:].bitcast(I32), 0)
         for q in range(QUADS):
             nc.sync.dma_start(
@@ -165,284 +183,248 @@ def tile_list_street_shade_exposure_kernel(
         def bank(i):
             return psum.tile([P, BANK], F32, name="bank%d" % i, tag="bank%d" % i)
 
-        def first_pass(acc, b, t, a, h):
+        h_banks = {}
+
+        def first_pass(b, t, h, a):
+            if a == 0:
+                h_banks[(t, h)] = bank(2 * t + h)
             w0 = a * K_PASS + t * P
             s0 = S + b * K_PASS + t * P
             nc.tensor.matmul_mx(
-                out=acc[:],
+                out=h_banks[(t, h)][:],
                 lhsT=wf_sb[b][:, 2 * w0 : 2 * (w0 + P)].bitcast(FP4X4),
-                lhsT_scale=pass_planes[a][:, s0 : s0 + P],
+                lhsT_scale=plane[a][:, s0 : s0 + P],
                 rhs=v_sb[a][h][:].bitcast(FP8X4),
-                rhs_scale=pass_planes[a][:, h * BANK : (h + 1) * BANK],
+                rhs_scale=plane[a][:, h * BANK : (h + 1) * BANK],
                 start=(a == 0),
                 stop=(a == A - 1),
             )
 
-        h_banks = {}
-        for t in range(PACK):
-            for h in range(2):
-                h_banks[(t, h)] = bank(2 * t + h)
         for a in range(A):
             for pair in range(2):
                 for h in range(2):
                     for t in (2 * pair, 2 * pair + 1):
-                        first_pass(h_banks[(t, h)], 0, t, a, h)
+                        first_pass(0, t, h, a)
 
-        def small(name):
-            return keep.tile([P, B * PACK], F32, name=name)
+        h_sb, gates, towers, canopies, rounded, codes_of, wa_bf, wa_q, y_banks = {}, {}, {}, {}, {}, {}, {}, {}, {}
 
-        size, sign = small("size"), small("sign")
-        nc.scalar.activation(size[:].rearrange("p (b t) -> p b t", b=B), gt_sb, ACT.Abs)
-        nc.scalar.activation(sign[:].rearrange("p (b t) -> p b t", b=B), gt_sb, ACT.Sign)
-        half, root = small("half"), small("root")
-        nc.gpsimd.memset(half[:], 0.5)
-        nc.gpsimd.tensor_tensor(root[:], size[:], half[:], POW)
-        roots = keep.tile([P, B * PACK, M], F32, name="roots")
-        nc.scalar.copy(roots[:], root[:].unsqueeze(2).to_broadcast([P, B * PACK, M]))
-        signs = keep.tile([P, B, SIGN_COLS, PACK], BF16, name="signs", align_bytes=64)
-        nc.scalar.copy(
-            signs[:], sign[:].rearrange("p (b t) -> p b t", b=B).unsqueeze(2).to_broadcast([P, B, SIGN_COLS, PACK])
-        )
+        squares = {}
 
-        work = ctx.enter_context(tc.tile_pool(name="work", bufs=1))
-        shared = ctx.enter_context(tc.tile_pool(name="shared", bufs=1))
-        whole = slice(0, M)
-        first = slice(0, HALF)
-        third, fourth = slice(HALF, HALF + P), slice(HALF + P, M)
-        h_sb = {}
-        gates = {}
-        wa_tiles = {}
-        wa_rounded = {}
-        towers = {}
-        canopies = {}
-        rounded_maps = {}
-        z_codes = {}
-        y_banks = {}
-        emptied = set()
-
-        def empty_half(b, t, h):
+        def empty(b, t, h, on_vector=False):
             if (b, t) not in h_sb:
                 h_sb[(b, t)] = keep.tile([P, S], F32, name="h_sb%d_%d" % (b, t))
-            nc.scalar.copy(h_sb[(b, t)][:, h * BANK : (h + 1) * BANK], h_banks[(t, h)][:])
-            emptied.add((b, t, h))
-
-        def empty(b, t):
-            if b > 0:
-                for h in range(2):
-                    h_banks[(t, h)] = bank(2 * t + h)
-                    for a in range(A):
-                        first_pass(h_banks[(t, h)], b, t, a, h)
-            for h in range(2):
-                if (b, t, h) not in emptied:
-                    empty_half(b, t, h)
+            half = h_sb[(b, t)][:, h * BANK : (h + 1) * BANK]
+            if on_vector:
+                nc.vector.tensor_copy(half, h_banks[(t, h)][:])
+            else:
+                nc.scalar.copy(half, h_banks[(t, h)][:])
 
         def picked(b, t, which, cols):
             return h_sb[(b, t)][:].indirect(pos_sb[which][:, cols.start // 16 : cols.stop // 16])
 
-        def gate(b, t, cols):
-            if (b, t, cols) == (1, 2, fourth):
-                tile = shared.tile([P, P], F32, name="gate_late", offset=0, align_bytes=64)
-            elif (b, t) == (0, 2):
-                tile = shared.tile([P, M], F32, name="gate_early", offset=1024, align_bytes=64)
-            else:
-                tile = work.tile([P, cols.stop - cols.start], F32, name="gate%d_%d_%d" % (b, t, cols.start))
-            gates[(b, t, cols.start)] = tile
-            nc.scalar.activation(tile[:], picked(b, t, 0, cols), ACT.Sigmoid)
+        def slots(table, name, b, cols):
+            key = (b, cols.start)
+            if key not in table:
+                table[key] = keep.tile([P, PACK, cols.stop - cols.start], F32, name="%s%d_%d" % (name, b, cols.start))
+            return table[key]
 
-        def tower(b, t):
-            if b not in towers:
-                towers[b] = work.tile([P, PACK, M], F32, name="tower%d" % b)
-            nc.vector.tensor_tensor(towers[b][:, t, :], picked(b, t, 2, whole), roots[:, PACK * b + t, :], MULT)
+        def gate(b, t, cols):
+            tile = keep.tile([P, cols.stop - cols.start], F32, name="gate%d_%d_%d" % (b, t, cols.start))
+            nc.scalar.activation(tile[:], picked(b, t, 0, cols), ACT.Sigmoid)
+            gates[(b, t, cols.start)] = tile
+
+        def tower(b, t, cols):
+            nc.scalar.activation(slots(towers, "tower", b, cols)[:, t, :], picked(b, t, 2, cols), ACT.Copy)
 
         def canopy(b, t, cols):
-            key = (b, cols.start)
-            if key not in canopies:
-                canopies[key] = work.tile([P, PACK, cols.stop - cols.start], F32, name="canopy%d_%d" % key)
-            nc.vector.tensor_tensor(canopies[key][:, t, :], picked(b, t, 1, cols), gates[(b, t, cols.start)][:], MULT)
-
-        def square(b):
-            squared = work.tile([P, M * PACK], BF16, name="zt_bf%d" % b, align_bytes=64)
-            nc.scalar.activation(interleaved(squared[:], 2), by_slot(towers[b][:], 2), ACT.Square)
-            rounded_maps[("zt", b, 0)] = squared
-
-        def apply_sign(b):
-            runs = rounded_maps[("zt", b, 0)][:].rearrange("p (r x) -> p r x", x=SIGN_COLS * PACK)
-            pattern = signs[:, b, :, :].rearrange("p m t -> p (m t)").unsqueeze(1).to_broadcast([P, M // SIGN_COLS, SIGN_COLS * PACK])
-            nc.vector.tensor_tensor(runs, runs, pattern, MULT)
-
-        def apply_gain(b, cols, piece=None):
-            piece = piece or cols
-            width = cols.stop - cols.start
-            rounded = work.tile([P, width * PACK], BF16, name="za_bf%d_%d" % (b, cols.start), align_bytes=64)
             nc.vector.tensor_tensor(
-                interleaved(rounded[:]),
-                by_slot(canopies[(b, piece.start)][:, :, cols.start - piece.start : cols.stop - piece.start]),
-                ga_sb[:, b, :].unsqueeze(1).unsqueeze(3).to_broadcast([P, width // 4, PACK, 4]),
-                MULT,
-            )
-            rounded_maps[("za", b, cols.start)] = rounded
-
-        def holding(table, name, b, cols):
-            start = max(s for (n, bb, s) in table if (n, bb) == (name, b) and s <= cols.start)
-            return table[(name, b, start)], slice(cols.start - start, cols.stop - start)
-
-        def quantize_map(name, b, cols, piece=None, late=False):
-            piece = piece or cols
-            width = piece.stop - piece.start
-            key = (name, b, piece.start)
-            if key not in z_codes:
-                if late:
-                    codes = shared.tile([P, width], U32, name="codes_late", offset=0, align_bytes=64)
-                else:
-                    codes = keep.tile([P, width], U32, name="%s_codes%d_%d" % key, align_bytes=64)
-                z_codes[key] = (codes, keep.tile([P, width], U8, name="%s_scales%d_%d" % key, align_bytes=64))
-            (codes, scales), local = holding(z_codes, name, b, cols)
-            rounded, source = holding(rounded_maps, name, b, cols)
-            nc.vector.quantize_mx(
-                out=codes[:, local].bitcast(FP8X4),
-                scales=scales[:, local],
-                in_=rounded[:, PACK * source.start : PACK * source.stop],
+                slots(canopies, "canopy", b, cols)[:, t, :], picked(b, t, 1, cols), gates[(b, t, cols.start)][:], MULT
             )
 
-        def round_wa(on_vector, b, j):
-            if on_vector:
-                rounded = shared.tile([P, WA_CHUNK * PACK], BF16, name="wa_bf_vector", offset=1024, align_bytes=64)
+        def square(b, t, cols):
+            values = towers[(b, cols.start)][:, t, :]
+            squared = squares.setdefault((b, cols.start), towers[(b, cols.start)])
+            nc.vector.scalar_tensor_tensor(squared[:, t, :], values, gt_sb[:, b, t : t + 1], values, MULT, MULT)
+
+        def round_map(name, b, cols, on_scalar=False):
+            width = cols.stop - cols.start
+            if (name, b) == ("za", 0):
+                tile = stream.tile([P, width * PACK], BF16, name="za_bf0", offset=24 * S, align_bytes=64)
             else:
-                rounded = ring.tile([P, WA_CHUNK * PACK], BF16, name="wa_bf", bufs=4, align_bytes=64)
-            src = wa_raw[b][:, :, j * WA_CHUNK : (j + 1) * WA_CHUNK]
-            if on_vector:
-                nc.vector.tensor_copy(interleaved(rounded[:]), by_slot(src))
+                tile = keep.tile([P, width * PACK], BF16, name="%s_bf%d_%d" % (name, b, cols.start), align_bytes=64)
+            rounded[(name, b, cols.start)] = tile
+            if name == "zt":
+                made = max(c for (bb, c) in squares if bb == b and c <= cols.start)
+                source = squares[(b, made)][:, :, cols.start - made : cols.stop - made]
+                copy = nc.scalar.copy if on_scalar else nc.vector.tensor_copy
+                copy(woven(tile[:]), by_slot(source))
             else:
-                nc.scalar.copy(interleaved(rounded[:], 2), by_slot(src, 2))
-            wa_rounded[(b, j)] = rounded
+                nc.vector.tensor_tensor(
+                    woven(tile[:]),
+                    by_slot(canopies[(b, cols.start)][:, :, :]),
+                    ga_sb[:, b, 0:PACK].unsqueeze(1).unsqueeze(3).to_broadcast([P, width // 4, PACK, 4]),
+                    MULT,
+                )
+
+        def quantize(name, width, source):
+            codes = keep.tile([P, width], U32, name=name + "_codes", align_bytes=64)
+            scales = keep.tile([P, width], U8, name=name + "_scales", align_bytes=64)
+            nc.vector.quantize_mx(out=codes[:].bitcast(FP8X4), scales=scales[:], in_=source[:])
+            return codes, scales
+
+        def quantize_map(name, b, cols):
+            key = (name, b, cols.start)
+            codes_of[key] = quantize("%s%d_%d" % key, cols.stop - cols.start, rounded[key])
+
+        def round_wa(b, j):
+            tile = ring.tile([P, WA_CHUNK * PACK], BF16, name="wa_bf", align_bytes=64)
+            nc.vector.tensor_copy(woven(tile[:]), by_slot(wa_raw[(b, j)]))
+            wa_bf[(b, j)] = tile
 
         def quantize_wa(b, j):
-            codes = keep.tile([P, WA_CHUNK], U32, name="wa_codes%d_%d" % (b, j), align_bytes=64)
-            scales = keep.tile([P, WA_CHUNK], U8, name="wa_scales%d_%d" % (b, j), align_bytes=64)
-            nc.vector.quantize_mx(out=codes[:].bitcast(FP8X4), scales=scales[:], in_=wa_rounded[(b, j)][:])
-            for i in range(WA_CHUNK // P):
-                wa_tiles[(b, j * (WA_CHUNK // P) + i)] = (codes[:, i * P : (i + 1) * P], scales[:, i * P : (i + 1) * P])
+            wa_q[(b, j)] = quantize("wa%d_%d" % (b, j), WA_CHUNK, wa_bf[(b, j)])
 
         def weights(name, b, n_tile):
             if name == "za":
-                return wa_tiles[(b, n_tile)]
+                codes, scales = wa_q[(b, n_tile * P // WA_CHUNK)]
+                n0 = n_tile * P % WA_CHUNK
+                return codes[:, n0 : n0 + P], scales[:, n0 : n0 + P]
             n0 = b * N + n_tile * P
             return wt_sb[:, n0 : n0 + P], wts[:, n0 : n0 + P]
 
-        def groups(cols):
-            width = cols.stop - cols.start
-            per_bank = 3 if cols == third else 2
-            first_bank = 0 if cols.start < HALF else 3 + 2 * ((cols.start - HALF) // width)
-            return [(first_bank + g, range(g * per_bank, (g + 1) * per_bank)) for g in range(N_TILES // per_bank)]
+        whole = slice(0, M)
+        pieces = [slice(0, 2 * P), slice(2 * P, 3 * P), slice(3 * P, M)]
+        piece_banks = [(0, 1, 2), (3, 4), (5, 6, 7)]
 
-        def second_passes(name, b, cols, start, stop, only=None):
-            (codes, scales), local = holding(z_codes, name, b, cols)
+        def groups(i):
+            per_bank = N_TILES // len(piece_banks[i])
+            return [(no, range(g * per_bank, (g + 1) * per_bank)) for g, no in enumerate(piece_banks[i])]
+
+        def second_passes(name, b, i, start, stop):
+            cols = pieces[i]
             width = cols.stop - cols.start
-            for g, (bank_no, n_tiles) in enumerate(groups(cols)):
-                if only is not None and g not in only:
-                    continue
+            made = max(c for (n, bb, c) in codes_of if (n, bb) == (name, b) and c <= cols.start)
+            c0 = cols.start - made
+            codes, scales = codes_of[(name, b, made)]
+            for no, n_tiles in groups(i):
                 if start:
-                    y_banks[bank_no] = bank(bank_no)
+                    y_banks[no] = bank(no)
                 for j, n_tile in enumerate(n_tiles):
                     w_codes, w_scales = weights(name, b, n_tile)
                     nc.tensor.matmul_mx(
-                        out=y_banks[bank_no][:, j * width : (j + 1) * width],
+                        out=y_banks[no][:, j * width : (j + 1) * width],
                         lhsT=w_codes.bitcast(FP8X4),
                         lhsT_scale=w_scales,
-                        rhs=codes[:, local].bitcast(FP8X4),
-                        rhs_scale=scales[:, local],
+                        rhs=codes[:, c0 : c0 + width].bitcast(FP8X4),
+                        rhs_scale=scales[:, c0 : c0 + width],
                         start=(start and j == 0),
                         stop=(stop and j == len(n_tiles) - 1),
                     )
 
-        def finish(cols, only=None):
+        def finish(i):
+            cols = pieces[i]
             width = cols.stop - cols.start
-            for g, (bank_no, n_tiles) in enumerate(groups(cols)):
-                if only is not None and g not in only:
-                    continue
-                result = keep.tile([P, len(n_tiles), width], F32, name="result%d" % bank_no)
+            for no, n_tiles in groups(i):
+                result = keep.tile([P, len(n_tiles), width], F32, name="result%d" % no)
                 nc.scalar.activation(
-                    result[:].rearrange("p j m -> p (j m)"), y_banks[bank_no][:, 0 : len(n_tiles) * width], ACT.Sigmoid
+                    result[:].rearrange("p j m -> p (j m)"), y_banks[no][:, 0 : len(n_tiles) * width], ACT.Sigmoid
                 )
                 rows_out = out[n_tiles.start * P : n_tiles.stop * P, cols]
                 nc.sync.dma_start(rows_out.rearrange("(j p) m -> p j m", p=P), result[:])
 
-        pieces = [first, third, fourth]
-        empty_half(0, 0, 0)
-        empty_half(0, 1, 0)
-        for t in range(2):
-            empty(0, t)
-            gate(0, t, whole)
-            tower(0, t)
-            canopy(0, t, whole)
-        for t in range(2, PACK):
-            empty(0, t)
-            tower(0, t)
-        for t in range(2, PACK):
-            gate(0, t, whole)
-            canopy(0, t, whole)
-        square(0)
-        round_wa(True, 0, 0)
-        apply_gain(0, whole)
-        empty(1, 0)
-        apply_sign(0)
-        empty(1, 1)
-        quantize_map("za", 0, whole)
-        quantize_map("zt", 0, whole)
-        tower(1, 0)
-        tower(1, 1)
-        for t in range(2, PACK):
-            empty(1, t)
-            tower(1, t)
+        def refill(t):
+            for h in range(2):
+                for a in range(A):
+                    first_pass(1, t, h, a)
+
+        both = maps0[:].rearrange("p (t u m) -> p u t m", t=PACK, u=2)
+        canopies[(0, 0)] = both[:, 0, :, :]
+        squares[(0, 0)] = both[:, 1, :, :]
+        canopies[(1, 0)] = stream.tile([P, PACK, M], F32, name="canopy1", offset=28 * S, align_bytes=64)
+        h_sb[(0, 0)] = stream.tile([P, S], F32, name="h_sb0_0", offset=0, align_bytes=64)
+
+        empty(0, 0, 0)
+        empty(0, 0, 1)
+        empty(0, 1, 0, True)
+        empty(0, 1, 1, True)
+        empty(0, 2, 0)
+        gate(0, 0, whole)
+        empty(0, 2, 1)
+        gate(0, 1, whole)
+        tiles = [(b, t) for b in range(B) for t in range(PACK)]
+        for ahead, behind in zip(tiles[3:], tiles[2:]):
+            if ahead[0] == 1:
+                refill(ahead[1])
+            empty(*ahead, 0)
+            empty(*ahead, 1)
+            gate(*behind, whole)
+        gate(1, PACK - 1, whole)
+        for t in range(PACK):
+            tower(0, t, whole)
+        for cols in pieces:
+            for t in range(PACK):
+                tower(1, t, cols)
+
+        round_wa(0, 0)
+        round_wa(0, 1)
         quantize_wa(0, 0)
-        for cols in pieces:
-            second_passes("zt", 0, cols, True, False)
-        for t in range(PACK):
-            gate(1, t, first)
-            canopy(1, t, first)
-        round_wa(False, 0, 1)
-        round_wa(False, 0, 2)
-        square(1)
-        round_wa(False, 1, 0)
-        round_wa(False, 1, 1)
+        canopy(0, 0, whole)
+        round_wa(0, 2)
         quantize_wa(0, 1)
+        canopy(0, 1, whole)
+        round_wa(1, 0)
         quantize_wa(0, 2)
-        for cols in pieces:
-            second_passes("za", 0, cols, False, False)
-        apply_gain(1, first)
-        apply_sign(1)
-        quantize_map("za", 1, first)
-        quantize_map("zt", 1, first)
-        quantize_map("zt", 1, third)
-        for cols in (first, third):
-            second_passes("zt", 1, cols, False, False)
-        for t in range(PACK):
-            gate(1, t, third)
-        round_wa(False, 1, 2)
-        for t in range(PACK):
-            gate(1, t, fourth)
+        canopy(0, 2, whole)
+        round_wa(1, 1)
         quantize_wa(1, 0)
+        canopy(0, 3, whole)
+        round_wa(1, 2)
         quantize_wa(1, 1)
-        second_passes("za", 1, first, False, True, only=(0, 1))
-        finish(first, only=(0, 1))
-        for t in range(PACK):
-            canopy(1, t, third)
+        round_map("za", 0, whole)
         quantize_wa(1, 2)
-        second_passes("za", 1, first, False, True, only=(2,))
-        finish(first, only=(2,))
-        apply_gain(1, third)
-        canopy(1, 0, fourth)
-        quantize_map("za", 1, third)
-        second_passes("za", 1, third, False, True)
-        finish(third)
+        canopy(1, 0, whole)
+        quantize_map("za", 0, whole)
+        for i in range(len(pieces)):
+            second_passes("za", 0, i, True, False)
         for t in range(1, PACK):
-            canopy(1, t, fourth)
-        quantize_map("zt", 1, fourth, late=True)
-        second_passes("zt", 1, fourth, False, False)
-        eighths = [slice(fourth.start, fourth.start + P // 2), slice(fourth.start + P // 2, M)]
-        for cols in eighths:
-            apply_gain(1, cols, fourth)
-        for cols in eighths:
-            quantize_map("za", 1, cols, fourth)
-        second_passes("za", 1, fourth, False, True)
-        finish(fourth)
+            canopy(1, t, whole)
+        square(0, 0, whole)
+        round_map("za", 1, whole)
+        square(0, 1, whole)
+        quantize_map("za", 1, whole)
+        for i in range(len(pieces)):
+            second_passes("za", 1, i, False, False)
+        square(0, 2, whole)
+        square(0, 3, whole)
+        first, third, fourth = pieces
+        second = slice(third.start, fourth.stop)
+        square(1, 0, first)
+        round_map("zt", 0, first)
+        square(1, 1, first)
+        quantize_map("zt", 0, first)
+        second_passes("zt", 0, 0, False, False)
+        square(1, 2, first)
+        square(1, 3, first)
+        square(1, 0, third)
+        round_map("zt", 1, first)
+        square(1, 1, third)
+        quantize_map("zt", 1, first)
+        second_passes("zt", 1, 0, False, True)
+        finish(0)
+        square(1, 2, third)
+        round_map("zt", 0, second)
+        square(1, 3, third)
+        quantize_map("zt", 0, second)
+        for i in (1, 2):
+            second_passes("zt", 0, i, False, False)
+        round_map("zt", 1, third)
+        square(1, 0, fourth)
+        quantize_map("zt", 1, third)
+        second_passes("zt", 1, 1, False, True)
+        finish(1)
+        for t in range(1, PACK):
+            square(1, t, fourth)
+        round_map("zt", 1, fourth)
+        quantize_map("zt", 1, fourth)
+        second_passes("zt", 1, 2, False, True)
+        finish(2)

@@ -15,6 +15,7 @@ FP8X4 = mybir.dt.float8_e4m3fn_x4
 FP4X4 = mybir.dt.float4_e2m1fn_x4
 ACT = mybir.ActivationFunctionType
 MULT = mybir.AluOpType.mult
+ADD = mybir.AluOpType.add
 
 P = 128
 PACK = 4
@@ -266,10 +267,13 @@ def tile_list_street_shade_exposure_kernel(
                     MULT,
                 )
 
-        def quantize(name, width, source):
+        def quantize(name, width, *sources):
             codes = keep.tile([P, width], U32, name=name + "_codes", align_bytes=64)
             scales = keep.tile([P, width], U8, name=name + "_scales", align_bytes=64)
-            nc.vector.quantize_mx(out=codes[:].bitcast(FP8X4), scales=scales[:], in_=source[:])
+            part = width // len(sources)
+            for i, source in enumerate(sources):
+                at = slice(i * part, (i + 1) * part)
+                nc.vector.quantize_mx(out=codes[:, at].bitcast(FP8X4), scales=scales[:, at], in_=source[:])
             return codes, scales
 
         def quantize_map(name, b, cols):
@@ -278,7 +282,13 @@ def tile_list_street_shade_exposure_kernel(
 
         def round_wa(b, j):
             tile = ring.tile([P, WA_CHUNK * PACK], BF16, name="wa_bf", align_bytes=64)
-            nc.vector.tensor_copy(woven(tile[:]), by_slot(wa_raw[(b, j)]))
+            raw = wa_raw[(b, j)]
+            if (b, j) == (0, 0):
+                nc.gpsimd.tensor_scalar(
+                    tile[:].rearrange("p (c t) -> p c t", t=PACK), raw.rearrange("p t c -> p c t"), 1.0, 0.0, MULT, ADD
+                )
+            else:
+                nc.vector.tensor_copy(woven(tile[:]), by_slot(raw))
             wa_bf[(b, j)] = tile
 
         def quantize_wa(b, j):
@@ -424,7 +434,9 @@ def tile_list_street_shade_exposure_kernel(
         finish(1)
         for t in range(1, PACK):
             square(1, t, fourth)
-        round_map("zt", 1, fourth)
-        quantize_map("zt", 1, fourth)
+        eighths = [slice(fourth.start, fourth.start + P // 2), slice(fourth.start + P // 2, M)]
+        for cols in eighths:
+            round_map("zt", 1, cols)
+        codes_of[("zt", 1, fourth.start)] = quantize("zt_last", P, *[rounded[("zt", 1, cols.start)] for cols in eighths])
         second_passes("zt", 1, 2, False, True)
         finish(2)

@@ -29,6 +29,7 @@ N_TILES = N // P
 WA_CHUNK = 256
 TAB_BYTES = 4 * T
 WA_BYTES = 4 * PACK * WA_CHUNK
+PASS_BYTES = 2 * K_PASS
 PLANE = S + H
 ROW0 = (0, 56, 72)
 TAB0_CUT = 3 * T // 8
@@ -86,17 +87,20 @@ def tile_list_street_shade_exposure_kernel(
 
         wf_hbm = wf_words.bitcast(I32).rearrange("a p (b x) -> b p a x", b=B)
 
-        def load_wf(b, raw):
-            nc.sync.dma_start(raw[:].bitcast(I32).rearrange("p (a x) -> p a x", a=A), wf_hbm[b])
+        wf_sb = {}
+
+        def load_wf(b, passes, raw):
+            count = passes.stop - passes.start
+            nc.sync.dma_start(raw[:].bitcast(I32).rearrange("p (a x) -> p a x", a=count), wf_hbm[b][:, passes, :])
             return raw
 
-        def order_wf(b, raw, copy):
-            ordered = keep.tile([P, A * K_PASS * 2], U8, name="wf_sb%d" % b, align_bytes=64)
+        def order_wf(b, passes, raw, ordered, copy):
             copy(
                 ordered[:].bitcast(U16).rearrange("p (a t m) -> p t a m", t=PACK, m=P),
                 raw[:].bitcast(U16).rearrange("p (a m t) -> p t a m", t=PACK, m=P),
             )
-            return ordered
+            for a in range(passes.start, passes.stop):
+                wf_sb[(b, a)] = ordered[:, (a - passes.start) * PASS_BYTES : (a - passes.start + 1) * PASS_BYTES]
 
         load_table(0, 0, TAB0_CUT)
         offs_sb = keep.tile([P, S // 16], U16, name="offs_sb")
@@ -108,7 +112,7 @@ def tile_list_street_shade_exposure_kernel(
             lst = keep.tile([P, M // 16], U16, name="pos%d" % i)
             nc.sync.dma_start(lst[:], pos)
             pos_sb.append(lst)
-        wf_raw0 = load_wf(0, stream.tile([P, A * K_PASS * 2], U8, name="wf_raw0", offset=3 * TAB_BYTES, align_bytes=64))
+        wf_raw0 = load_wf(0, slice(0, A), stream.tile([P, A * K_PASS * 2], U8, name="wf_raw0", offset=3 * TAB_BYTES, align_bytes=64))
         load_table(1, 0, T)
 
         planes = keep.tile([P, A * PLANE], U8, name="planes", align_bytes=64)
@@ -138,7 +142,6 @@ def tile_list_street_shade_exposure_kernel(
         load_table(2, TAB2_CUT, T)
 
         v_sb = []
-        wf_sb = []
         for a in range(A):
             picks = []
             for h in range(S // BANK):
@@ -147,10 +150,13 @@ def tile_list_street_shade_exposure_kernel(
                 picks.append(picked)
             v_sb.append(picks)
             if a == 0:
-                wf_sb.append(order_wf(0, wf_raw0, nc.scalar.copy))
+                wf_first = keep.tile([P, A * PASS_BYTES], U8, name="wf_sb0", align_bytes=64)
+                order_wf(0, slice(0, A), wf_raw0, wf_first, nc.scalar.copy)
 
-        wf_raw1 = load_wf(1, stream.tile([P, A * K_PASS * 2], U8, name="wf_raw1", offset=0, align_bytes=64))
-        wf_sb.append(order_wf(1, wf_raw1, nc.scalar.copy))
+        wf_raw1 = load_wf(1, slice(0, 2), stream.tile([P, 2 * PASS_BYTES], U8, name="wf_raw1", offset=0, align_bytes=64))
+        wf_raw2 = load_wf(1, slice(2, A), stream.tile([P, PASS_BYTES], U8, name="wf_raw2", offset=4 * S, align_bytes=64))
+        wf_early = keep.tile([P, 2 * PASS_BYTES], U8, name="wf_sb1", align_bytes=64)
+        order_wf(1, slice(0, 2), wf_raw1, wf_early, nc.scalar.copy)
         wa_raw = {}
 
         def load_wa(b, j0, j1, flat):
@@ -163,11 +169,11 @@ def tile_list_street_shade_exposure_kernel(
         def raw_tile(name, pieces, offset):
             return stream.tile([P, pieces * PACK * WA_CHUNK], F32, name=name, offset=offset, align_bytes=64)
 
-        load_wa(0, 0, 1, raw_tile("wa_first", 1, 4 * S)[:])
-        maps0 = stream.tile([P, PACK * 2 * M], F32, name="maps0", offset=8 * S, align_bytes=64)
+        load_wa(0, 0, 1, raw_tile("wa_first", 1, 5 * S)[:])
+        maps0 = stream.tile([P, PACK * 2 * M], F32, name="maps0", offset=9 * S, align_bytes=64)
         for slot, (b, j) in enumerate(((0, 1), (0, 2), (1, 0), (1, 1))):
             load_wa(b, j, j + 1, maps0[:, 2 * slot * M : 2 * (slot + 1) * M])
-        load_wa(1, 2, 3, raw_tile("wa_last", 1, 26 * S)[:])
+        load_wa(1, 2, 3, raw_tile("wa_last", 1, 27 * S)[:])
         wt_sb = stream.tile([P, B * N], U32, name="wt_sb", offset=40 * S, align_bytes=64)
         nc.sync.dma_start(
             wt_sb[:].bitcast(I32).rearrange("p (b n) -> p b n", b=B),
@@ -189,11 +195,10 @@ def tile_list_street_shade_exposure_kernel(
         def first_pass(b, t, h, a):
             if a == 0:
                 h_banks[(t, h)] = bank(2 * t + h)
-            w0 = a * K_PASS + t * P
             s0 = S + b * K_PASS + t * P
             nc.tensor.matmul_mx(
                 out=h_banks[(t, h)][:],
-                lhsT=wf_sb[b][:, 2 * w0 : 2 * (w0 + P)].bitcast(FP4X4),
+                lhsT=wf_sb[(b, a)][:, 2 * t * P : 2 * (t + 1) * P].bitcast(FP4X4),
                 lhsT_scale=plane[a][:, s0 : s0 + P],
                 rhs=v_sb[a][h][:].bitcast(FP8X4),
                 rhs_scale=plane[a][:, h * BANK : (h + 1) * BANK],
@@ -250,7 +255,7 @@ def tile_list_street_shade_exposure_kernel(
         def round_map(name, b, cols, on_scalar=False):
             width = cols.stop - cols.start
             if (name, b) == ("za", 0):
-                tile = stream.tile([P, width * PACK], BF16, name="za_bf0", offset=24 * S, align_bytes=64)
+                tile = stream.tile([P, width * PACK], BF16, name="za_bf0", offset=25 * S, align_bytes=64)
             else:
                 tile = keep.tile([P, width * PACK], BF16, name="%s_bf%d_%d" % (name, b, cols.start), align_bytes=64)
             rounded[(name, b, cols.start)] = tile
@@ -350,13 +355,16 @@ def tile_list_street_shade_exposure_kernel(
         both = maps0[:].rearrange("p (t u m) -> p u t m", t=PACK, u=2)
         canopies[(0, 0)] = both[:, 0, :, :]
         squares[(0, 0)] = both[:, 1, :, :]
-        canopies[(1, 0)] = stream.tile([P, PACK, M], F32, name="canopy1", offset=28 * S, align_bytes=64)
+        canopies[(1, 0)] = stream.tile([P, PACK, M], F32, name="canopy1", offset=29 * S, align_bytes=64)
         h_sb[(0, 0)] = stream.tile([P, S], F32, name="h_sb0_0", offset=0, align_bytes=64)
 
         empty(0, 0, 0)
         empty(0, 0, 1)
         empty(0, 1, 0, True)
         empty(0, 1, 1, True)
+        round_wa(0, 0)
+        wf_late = stream.tile([P, PASS_BYTES], U8, name="wf_sb2", offset=5 * S, align_bytes=64)
+        order_wf(1, slice(2, A), wf_raw2, wf_late, nc.vector.tensor_copy)
         empty(0, 2, 0)
         gate(0, 0, whole)
         empty(0, 2, 1)
@@ -375,7 +383,6 @@ def tile_list_street_shade_exposure_kernel(
             for t in range(PACK):
                 tower(1, t, cols)
 
-        round_wa(0, 0)
         round_wa(0, 1)
         quantize_wa(0, 0)
         canopy(0, 0, whole)

@@ -76,6 +76,9 @@ def tile_list_street_shade_exposure_kernel(
             nc.gpsimd.dma_start(padded[:, :, 0:PACK], gain.rearrange("(b p t) -> p b t", b=B, t=PACK))
             gains.append(padded)
         ga_sb, gt_sb = gains
+        ga_rows = keep.tile([P, B, PACK, M], F32, name="ga_rows")
+        for b in range(B):
+            nc.scalar.copy(ga_rows[:, b, :, :], ga_sb[:, b, 0:PACK].unsqueeze(2).to_broadcast([P, PACK, M]))
 
         tab_sb = []
 
@@ -171,10 +174,11 @@ def tile_list_street_shade_exposure_kernel(
 
         load_wa(0, 0, 1, raw_tile("wa_first", 1, 5 * S)[:])
         maps0 = stream.tile([P, PACK * 2 * M], F32, name="maps0", offset=9 * S, align_bytes=64)
-        for slot, (b, j) in enumerate(((0, 1), (0, 2), (1, 0), (1, 1))):
+        for slot, (b, j) in ((1, (0, 1)), (2, (0, 2)), (3, (1, 0))):
             load_wa(b, j, j + 1, maps0[:, 2 * slot * M : 2 * (slot + 1) * M])
-        load_wa(1, 2, 3, raw_tile("wa_last", 1, 27 * S)[:])
-        wt_sb = stream.tile([P, B * N], U32, name="wt_sb", offset=40 * S, align_bytes=64)
+        load_wa(1, 1, 2, raw_tile("wa_fifth", 1, 25 * S)[:])
+        load_wa(1, 2, 3, raw_tile("wa_last", 1, 31 * S)[:])
+        wt_sb = stream.tile([P, B * N], U32, name="wt_sb", offset=41 * S, align_bytes=64)
         nc.sync.dma_start(
             wt_sb[:].bitcast(I32).rearrange("p (b n) -> p b n", b=B),
             wt_words.rearrange("b p n i -> p b (n i)").bitcast(I32),
@@ -235,16 +239,14 @@ def tile_list_street_shade_exposure_kernel(
             return table[key]
 
         def gate(b, t, cols):
-            tile = keep.tile([P, cols.stop - cols.start], F32, name="gate%d_%d_%d" % (b, t, cols.start))
-            nc.scalar.activation(tile[:], picked(b, t, 0, cols), ACT.Sigmoid)
-            gates[(b, t, cols.start)] = tile
+            nc.scalar.activation(slots(gates, "gate", b, cols)[:, t, :], picked(b, t, 0, cols), ACT.Sigmoid)
 
         def tower(b, t, cols):
             nc.scalar.activation(slots(towers, "tower", b, cols)[:, t, :], picked(b, t, 2, cols), ACT.Copy)
 
         def canopy(b, t, cols):
             nc.vector.tensor_tensor(
-                slots(canopies, "canopy", b, cols)[:, t, :], picked(b, t, 1, cols), gates[(b, t, cols.start)][:], MULT
+                slots(canopies, "canopy", b, cols)[:, t, :], picked(b, t, 1, cols), ga_rows[:, b, t, :], MULT
             )
 
         def square(b, t, cols):
@@ -255,7 +257,7 @@ def tile_list_street_shade_exposure_kernel(
         def round_map(name, b, cols, on_scalar=False):
             width = cols.stop - cols.start
             if (name, b) == ("za", 0):
-                tile = stream.tile([P, width * PACK], BF16, name="za_bf0", offset=25 * S, align_bytes=64)
+                tile = stream.tile([P, width * PACK], BF16, name="za_bf0", offset=29 * S, align_bytes=64)
             else:
                 tile = keep.tile([P, width * PACK], BF16, name="%s_bf%d_%d" % (name, b, cols.start), align_bytes=64)
             rounded[(name, b, cols.start)] = tile
@@ -268,7 +270,7 @@ def tile_list_street_shade_exposure_kernel(
                 nc.vector.tensor_tensor(
                     woven(tile[:]),
                     by_slot(canopies[(b, cols.start)][:, :, :]),
-                    ga_sb[:, b, 0:PACK].unsqueeze(1).unsqueeze(3).to_broadcast([P, width // 4, PACK, 4]),
+                    by_slot(gates[(b, cols.start)][:]),
                     MULT,
                 )
 
@@ -355,7 +357,7 @@ def tile_list_street_shade_exposure_kernel(
         both = maps0[:].rearrange("p (t u m) -> p u t m", t=PACK, u=2)
         canopies[(0, 0)] = both[:, 0, :, :]
         squares[(0, 0)] = both[:, 1, :, :]
-        canopies[(1, 0)] = stream.tile([P, PACK, M], F32, name="canopy1", offset=29 * S, align_bytes=64)
+        canopies[(1, 0)] = stream.tile([P, PACK, M], F32, name="canopy1", offset=33 * S, align_bytes=64)
         h_sb[(0, 0)] = stream.tile([P, S], F32, name="h_sb0_0", offset=0, align_bytes=64)
 
         empty(0, 0, 0)
@@ -383,18 +385,18 @@ def tile_list_street_shade_exposure_kernel(
             for t in range(PACK):
                 tower(1, t, cols)
 
+        canopy(0, 0, whole)
         round_wa(0, 1)
         quantize_wa(0, 0)
-        canopy(0, 0, whole)
+        canopy(0, 1, whole)
         round_wa(0, 2)
         quantize_wa(0, 1)
-        canopy(0, 1, whole)
+        canopy(0, 2, whole)
         round_wa(1, 0)
         quantize_wa(0, 2)
-        canopy(0, 2, whole)
+        canopy(0, 3, whole)
         round_wa(1, 1)
         quantize_wa(1, 0)
-        canopy(0, 3, whole)
         round_wa(1, 2)
         quantize_wa(1, 1)
         round_map("za", 0, whole)

@@ -218,8 +218,6 @@ def tile_list_street_shade_exposure_kernel(
 
         h_sb, gates, towers, canopies, rounded, codes_of, wa_bf, wa_q, y_banks = {}, {}, {}, {}, {}, {}, {}, {}, {}
 
-        squares = {}
-
         def empty(b, t, h, on_vector=False):
             if (b, t) not in h_sb:
                 h_sb[(b, t)] = keep.tile([P, S], F32, name="h_sb%d_%d" % (b, t))
@@ -246,31 +244,28 @@ def tile_list_street_shade_exposure_kernel(
 
         def canopy(b, t, cols):
             nc.vector.tensor_tensor(
-                slots(canopies, "canopy", b, cols)[:, t, :], picked(b, t, 1, cols), ga_rows[:, b, t, :], MULT
+                canopies[(b, 0)][:, t, cols], picked(b, t, 1, cols), ga_rows[:, b, t, cols], MULT
             )
 
         def square(b, t, cols):
-            values = towers[(b, cols.start)][:, t, :]
-            squared = squares.setdefault((b, cols.start), towers[(b, cols.start)])
-            nc.vector.scalar_tensor_tensor(squared[:, t, :], values, gt_sb[:, b, t : t + 1], values, MULT, MULT)
+            values = towers[(b, 0)][:, t, cols]
+            nc.vector.scalar_tensor_tensor(values, values, gt_sb[:, b, t : t + 1], values, MULT, MULT)
 
-        def round_map(name, b, cols, on_scalar=False):
+        def round_map(name, b, cols):
             width = cols.stop - cols.start
-            if (name, b) == ("za", 0):
-                tile = stream.tile([P, width * PACK], BF16, name="za_bf0", offset=29 * S, align_bytes=64)
+            if (name, b) == ("zt", 0):
+                tile = stream.tile([P, width * PACK], BF16, name="zt_bf0", offset=29 * S, align_bytes=64)
             else:
                 tile = keep.tile([P, width * PACK], BF16, name="%s_bf%d_%d" % (name, b, cols.start), align_bytes=64)
             rounded[(name, b, cols.start)] = tile
             if name == "zt":
-                made = max(c for (bb, c) in squares if bb == b and c <= cols.start)
-                source = squares[(b, made)][:, :, cols.start - made : cols.stop - made]
-                copy = nc.scalar.copy if on_scalar else nc.vector.tensor_copy
-                copy(woven(tile[:]), by_slot(source))
+                nc.vector.tensor_copy(woven(tile[:]), by_slot(towers[(b, 0)][:, :, cols]))
             else:
+                made = max(c for (bb, c) in gates if bb == b and c <= cols.start)
                 nc.vector.tensor_tensor(
                     woven(tile[:]),
-                    by_slot(canopies[(b, cols.start)][:, :, :]),
-                    by_slot(gates[(b, cols.start)][:]),
+                    by_slot(canopies[(b, 0)][:, :, cols]),
+                    by_slot(gates[(b, made)][:, :, cols.start - made : cols.stop - made]),
                     MULT,
                 )
 
@@ -356,7 +351,6 @@ def tile_list_street_shade_exposure_kernel(
 
         both = maps0[:].rearrange("p (t u m) -> p u t m", t=PACK, u=2)
         canopies[(0, 0)] = both[:, 0, :, :]
-        squares[(0, 0)] = both[:, 1, :, :]
         canopies[(1, 0)] = stream.tile([P, PACK, M], F32, name="canopy1", offset=33 * S, align_bytes=64)
         h_sb[(0, 0)] = stream.tile([P, S], F32, name="h_sb0_0", offset=0, align_bytes=64)
 
@@ -368,22 +362,25 @@ def tile_list_street_shade_exposure_kernel(
         wf_late = stream.tile([P, PASS_BYTES], U8, name="wf_sb2", offset=5 * S, align_bytes=64)
         order_wf(1, slice(2, A), wf_raw2, wf_late, nc.vector.tensor_copy)
         empty(0, 2, 0)
-        gate(0, 0, whole)
+        tower(0, 0, whole)
         empty(0, 2, 1)
-        gate(0, 1, whole)
+        tower(0, 1, whole)
         tiles = [(b, t) for b in range(B) for t in range(PACK)]
         for ahead, behind in zip(tiles[3:], tiles[2:]):
             if ahead[0] == 1:
                 refill(ahead[1])
             empty(*ahead, 0)
             empty(*ahead, 1)
-            gate(*behind, whole)
-        gate(1, PACK - 1, whole)
+            tower(*behind, whole)
+            if behind == (1, 0):
+                for t in range(PACK):
+                    gate(0, t, whole)
         for t in range(PACK):
-            tower(0, t, whole)
-        for cols in pieces:
+            gate(1, t, pieces[0])
+        tower(1, PACK - 1, whole)
+        for cols in pieces[1:]:
             for t in range(PACK):
-                tower(1, t, cols)
+                gate(1, t, cols)
 
         canopy(0, 0, whole)
         round_wa(0, 1)
@@ -394,58 +391,55 @@ def tile_list_street_shade_exposure_kernel(
         canopy(0, 2, whole)
         round_wa(1, 0)
         quantize_wa(0, 2)
+        square(0, 0, whole)
         canopy(0, 3, whole)
         round_wa(1, 1)
         quantize_wa(1, 0)
+        square(0, 1, whole)
         round_wa(1, 2)
         quantize_wa(1, 1)
-        round_map("za", 0, whole)
-        quantize_wa(1, 2)
-        canopy(1, 0, whole)
-        quantize_map("za", 0, whole)
-        for i in range(len(pieces)):
-            second_passes("za", 0, i, True, False)
-        for t in range(1, PACK):
-            canopy(1, t, whole)
-        square(0, 0, whole)
-        round_map("za", 1, whole)
-        square(0, 1, whole)
-        quantize_map("za", 1, whole)
-        for i in range(len(pieces)):
-            second_passes("za", 1, i, False, False)
         square(0, 2, whole)
         square(0, 3, whole)
+        quantize_wa(1, 2)
+        round_map("zt", 0, whole)
+        canopy(1, 0, whole)
+        quantize_map("zt", 0, whole)
+        for i in range(len(pieces)):
+            second_passes("zt", 0, i, True, False)
+        canopy(1, 1, whole)
+        square(1, 0, whole)
+        round_map("za", 0, whole)
+        canopy(1, 2, whole)
         first, third, fourth = pieces
         second = slice(third.start, fourth.stop)
-        square(1, 0, first)
-        round_map("zt", 0, first)
-        square(1, 1, first)
-        quantize_map("zt", 0, first)
-        second_passes("zt", 0, 0, False, False)
+        square(1, 1, whole)
+        canopy(1, 3, first)
         square(1, 2, first)
+        quantize_map("za", 0, whole)
+        for i in range(len(pieces)):
+            second_passes("za", 0, i, False, False)
+        round_map("za", 1, first)
         square(1, 3, first)
-        square(1, 0, third)
+        quantize_map("za", 1, first)
+        second_passes("za", 1, 0, False, False)
         round_map("zt", 1, first)
-        square(1, 1, third)
+        square(1, 2, second)
         quantize_map("zt", 1, first)
         second_passes("zt", 1, 0, False, True)
         finish(0)
-        square(1, 2, third)
-        round_map("zt", 0, second)
-        square(1, 3, third)
-        quantize_map("zt", 0, second)
+        square(1, 3, second)
+        canopy(1, 3, second)
+        round_map("zt", 1, second)
+        round_map("za", 1, third)
+        quantize_map("zt", 1, second)
         for i in (1, 2):
-            second_passes("zt", 0, i, False, False)
-        round_map("zt", 1, third)
-        square(1, 0, fourth)
-        quantize_map("zt", 1, third)
-        second_passes("zt", 1, 1, False, True)
+            second_passes("zt", 1, i, False, False)
+        quantize_map("za", 1, third)
+        second_passes("za", 1, 1, False, True)
         finish(1)
-        for t in range(1, PACK):
-            square(1, t, fourth)
         eighths = [slice(fourth.start, fourth.start + P // 2), slice(fourth.start + P // 2, M)]
         for cols in eighths:
-            round_map("zt", 1, cols)
-        codes_of[("zt", 1, fourth.start)] = quantize("zt_last", P, *[rounded[("zt", 1, cols.start)] for cols in eighths])
-        second_passes("zt", 1, 2, False, True)
+            round_map("za", 1, cols)
+        codes_of[("za", 1, fourth.start)] = quantize("za_last", P, *[rounded[("za", 1, cols.start)] for cols in eighths])
+        second_passes("za", 1, 2, False, True)
         finish(2)

@@ -432,10 +432,10 @@ def tile_list_street_shade_exposure_kernel(
         round_map("zt", 1, second)
         round_map("za", 1, third)
         quantize_map("zt", 1, second)
-        for i in (1, 2):
-            second_passes("zt", 1, i, False, False)
+        second_passes("zt", 1, 1, False, False)
         quantize_map("za", 1, third)
         second_passes("za", 1, 1, False, True)
+        second_passes("zt", 1, 2, False, False)
         finish(1)
         eighths = [slice(fourth.start, fourth.start + P // 2), slice(fourth.start + P // 2, M)]
         for cols in eighths:

@@ -149,7 +149,11 @@ def tile_list_street_shade_exposure_kernel(
             picks = []
             for h in range(S // BANK):
                 picked = keep.tile([P, BANK], U32, name="v%d_%d" % (a, h), align_bytes=64)
-                nc.vector.tensor_copy(picked[:], tab_sb[a][:].indirect(offs_sb[:, 32 * h : 32 * (h + 1)]))
+                parts = 2 if (a, h) == (A - 1, 1) else 1
+                for i in range(parts):
+                    c0, c1 = i * BANK // parts, (i + 1) * BANK // parts
+                    listed = offs_sb[:, (h * BANK + c0) // 16 : (h * BANK + c1) // 16]
+                    nc.vector.tensor_copy(picked[:, c0:c1], tab_sb[a][:].indirect(listed))
                 picks.append(picked)
             v_sb.append(picks)
             if a == 0:
@@ -196,25 +200,27 @@ def tile_list_street_shade_exposure_kernel(
 
         h_banks = {}
 
-        def first_pass(b, t, h, a):
+        def first_pass(b, t, h, a, cols=slice(0, BANK)):
             if a == 0:
                 h_banks[(t, h)] = bank(2 * t + h)
             s0 = S + b * K_PASS + t * P
             nc.tensor.matmul_mx(
-                out=h_banks[(t, h)][:],
+                out=h_banks[(t, h)][:, cols],
                 lhsT=wf_sb[(b, a)][:, 2 * t * P : 2 * (t + 1) * P].bitcast(FP4X4),
                 lhsT_scale=plane[a][:, s0 : s0 + P],
-                rhs=v_sb[a][h][:].bitcast(FP8X4),
-                rhs_scale=plane[a][:, h * BANK : (h + 1) * BANK],
+                rhs=v_sb[a][h][:, cols].bitcast(FP8X4),
+                rhs_scale=plane[a][:, h * BANK + cols.start : h * BANK + cols.stop],
                 start=(a == 0),
-                stop=(a == A - 1),
+                stop=(a == A - 1 and cols.stop == BANK),
             )
 
         for a in range(A):
             for pair in range(2):
                 for h in range(2):
-                    for t in (2 * pair, 2 * pair + 1):
-                        first_pass(0, t, h, a)
+                    split = (a, pair, h) == (A - 1, 0, 1)
+                    for cols in (slice(0, BANK // 2), slice(BANK // 2, BANK)) if split else (slice(0, BANK),):
+                        for t in (2 * pair, 2 * pair + 1):
+                            first_pass(0, t, h, a, cols)
 
         h_sb, gates, towers, canopies, rounded, codes_of, wa_bf, wa_q, y_banks = {}, {}, {}, {}, {}, {}, {}, {}, {}
 
@@ -275,12 +281,14 @@ def tile_list_street_shade_exposure_kernel(
             part = width // len(sources)
             for i, source in enumerate(sources):
                 at = slice(i * part, (i + 1) * part)
-                nc.vector.quantize_mx(out=codes[:, at].bitcast(FP8X4), scales=scales[:, at], in_=source[:])
+                nc.vector.quantize_mx(out=codes[:, at].bitcast(FP8X4), scales=scales[:, at], in_=source[:, :])
             return codes, scales
 
         def quantize_map(name, b, cols):
             key = (name, b, cols.start)
-            codes_of[key] = quantize("%s%d_%d" % key, cols.stop - cols.start, rounded[key])
+            made = max(c for (n, bb, c) in rounded if (n, bb) == (name, b) and c <= cols.start)
+            source = rounded[(name, b, made)][:, PACK * (cols.start - made) : PACK * (cols.stop - made)]
+            codes_of[key] = quantize("%s%d_%d" % key, cols.stop - cols.start, source)
 
         def round_wa(b, j):
             tile = ring.tile([P, WA_CHUNK * PACK], BF16, name="wa_bf", align_bytes=64)
@@ -372,15 +380,14 @@ def tile_list_street_shade_exposure_kernel(
             empty(*ahead, 0)
             empty(*ahead, 1)
             tower(*behind, whole)
-            if behind == (1, 0):
+            if behind == (0, 3):
                 for t in range(PACK):
                     gate(0, t, whole)
         for t in range(PACK):
             gate(1, t, pieces[0])
         tower(1, PACK - 1, whole)
-        for cols in pieces[1:]:
-            for t in range(PACK):
-                gate(1, t, cols)
+        for t in range(PACK):
+            gate(1, t, slice(pieces[1].start, M))
 
         canopy(0, 0, whole)
         round_wa(0, 1)
@@ -406,9 +413,9 @@ def tile_list_street_shade_exposure_kernel(
         quantize_map("zt", 0, whole)
         for i in range(len(pieces)):
             second_passes("zt", 0, i, True, False)
+        round_map("za", 0, whole)
         canopy(1, 1, whole)
         square(1, 0, whole)
-        round_map("za", 0, whole)
         canopy(1, 2, whole)
         first, third, fourth = pieces
         second = slice(third.start, fourth.stop)
@@ -424,19 +431,21 @@ def tile_list_street_shade_exposure_kernel(
         second_passes("za", 1, 0, False, False)
         round_map("zt", 1, first)
         square(1, 2, second)
+        square(1, 3, second)
         quantize_map("zt", 1, first)
         second_passes("zt", 1, 0, False, True)
         finish(0)
-        square(1, 3, second)
-        canopy(1, 3, second)
         round_map("zt", 1, second)
-        round_map("za", 1, third)
-        quantize_map("zt", 1, second)
+        canopy(1, 3, third)
+        quantize_map("zt", 1, third)
         second_passes("zt", 1, 1, False, False)
+        round_map("za", 1, third)
+        canopy(1, 3, fourth)
         quantize_map("za", 1, third)
         second_passes("za", 1, 1, False, True)
-        second_passes("zt", 1, 2, False, False)
         finish(1)
+        quantize_map("zt", 1, fourth)
+        second_passes("zt", 1, 2, False, False)
         eighths = [slice(fourth.start, fourth.start + P // 2), slice(fourth.start + P // 2, M)]
         for cols in eighths:
             round_map("za", 1, cols)

@@ -54,12 +54,12 @@ def tile_list_street_shade_exposure_kernel(
         ring = ctx.enter_context(tc.tile_pool(name="ring", bufs=3))
         psum = ctx.enter_context(tc.psum_pool(name="psum", bufs=1))
 
-        wfs_raw = keep.tile([P, H], U8, name="wfs_raw", align_bytes=64)
+        wfs_raw = keep.tile([P, H], U8, name="wfs_raw", align_bytes=256)
         nc.gpsimd.memset(wfs_raw[:].bitcast(I32), 0)
-        ts_rows = keep.tile([P, T], U8, name="ts_rows", align_bytes=64)
+        ts_rows = keep.tile([P, T], U8, name="ts_rows", align_bytes=256)
         nc.vector.memset(ts_rows[:].bitcast(I32), 0)
-        warm = keep.tile([P, 1], F32, name="warm")
-        warm_out = keep.tile([P, 1], F32, name="warm_out")
+        warm = keep.tile([P, 1], F32, name="warm", align_bytes=256)
+        warm_out = keep.tile([P, 1], F32, name="warm_out", align_bytes=256)
         nc.vector.memset(warm[:], 0.0)
 
         def load_rows(queue, rows_sb, rows_hbm):
@@ -72,11 +72,11 @@ def tile_list_street_shade_exposure_kernel(
 
         gains = []
         for name, gain in (("ga_sb", ga), ("gt_sb", gt)):
-            padded = keep.tile([P, B, 2 * PACK], F32, name=name)
+            padded = keep.tile([P, B, 2 * PACK], F32, name=name, align_bytes=256)
             nc.gpsimd.dma_start(padded[:, :, 0:PACK], gain.rearrange("(b p t) -> p b t", b=B, t=PACK))
             gains.append(padded)
         ga_sb, gt_sb = gains
-        ga_rows = keep.tile([P, B, PACK, M], F32, name="ga_rows")
+        ga_rows = keep.tile([P, B, PACK, M], F32, name="ga_rows", align_bytes=256)
         for b in range(B):
             nc.scalar.copy(ga_rows[:, b, :, :], ga_sb[:, b, 0:PACK].unsqueeze(2).to_broadcast([P, PACK, M]))
 
@@ -84,7 +84,7 @@ def tile_list_street_shade_exposure_kernel(
 
         def load_table(a, t0, t1):
             if len(tab_sb) == a:
-                tab_sb.append(stream.tile([P, T], U32, name="tab%d" % a, offset=TAB_BYTES * a, align_bytes=64))
+                tab_sb.append(stream.tile([P, T], U32, name="tab%d" % a, offset=TAB_BYTES * a, align_bytes=256))
             words = tab_words[a].rearrange("p t i -> p (t i)").bitcast(I32)
             nc.sync.dma_start(tab_sb[a][:].bitcast(I32)[:, t0:t1], words[:, t0:t1])
 
@@ -106,19 +106,19 @@ def tile_list_street_shade_exposure_kernel(
                 wf_sb[(b, a)] = ordered[:, (a - passes.start) * PASS_BYTES : (a - passes.start + 1) * PASS_BYTES]
 
         load_table(0, 0, TAB0_CUT)
-        offs_sb = keep.tile([P, S // 16], U16, name="offs_sb")
+        offs_sb = keep.tile([P, S // 16], U16, name="offs_sb", align_bytes=256)
         nc.sync.dma_start(offs_sb[:], offs)
         load_rows(nc.sync, ts_rows, tab_scales)
         load_table(0, TAB0_CUT, T)
         pos_sb = []
         for i, pos in enumerate((pos1, pos2, pos3)):
-            lst = keep.tile([P, M // 16], U16, name="pos%d" % i)
+            lst = keep.tile([P, M // 16], U16, name="pos%d" % i, align_bytes=256)
             nc.sync.dma_start(lst[:], pos)
             pos_sb.append(lst)
-        wf_raw0 = load_wf(0, slice(0, A), stream.tile([P, A * K_PASS * 2], U8, name="wf_raw0", offset=3 * TAB_BYTES, align_bytes=64))
+        wf_raw0 = load_wf(0, slice(0, 2), stream.tile([P, 2 * PASS_BYTES], U8, name="wf_raw0", offset=3 * TAB_BYTES, align_bytes=256))
         load_table(1, 0, T)
 
-        planes = keep.tile([P, A * PLANE], U8, name="planes", align_bytes=64)
+        planes = keep.tile([P, A * PLANE], U8, name="planes", align_bytes=256)
         plane = [planes[:, a * PLANE : (a + 1) * PLANE] for a in range(A)]
         nc.vector.memset(plane[2].bitcast(I32), 0)
         nc.vector.tensor_copy(
@@ -126,7 +126,7 @@ def tile_list_street_shade_exposure_kernel(
             wfs_raw[:].rearrange("p (b m t) -> p b t m", t=PACK, m=P),
         )
         nc.vector.tensor_copy(plane[1][:, S:PLANE].bitcast(I32), plane[0][:, S:PLANE].bitcast(I32))
-        vs_rows = stream.tile([P, S], U8, name="vs_rows", offset=2 * TAB_BYTES, align_bytes=64)
+        vs_rows = stream.tile([P, S], U8, name="vs_rows", offset=2 * TAB_BYTES, align_bytes=256)
         nc.vector.tensor_copy(vs_rows[:], ts_rows[:].indirect(offs_sb[:]))
         for a in range(2):
             nc.vector.tensor_copy(plane[a][:, 0:S].bitcast(I32), vs_rows[:].bitcast(I32))
@@ -148,7 +148,7 @@ def tile_list_street_shade_exposure_kernel(
         for a in range(A):
             picks = []
             for h in range(S // BANK):
-                picked = keep.tile([P, BANK], U32, name="v%d_%d" % (a, h), align_bytes=64)
+                picked = keep.tile([P, BANK], U32, name="v%d_%d" % (a, h), align_bytes=256)
                 parts = 2 if (a, h) == (A - 1, 1) else 1
                 for i in range(parts):
                     c0, c1 = i * BANK // parts, (i + 1) * BANK // parts
@@ -157,12 +157,14 @@ def tile_list_street_shade_exposure_kernel(
                 picks.append(picked)
             v_sb.append(picks)
             if a == 0:
-                wf_first = keep.tile([P, A * PASS_BYTES], U8, name="wf_sb0", align_bytes=64)
-                order_wf(0, slice(0, A), wf_raw0, wf_first, nc.scalar.copy)
+                wf_first = keep.tile([P, 2 * PASS_BYTES], U8, name="wf_sb0", align_bytes=256)
+                order_wf(0, slice(0, 2), wf_raw0, wf_first, nc.scalar.copy)
 
-        wf_raw1 = load_wf(1, slice(0, 2), stream.tile([P, 2 * PASS_BYTES], U8, name="wf_raw1", offset=0, align_bytes=64))
-        wf_raw2 = load_wf(1, slice(2, A), stream.tile([P, PASS_BYTES], U8, name="wf_raw2", offset=4 * S, align_bytes=64))
-        wf_early = keep.tile([P, 2 * PASS_BYTES], U8, name="wf_sb1", align_bytes=64)
+        wf_raw3 = load_wf(0, slice(2, A), stream.tile([P, PASS_BYTES], U8, name="wf_raw3", offset=2 * S, align_bytes=256))
+        wf_third = keep.tile([P, PASS_BYTES], U8, name="wf_sb3", align_bytes=256)
+        order_wf(0, slice(2, A), wf_raw3, wf_third, nc.scalar.copy)
+        wf_raw1 = load_wf(1, slice(0, 2), stream.tile([P, 2 * PASS_BYTES], U8, name="wf_raw1", offset=0, align_bytes=256))
+        wf_early = keep.tile([P, 2 * PASS_BYTES], U8, name="wf_sb1", align_bytes=256)
         order_wf(1, slice(0, 2), wf_raw1, wf_early, nc.scalar.copy)
         wa_raw = {}
 
@@ -174,20 +176,21 @@ def tile_list_street_shade_exposure_kernel(
                 wa_raw[(b, j)] = raw[:, :, (j - j0) * WA_CHUNK : (j - j0 + 1) * WA_CHUNK]
 
         def raw_tile(name, pieces, offset):
-            return stream.tile([P, pieces * PACK * WA_CHUNK], F32, name=name, offset=offset, align_bytes=64)
+            return stream.tile([P, pieces * PACK * WA_CHUNK], F32, name=name, offset=offset, align_bytes=256)
 
         load_wa(0, 0, 1, raw_tile("wa_first", 1, 5 * S)[:])
-        maps0 = stream.tile([P, PACK * 2 * M], F32, name="maps0", offset=9 * S, align_bytes=64)
+        wf_raw2 = load_wf(1, slice(2, A), stream.tile([P, PASS_BYTES], U8, name="wf_raw2", offset=4 * S, align_bytes=256))
+        maps0 = stream.tile([P, PACK * 2 * M], F32, name="maps0", offset=9 * S, align_bytes=256)
         for slot, (b, j) in ((1, (0, 1)), (2, (0, 2)), (3, (1, 0))):
             load_wa(b, j, j + 1, maps0[:, 2 * slot * M : 2 * (slot + 1) * M])
         load_wa(1, 1, 2, raw_tile("wa_fifth", 1, 25 * S)[:])
         load_wa(1, 2, 3, raw_tile("wa_last", 1, 31 * S)[:])
-        wt_sb = stream.tile([P, B * N], U32, name="wt_sb", offset=41 * S, align_bytes=64)
+        wt_sb = stream.tile([P, B * N], U32, name="wt_sb", offset=41 * S, align_bytes=256)
         nc.sync.dma_start(
             wt_sb[:].bitcast(I32).rearrange("p (b n) -> p b n", b=B),
             wt_words.rearrange("b p n i -> p b (n i)").bitcast(I32),
         )
-        wts = stream.tile([P, B * N], U8, name="wts", offset=3 * TAB_BYTES, align_bytes=64)
+        wts = stream.tile([P, B * N], U8, name="wts", offset=3 * TAB_BYTES, align_bytes=256)
         nc.vector.memset(wts[:].bitcast(I32), 0)
         for q in range(QUADS):
             nc.sync.dma_start(
@@ -226,7 +229,7 @@ def tile_list_street_shade_exposure_kernel(
 
         def empty(b, t, h, on_vector=False):
             if (b, t) not in h_sb:
-                h_sb[(b, t)] = keep.tile([P, S], F32, name="h_sb%d_%d" % (b, t))
+                h_sb[(b, t)] = keep.tile([P, S], F32, name="h_sb%d_%d" % (b, t), align_bytes=256)
             half = h_sb[(b, t)][:, h * BANK : (h + 1) * BANK]
             if on_vector:
                 nc.vector.tensor_copy(half, h_banks[(t, h)][:])
@@ -239,7 +242,7 @@ def tile_list_street_shade_exposure_kernel(
         def slots(table, name, b, cols):
             key = (b, cols.start)
             if key not in table:
-                table[key] = keep.tile([P, PACK, cols.stop - cols.start], F32, name="%s%d_%d" % (name, b, cols.start))
+                table[key] = keep.tile([P, PACK, cols.stop - cols.start], F32, name="%s%d_%d" % (name, b, cols.start), align_bytes=256)
             return table[key]
 
         def gate(b, t, cols):
@@ -260,9 +263,9 @@ def tile_list_street_shade_exposure_kernel(
         def round_map(name, b, cols):
             width = cols.stop - cols.start
             if (name, b) == ("zt", 0):
-                tile = stream.tile([P, width * PACK], BF16, name="zt_bf0", offset=29 * S, align_bytes=64)
+                tile = stream.tile([P, width * PACK], BF16, name="zt_bf0", offset=29 * S, align_bytes=256)
             else:
-                tile = keep.tile([P, width * PACK], BF16, name="%s_bf%d_%d" % (name, b, cols.start), align_bytes=64)
+                tile = keep.tile([P, width * PACK], BF16, name="%s_bf%d_%d" % (name, b, cols.start), align_bytes=256)
             rounded[(name, b, cols.start)] = tile
             if name == "zt":
                 nc.vector.tensor_copy(woven(tile[:]), by_slot(towers[(b, 0)][:, :, cols]))
@@ -276,8 +279,8 @@ def tile_list_street_shade_exposure_kernel(
                 )
 
         def quantize(name, width, *sources):
-            codes = keep.tile([P, width], U32, name=name + "_codes", align_bytes=64)
-            scales = keep.tile([P, width], U8, name=name + "_scales", align_bytes=64)
+            codes = keep.tile([P, width], U32, name=name + "_codes", align_bytes=256)
+            scales = keep.tile([P, width], U8, name=name + "_scales", align_bytes=256)
             part = width // len(sources)
             for i, source in enumerate(sources):
                 at = slice(i * part, (i + 1) * part)
@@ -291,7 +294,7 @@ def tile_list_street_shade_exposure_kernel(
             codes_of[key] = quantize("%s%d_%d" % key, cols.stop - cols.start, source)
 
         def round_wa(b, j):
-            tile = ring.tile([P, WA_CHUNK * PACK], BF16, name="wa_bf", align_bytes=64)
+            tile = ring.tile([P, WA_CHUNK * PACK], BF16, name="wa_bf", align_bytes=256)
             raw = wa_raw[(b, j)]
             if (b, j) == (0, 0):
                 nc.gpsimd.tensor_scalar(
@@ -345,7 +348,7 @@ def tile_list_street_shade_exposure_kernel(
             cols = pieces[i]
             width = cols.stop - cols.start
             for no, n_tiles in groups(i):
-                result = keep.tile([P, len(n_tiles), width], F32, name="result%d" % no)
+                result = keep.tile([P, len(n_tiles), width], F32, name="result%d" % no, align_bytes=256)
                 nc.scalar.activation(
                     result[:].rearrange("p j m -> p (j m)"), y_banks[no][:, 0 : len(n_tiles) * width], ACT.Sigmoid
                 )
@@ -359,15 +362,15 @@ def tile_list_street_shade_exposure_kernel(
 
         both = maps0[:].rearrange("p (t u m) -> p u t m", t=PACK, u=2)
         canopies[(0, 0)] = both[:, 0, :, :]
-        canopies[(1, 0)] = stream.tile([P, PACK, M], F32, name="canopy1", offset=33 * S, align_bytes=64)
-        h_sb[(0, 0)] = stream.tile([P, S], F32, name="h_sb0_0", offset=0, align_bytes=64)
+        canopies[(1, 0)] = stream.tile([P, PACK, M], F32, name="canopy1", offset=33 * S, align_bytes=256)
+        h_sb[(0, 0)] = stream.tile([P, S], F32, name="h_sb0_0", offset=0, align_bytes=256)
 
         empty(0, 0, 0)
         empty(0, 0, 1)
         empty(0, 1, 0, True)
         empty(0, 1, 1, True)
         round_wa(0, 0)
-        wf_late = stream.tile([P, PASS_BYTES], U8, name="wf_sb2", offset=5 * S, align_bytes=64)
+        wf_late = stream.tile([P, PASS_BYTES], U8, name="wf_sb2", offset=5 * S, align_bytes=256)
         order_wf(1, slice(2, A), wf_raw2, wf_late, nc.vector.tensor_copy)
         empty(0, 2, 0)
         tower(0, 0, whole)

@@ -70,12 +70,8 @@ def tile_list_street_shade_exposure_kernel(
         load_rows(nc.scalar, wfs_raw, wf_scales)
         nc.scalar.activation(warm_out[:], warm[:], ACT.Sigmoid)
 
-        gains = []
-        for name, gain in (("ga_sb", ga), ("gt_sb", gt)):
-            padded = keep.tile([P, B, 2 * PACK], F32, name=name, align_bytes=256)
-            nc.gpsimd.dma_start(padded[:, :, 0:PACK], gain.rearrange("(b p t) -> p b t", b=B, t=PACK))
-            gains.append(padded)
-        ga_sb, gt_sb = gains
+        ga_sb = keep.tile([P, B, 2 * PACK], F32, name="ga_sb", align_bytes=256)
+        nc.gpsimd.dma_start(ga_sb[:, :, 0:PACK], ga.rearrange("(b p t) -> p b t", b=B, t=PACK))
         ga_rows = keep.tile([P, B, PACK, M], F32, name="ga_rows", align_bytes=256)
         for b in range(B):
             nc.scalar.copy(ga_rows[:, b, :, :], ga_sb[:, b, 0:PACK].unsqueeze(2).to_broadcast([P, PACK, M]))
@@ -115,7 +111,7 @@ def tile_list_street_shade_exposure_kernel(
             lst = keep.tile([P, M // 16], U16, name="pos%d" % i, align_bytes=256)
             nc.sync.dma_start(lst[:], pos)
             pos_sb.append(lst)
-        wf_raw0 = load_wf(0, slice(0, 2), stream.tile([P, 2 * PASS_BYTES], U8, name="wf_raw0", offset=3 * TAB_BYTES, align_bytes=256))
+        wf_raw0 = load_wf(0, slice(0, 2), stream.tile([P, 2 * PASS_BYTES], U8, name="wf_raw0", offset=50 * S, align_bytes=256))
         load_table(1, 0, T)
 
         planes = keep.tile([P, A * PLANE], U8, name="planes", align_bytes=256)
@@ -183,14 +179,16 @@ def tile_list_street_shade_exposure_kernel(
         maps0 = stream.tile([P, PACK * 2 * M], F32, name="maps0", offset=9 * S, align_bytes=256)
         for slot, (b, j) in ((1, (0, 1)), (2, (0, 2)), (3, (1, 0))):
             load_wa(b, j, j + 1, maps0[:, 2 * slot * M : 2 * (slot + 1) * M])
+        gt_sb = stream.tile([P, B, 2 * PACK], F32, name="gt_sb", offset=30 * S, align_bytes=256)
+        nc.sync.dma_start(gt_sb[:, :, 0:PACK], gt.rearrange("(b p t) -> p b t", b=B, t=PACK))
         load_wa(1, 1, 2, raw_tile("wa_fifth", 1, 25 * S)[:])
-        load_wa(1, 2, 3, raw_tile("wa_last", 1, 31 * S)[:])
-        wt_sb = stream.tile([P, B * N], U32, name="wt_sb", offset=41 * S, align_bytes=256)
+        load_wa(1, 2, 3, raw_tile("wa_last", 1, 33 * S)[:])
+        wt_sb = stream.tile([P, B * N], U32, name="wt_sb", offset=43 * S, align_bytes=256)
         nc.sync.dma_start(
             wt_sb[:].bitcast(I32).rearrange("p (b n) -> p b n", b=B),
             wt_words.rearrange("b p n i -> p b (n i)").bitcast(I32),
         )
-        wts = stream.tile([P, B * N], U8, name="wts", offset=3 * TAB_BYTES, align_bytes=256)
+        wts = stream.tile([P, B * N], U8, name="wts", offset=50 * S, align_bytes=256)
         nc.vector.memset(wts[:].bitcast(I32), 0)
         for q in range(QUADS):
             nc.sync.dma_start(
@@ -263,7 +261,7 @@ def tile_list_street_shade_exposure_kernel(
         def round_map(name, b, cols):
             width = cols.stop - cols.start
             if (name, b) == ("zt", 0):
-                tile = stream.tile([P, width * PACK], BF16, name="zt_bf0", offset=29 * S, align_bytes=256)
+                tile = stream.tile([P, width * PACK], BF16, name="zt_bf0", offset=31 * S, align_bytes=256)
             else:
                 tile = keep.tile([P, width * PACK], BF16, name="%s_bf%d_%d" % (name, b, cols.start), align_bytes=256)
             rounded[(name, b, cols.start)] = tile
@@ -362,7 +360,7 @@ def tile_list_street_shade_exposure_kernel(
 
         both = maps0[:].rearrange("p (t u m) -> p u t m", t=PACK, u=2)
         canopies[(0, 0)] = both[:, 0, :, :]
-        canopies[(1, 0)] = stream.tile([P, PACK, M], F32, name="canopy1", offset=33 * S, align_bytes=256)
+        canopies[(1, 0)] = stream.tile([P, PACK, M], F32, name="canopy1", offset=35 * S, align_bytes=256)
         h_sb[(0, 0)] = stream.tile([P, S], F32, name="h_sb0_0", offset=0, align_bytes=256)
 
         empty(0, 0, 0)

from contextlib import ExitStack

import concourse.mybir as mybir

K, T, S, H, M, N = 1536, 4096, 1024, 1024, 512, 768
FLOPS = 2 * K * H * S + 2 * 2 * H * N * M

F32 = mybir.dt.float32
BF16 = mybir.dt.bfloat16
I32 = mybir.dt.int32
U32 = mybir.dt.uint32
U16 = mybir.dt.uint16
U8 = mybir.dt.uint8
FP8X4 = mybir.dt.float8_e4m3fn_x4
FP4X4 = mybir.dt.float4_e2m1fn_x4
ACT = mybir.ActivationFunctionType
MULT = mybir.AluOpType.mult
ADD = mybir.AluOpType.add

P = 128
PACK = 4
K_PASS = P * PACK
A = K // K_PASS
B = H // K_PASS
BANK = 512
QUADS = 4
ROWS = 16
N_TILES = N // P
WA_CHUNK = 256
TAB_BYTES = 4 * T
WA_BYTES = 4 * PACK * WA_CHUNK
PASS_BYTES = 2 * K_PASS
PLANE = S + H
ROW0 = (0, 56, 72)
TAB0_CUT = 3 * T // 8
TAB2_CUT = 3 * T // 4


def woven(tile_ap):
    return tile_ap.rearrange("p (c i t) -> p c t i", i=4, t=PACK)


def by_slot(tile_ap):
    return tile_ap.rearrange("p t (c i) -> p c t i", i=4)


def tile_list_street_shade_exposure_kernel(
    tc, tab_words, tab_scales, offs, pos1, pos2, pos3, wf_words, wf_scales, ga, gt, wa, wt_words, wt_scales, out
):
    nc = tc.nc
    with ExitStack() as ctx:
        keep = ctx.enter_context(tc.tile_pool(name="keep", bufs=1))
        stream = ctx.enter_context(tc.tile_pool(name="stream", bufs=1))
        ring = ctx.enter_context(tc.tile_pool(name="ring", bufs=3))
        psum = ctx.enter_context(tc.psum_pool(name="psum", bufs=1))

        wfs_raw = keep.tile([P, H], U8, name="wfs_raw", align_bytes=256)
        nc.gpsimd.memset(wfs_raw[:].bitcast(I32), 0)
        ts_rows = keep.tile([P, T], U8, name="ts_rows", align_bytes=256)
        nc.vector.memset(ts_rows[:].bitcast(I32), 0)
        warm = keep.tile([P, 1], F32, name="warm", align_bytes=256)
        warm_out = keep.tile([P, 1], F32, name="warm_out", align_bytes=256)
        nc.vector.memset(warm[:], 0.0)

        def load_rows(queue, rows_sb, rows_hbm):
            rows_i32 = rows_hbm.rearrange("a q t -> (a q) t").bitcast(I32)
            queue.dma_start(rows_sb[:].bitcast(I32)[ROW0[0] : ROW0[0] + ROWS, :], rows_i32[0:ROWS, :])
            queue.dma_start(rows_sb[:].bitcast(I32)[ROW0[1] : ROW0[1] + 2 * ROWS, :], rows_i32[ROWS : 3 * ROWS, :])

        load_rows(nc.scalar, wfs_raw, wf_scales)
        nc.scalar.activation(warm_out[:], warm[:], ACT.Sigmoid)

        ga_sb = keep.tile([P, B, 2 * PACK], F32, name="ga_sb", align_bytes=256)
        nc.gpsimd.dma_start(ga_sb[:, :, 0:PACK], ga.rearrange("(b p t) -> p b t", b=B, t=PACK))
        ga_rows = keep.tile([P, B, PACK, M], F32, name="ga_rows", align_bytes=256)
        for b in range(B):
            nc.scalar.copy(ga_rows[:, b, :, :], ga_sb[:, b, 0:PACK].unsqueeze(2).to_broadcast([P, PACK, M]))

        tab_sb = []

        def load_table(a, t0, t1):
            if len(tab_sb) == a:
                tab_sb.append(stream.tile([P, T], U32, name="tab%d" % a, offset=TAB_BYTES * a, align_bytes=256))
            words = tab_words[a].rearrange("p t i -> p (t i)").bitcast(I32)
            nc.sync.dma_start(tab_sb[a][:].bitcast(I32)[:, t0:t1], words[:, t0:t1])

        wf_hbm = wf_words.bitcast(I32).rearrange("a p (b x) -> b p a x", b=B)

        wf_sb = {}

        def load_wf(b, passes, raw):
            count = passes.stop - passes.start
            nc.sync.dma_start(raw[:].bitcast(I32).rearrange("p (a x) -> p a x", a=count), wf_hbm[b][:, passes, :])
            return raw

        def order_wf(b, passes, raw, ordered, copy):
            copy(
                ordered[:].bitcast(U16).rearrange("p (a t m) -> p t a m", t=PACK, m=P),
                raw[:].bitcast(U16).rearrange("p (a m t) -> p t a m", t=PACK, m=P),
            )
            for a in range(passes.start, passes.stop):
                wf_sb[(b, a)] = ordered[:, (a - passes.start) * PASS_BYTES : (a - passes.start + 1) * PASS_BYTES]

        load_table(0, 0, TAB0_CUT)
        offs_sb = keep.tile([P, S // 16], U16, name="offs_sb", align_bytes=256)
        nc.sync.dma_start(offs_sb[:], offs)
        load_rows(nc.sync, ts_rows, tab_scales)
        load_table(0, TAB0_CUT, T)
        pos_sb = []
        for i, pos in enumerate((pos1, pos2, pos3)):
            lst = keep.tile([P, M // 16], U16, name="pos%d" % i, align_bytes=256)
            nc.sync.dma_start(lst[:], pos)
            pos_sb.append(lst)
        wf_raw0 = load_wf(0, slice(0, 2), stream.tile([P, 2 * PASS_BYTES], U8, name="wf_raw0", offset=50 * S, align_bytes=256))
        load_table(1, 0, T)

        planes = keep.tile([P, A * PLANE], U8, name="planes", align_bytes=256)
        plane = [planes[:, a * PLANE : (a + 1) * PLANE] for a in range(A)]
        nc.vector.memset(plane[2].bitcast(I32), 0)
        nc.vector.tensor_copy(
            plane[0][:, S:PLANE].rearrange("p (b t m) -> p b t m", t=PACK, m=P),
            wfs_raw[:].rearrange("p (b m t) -> p b t m", t=PACK, m=P),
        )
        nc.vector.tensor_copy(plane[1][:, S:PLANE].bitcast(I32), plane[0][:, S:PLANE].bitcast(I32))
        vs_rows = stream.tile([P, S], U8, name="vs_rows", offset=2 * TAB_BYTES, align_bytes=256)
        nc.vector.tensor_copy(vs_rows[:], ts_rows[:].indirect(offs_sb[:]))
        for a in range(2):
            nc.vector.tensor_copy(plane[a][:, 0:S].bitcast(I32), vs_rows[:].bitcast(I32))

        def carry(a):
            source = plane[min(a, 1)].bitcast(I32)
            for q in (0, 2, 1, 3):
                r0 = ROW0[a] + 4 * q
                if r0 != 32 * q:
                    nc.sync.dma_start(plane[a].bitcast(I32)[32 * q : 32 * q + 4, :], source[r0 : r0 + 4, :])

        carry(0)
        carry(1)
        load_table(2, 0, TAB2_CUT)
        carry(2)
        load_table(2, TAB2_CUT, T)

        v_sb = []
        for a in range(A):
            picks = []
            for h in range(S // BANK):
                picked = keep.tile([P, BANK], U32, name="v%d_%d" % (a, h), align_bytes=256)
                parts = 2 if (a, h) == (A - 1, 1) else 1
                for i in range(parts):
                    c0, c1 = i * BANK // parts, (i + 1) * BANK // parts
                    listed = offs_sb[:, (h * BANK + c0) // 16 : (h * BANK + c1) // 16]
                    nc.vector.tensor_copy(picked[:, c0:c1], tab_sb[a][:].indirect(listed))
                picks.append(picked)
            v_sb.append(picks)
            if a == 0:
                wf_first = keep.tile([P, 2 * PASS_BYTES], U8, name="wf_sb0", align_bytes=256)
                order_wf(0, slice(0, 2), wf_raw0, wf_first, nc.scalar.copy)

        wf_raw3 = load_wf(0, slice(2, A), stream.tile([P, PASS_BYTES], U8, name="wf_raw3", offset=2 * S, align_bytes=256))
        wf_third = keep.tile([P, PASS_BYTES], U8, name="wf_sb3", align_bytes=256)
        order_wf(0, slice(2, A), wf_raw3, wf_third, nc.scalar.copy)
        wf_raw1 = load_wf(1, slice(0, 2), stream.tile([P, 2 * PASS_BYTES], U8, name="wf_raw1", offset=0, align_bytes=256))
        wf_early = keep.tile([P, 2 * PASS_BYTES], U8, name="wf_sb1", align_bytes=256)
        order_wf(1, slice(0, 2), wf_raw1, wf_early, nc.scalar.copy)
        wa_raw = {}

        def load_wa(b, j0, j1, flat):
            raw = flat.rearrange("p (j n) -> p j n", j=PACK)
            rows = wa[b * K_PASS : (b + 1) * K_PASS, j0 * WA_CHUNK : j1 * WA_CHUNK]
            nc.sync.dma_start(raw, rows.rearrange("(p j) n -> p j n", j=PACK))
            for j in range(j0, j1):
                wa_raw[(b, j)] = raw[:, :, (j - j0) * WA_CHUNK : (j - j0 + 1) * WA_CHUNK]

        def raw_tile(name, pieces, offset):
            return stream.tile([P, pieces * PACK * WA_CHUNK], F32, name=name, offset=offset, align_bytes=256)

        load_wa(0, 0, 1, raw_tile("wa_first", 1, 5 * S)[:])
        wf_raw2 = load_wf(1, slice(2, A), stream.tile([P, PASS_BYTES], U8, name="wf_raw2", offset=4 * S, align_bytes=256))
        maps0 = stream.tile([P, PACK * 2 * M], F32, name="maps0", offset=9 * S, align_bytes=256)
        for slot, (b, j) in ((1, (0, 1)), (2, (0, 2)), (3, (1, 0))):
            load_wa(b, j, j + 1, maps0[:, 2 * slot * M : 2 * (slot + 1) * M])
        gt_sb = stream.tile([P, B, 2 * PACK], F32, name="gt_sb", offset=30 * S, align_bytes=256)
        nc.sync.dma_start(gt_sb[:, :, 0:PACK], gt.rearrange("(b p t) -> p b t", b=B, t=PACK))
        load_wa(1, 1, 2, raw_tile("wa_fifth", 1, 25 * S)[:])
        load_wa(1, 2, 3, raw_tile("wa_last", 1, 33 * S)[:])
        wt_sb = stream.tile([P, B * N], U32, name="wt_sb", offset=43 * S, align_bytes=256)
        nc.sync.dma_start(
            wt_sb[:].bitcast(I32).rearrange("p (b n) -> p b n", b=B),
            wt_words.rearrange("b p n i -> p b (n i)").bitcast(I32),
        )
        wts = stream.tile([P, B * N], U8, name="wts", offset=50 * S, align_bytes=256)
        nc.vector.memset(wts[:].bitcast(I32), 0)
        for q in range(QUADS):
            nc.sync.dma_start(
                wts[:].bitcast(I32)[32 * q : 32 * q + 4, :].rearrange("r (b x) -> r b x", b=B),
                wt_scales.bitcast(I32)[:, 4 * q : 4 * q + 4, :].rearrange("b r x -> r b x"),
            )

        def bank(i):
            return psum.tile([P, BANK], F32, name="bank%d" % i, tag="bank%d" % i)

        h_banks = {}

        def first_pass(b, t, h, a, cols=slice(0, BANK)):
            if a == 0:
                h_banks[(t, h)] = bank(2 * t + h)
            s0 = S + b * K_PASS + t * P
            nc.tensor.matmul_mx(
                out=h_banks[(t, h)][:, cols],
                lhsT=wf_sb[(b, a)][:, 2 * t * P : 2 * (t + 1) * P].bitcast(FP4X4),
                lhsT_scale=plane[a][:, s0 : s0 + P],
                rhs=v_sb[a][h][:, cols].bitcast(FP8X4),
                rhs_scale=plane[a][:, h * BANK + cols.start : h * BANK + cols.stop],
                start=(a == 0),
                stop=(a == A - 1 and cols.stop == BANK),
            )

        for a in range(A):
            for pair in range(2):
                for h in range(2):
                    split = (a, pair, h) == (A - 1, 0, 1)
                    for cols in (slice(0, BANK // 2), slice(BANK // 2, BANK)) if split else (slice(0, BANK),):
                        for t in (2 * pair, 2 * pair + 1):
                            first_pass(0, t, h, a, cols)

        h_sb, gates, towers, canopies, rounded, codes_of, wa_bf, wa_q, y_banks = {}, {}, {}, {}, {}, {}, {}, {}, {}

        def empty(b, t, h, on_vector=False):
            if (b, t) not in h_sb:
                h_sb[(b, t)] = keep.tile([P, S], F32, name="h_sb%d_%d" % (b, t), align_bytes=256)
            half = h_sb[(b, t)][:, h * BANK : (h + 1) * BANK]
            if on_vector:
                nc.vector.tensor_copy(half, h_banks[(t, h)][:])
            else:
                nc.scalar.copy(half, h_banks[(t, h)][:])

        def picked(b, t, which, cols):
            return h_sb[(b, t)][:].indirect(pos_sb[which][:, cols.start // 16 : cols.stop // 16])

        def slots(table, name, b, cols):
            key = (b, cols.start)
            if key not in table:
                table[key] = keep.tile([P, PACK, cols.stop - cols.start], F32, name="%s%d_%d" % (name, b, cols.start), align_bytes=256)
            return table[key]

        def gate(b, t, cols):
            nc.scalar.activation(slots(gates, "gate", b, cols)[:, t, :], picked(b, t, 0, cols), ACT.Sigmoid)

        def tower(b, t, cols):
            nc.scalar.activation(slots(towers, "tower", b, cols)[:, t, :], picked(b, t, 2, cols), ACT.Copy)

        def canopy(b, t, cols):
            nc.vector.tensor_tensor(
                canopies[(b, 0)][:, t, cols], picked(b, t, 1, cols), ga_rows[:, b, t, cols], MULT
            )

        def square(b, t, cols):
            values = towers[(b, 0)][:, t, cols]
            nc.vector.scalar_tensor_tensor(values, values, gt_sb[:, b, t : t + 1], values, MULT, MULT)

        def round_map(name, b, cols):
            width = cols.stop - cols.start
            if (name, b) == ("zt", 0):
                tile = stream.tile([P, width * PACK], BF16, name="zt_bf0", offset=31 * S, align_bytes=256)
            else:
                tile = keep.tile([P, width * PACK], BF16, name="%s_bf%d_%d" % (name, b, cols.start), align_bytes=256)
            rounded[(name, b, cols.start)] = tile
            if name == "zt":
                nc.vector.tensor_copy(woven(tile[:]), by_slot(towers[(b, 0)][:, :, cols]))
            else:
                made = max(c for (bb, c) in gates if bb == b and c <= cols.start)
                nc.vector.tensor_tensor(
                    woven(tile[:]),
                    by_slot(canopies[(b, 0)][:, :, cols]),
                    by_slot(gates[(b, made)][:, :, cols.start - made : cols.stop - made]),
                    MULT,
                )

        def quantize(name, width, *sources):
            codes = keep.tile([P, width], U32, name=name + "_codes", align_bytes=256)
            scales = keep.tile([P, width], U8, name=name + "_scales", align_bytes=256)
            part = width // len(sources)
            for i, source in enumerate(sources):
                at = slice(i * part, (i + 1) * part)
                nc.vector.quantize_mx(out=codes[:, at].bitcast(FP8X4), scales=scales[:, at], in_=source[:, :])
            return codes, scales

        def quantize_map(name, b, cols):
            key = (name, b, cols.start)
            made = max(c for (n, bb, c) in rounded if (n, bb) == (name, b) and c <= cols.start)
            source = rounded[(name, b, made)][:, PACK * (cols.start - made) : PACK * (cols.stop - made)]
            codes_of[key] = quantize("%s%d_%d" % key, cols.stop - cols.start, source)

        def round_wa(b, j):
            tile = ring.tile([P, WA_CHUNK * PACK], BF16, name="wa_bf", align_bytes=256)
            raw = wa_raw[(b, j)]
            if (b, j) == (0, 0):
                nc.gpsimd.tensor_scalar(
                    tile[:].rearrange("p (c t) -> p c t", t=PACK), raw.rearrange("p t c -> p c t"), 1.0, 0.0, MULT, ADD
                )
            else:
                nc.vector.tensor_copy(woven(tile[:]), by_slot(raw))
            wa_bf[(b, j)] = tile

        def quantize_wa(b, j):
            wa_q[(b, j)] = quantize("wa%d_%d" % (b, j), WA_CHUNK, wa_bf[(b, j)])

        def weights(name, b, n_tile):
            if name == "za":
                codes, scales = wa_q[(b, n_tile * P // WA_CHUNK)]
                n0 = n_tile * P % WA_CHUNK
                return codes[:, n0 : n0 + P], scales[:, n0 : n0 + P]
            n0 = b * N + n_tile * P
            return wt_sb[:, n0 : n0 + P], wts[:, n0 : n0 + P]

        whole = slice(0, M)
        pieces = [slice(0, 2 * P), slice(2 * P, 3 * P), slice(3 * P, M)]
        piece_banks = [(0, 1, 2), (3, 4), (5, 6, 7)]

        def groups(i):
            per_bank = N_TILES // len(piece_banks[i])
            return [(no, range(g * per_bank, (g + 1) * per_bank)) for g, no in enumerate(piece_banks[i])]

        def second_passes(name, b, i, start, stop):
            cols = pieces[i]
            width = cols.stop - cols.start
            made = max(c for (n, bb, c) in codes_of if (n, bb) == (name, b) and c <= cols.start)
            c0 = cols.start - made
            codes, scales = codes_of[(name, b, made)]
            for no, n_tiles in groups(i):
                if start:
                    y_banks[no] = bank(no)
                for j, n_tile in enumerate(n_tiles):
                    w_codes, w_scales = weights(name, b, n_tile)
                    nc.tensor.matmul_mx(
                        out=y_banks[no][:, j * width : (j + 1) * width],
                        lhsT=w_codes.bitcast(FP8X4),
                        lhsT_scale=w_scales,
                        rhs=codes[:, c0 : c0 + width].bitcast(FP8X4),
                        rhs_scale=scales[:, c0 : c0 + width],
                        start=(start and j == 0),
                        stop=(stop and j == len(n_tiles) - 1),
                    )

        def finish(i):
            cols = pieces[i]
            width = cols.stop - cols.start
            for no, n_tiles in groups(i):
                result = keep.tile([P, len(n_tiles), width], F32, name="result%d" % no, align_bytes=256)
                nc.scalar.activation(
                    result[:].rearrange("p j m -> p (j m)"), y_banks[no][:, 0 : len(n_tiles) * width], ACT.Sigmoid
                )
                rows_out = out[n_tiles.start * P : n_tiles.stop * P, cols]
                nc.sync.dma_start(rows_out.rearrange("(j p) m -> p j m", p=P), result[:])

        def refill(t):
            for h in range(2):
                for a in range(A):
                    first_pass(1, t, h, a)

        both = maps0[:].rearrange("p (t u m) -> p u t m", t=PACK, u=2)
        canopies[(0, 0)] = both[:, 0, :, :]
        canopies[(1, 0)] = stream.tile([P, PACK, M], F32, name="canopy1", offset=35 * S, align_bytes=256)
        h_sb[(0, 0)] = stream.tile([P, S], F32, name="h_sb0_0", offset=0, align_bytes=256)

        empty(0, 0, 0)
        empty(0, 0, 1)
        empty(0, 1, 0, True)
        empty(0, 1, 1, True)
        round_wa(0, 0)
        wf_late = stream.tile([P, PASS_BYTES], U8, name="wf_sb2", offset=5 * S, align_bytes=256)
        order_wf(1, slice(2, A), wf_raw2, wf_late, nc.vector.tensor_copy)
        empty(0, 2, 0)
        tower(0, 0, whole)
        empty(0, 2, 1)
        tower(0, 1, whole)
        tiles = [(b, t) for b in range(B) for t in range(PACK)]
        for ahead, behind in zip(tiles[3:], tiles[2:]):
            if ahead[0] == 1:
                refill(ahead[1])
            empty(*ahead, 0)
            empty(*ahead, 1)
            tower(*behind, whole)
            if behind == (0, 3):
                for t in range(PACK):
                    gate(0, t, whole)
        for t in range(PACK):
            gate(1, t, pieces[0])
        tower(1, PACK - 1, whole)
        for t in range(PACK):
            gate(1, t, slice(pieces[1].start, M))

        canopy(0, 0, whole)
        round_wa(0, 1)
        quantize_wa(0, 0)
        canopy(0, 1, whole)
        round_wa(0, 2)
        quantize_wa(0, 1)
        canopy(0, 2, whole)
        round_wa(1, 0)
        quantize_wa(0, 2)
        square(0, 0, whole)
        canopy(0, 3, whole)
        round_wa(1, 1)
        quantize_wa(1, 0)
        square(0, 1, whole)
        round_wa(1, 2)
        quantize_wa(1, 1)
        square(0, 2, whole)
        square(0, 3, whole)
        quantize_wa(1, 2)
        round_map("zt", 0, whole)
        canopy(1, 0, whole)
        quantize_map("zt", 0, whole)
        for i in range(len(pieces)):
            second_passes("zt", 0, i, True, False)
        round_map("za", 0, whole)
        canopy(1, 1, whole)
        square(1, 0, whole)
        canopy(1, 2, whole)
        first, third, fourth = pieces
        second = slice(third.start, fourth.stop)
        square(1, 1, whole)
        canopy(1, 3, first)
        square(1, 2, first)
        quantize_map("za", 0, whole)
        for i in range(len(pieces)):
            second_passes("za", 0, i, False, False)
        round_map("za", 1, first)
        square(1, 3, first)
        quantize_map("za", 1, first)
        second_passes("za", 1, 0, False, False)
        round_map("zt", 1, first)
        square(1, 2, second)
        square(1, 3, second)
        quantize_map("zt", 1, first)
        second_passes("zt", 1, 0, False, True)
        finish(0)
        round_map("zt", 1, second)
        canopy(1, 3, third)
        quantize_map("zt", 1, third)
        second_passes("zt", 1, 1, False, False)
        round_map("za", 1, third)
        canopy(1, 3, fourth)
        quantize_map("za", 1, third)
        second_passes("za", 1, 1, False, True)
        finish(1)
        quantize_map("zt", 1, fourth)
        second_passes("zt", 1, 2, False, False)
        eighths = [slice(fourth.start, fourth.start + P // 2), slice(fourth.start + P // 2, M)]
        for cols in eighths:
            round_map("za", 1, cols)
        codes_of[("za", 1, fourth.start)] = quantize("za_last", P, *[rounded[("za", 1, cols.start)] for cols in eighths])
        second_passes("za", 1, 2, False, True)
        finish(2)
